import numpy as np
import ml_dtypes


def mxq(x, axis, fmt="e4m3"):
    dtype, down = {"e4m3": (ml_dtypes.float8_e4m3fn, 7), "e5m2": (ml_dtypes.float8_e5m2, 14)}[fmt]
    v = np.moveaxis(np.asarray(x, np.float32).astype(ml_dtypes.bfloat16).astype(np.float64), axis, -1)
    blocks = v.reshape(v.shape[:-1] + (-1, 32))
    amax = np.abs(blocks).max(-1, keepdims=True)
    byte = np.maximum(np.where(amax > 0, np.frexp(amax)[1] - 1 + 127, 0) - down, 1)
    scale = np.exp2(byte - 127.0)
    codes = (blocks / scale).astype(np.float32).astype(dtype).astype(np.float64)
    return np.moveaxis((codes * scale).reshape(v.shape), -1, axis)


WIDE = False


def mx_kscale(k):
    if not WIDE:
        return np.ones(k)
    levels = np.array([10, -10, 5, -5, 0])
    if k % 512:
        return np.exp2(np.random.permutation(np.resize(levels, k // 32))).repeat(32)
    a = np.empty((k // 512, 16))
    for p in range(k // 512):
        a[p, :8] = np.random.permutation(np.resize(levels, 8))
        for g in range(8):
            far = levels[np.abs(levels - a[p, g]) >= 10]
            a[p, g + 8] = far[np.random.randint(len(far))]
    return np.exp2(a.ravel()).repeat(32)


def f64(x):
    return np.asarray(x).astype(np.float64)


def striped(idx):
    return np.tile(np.asarray(idx).reshape(-1, 16).T, (8, 1)).astype(np.uint16)


def unstriped(offs):
    return offs[:16].T.reshape(-1).astype(np.int64)


def striped8(idx):
    return np.asarray(idx).reshape(8, -1, 16).transpose(0, 2, 1).reshape(128, -1).astype(np.uint16)


def unstriped8(offs):
    return offs.reshape(8, 16, -1).transpose(0, 2, 1).reshape(8, -1).astype(np.int64)


def pick8(x, idx, run):
    r = np.arange(len(x))
    return x[r[:, None], idx[r % (8 * run) // run]]


E2M1 = np.array([0.0, 0.5, 1.0, 1.5, 2.0, 3.0, 4.0, 6.0, -0.0, -0.5, -1.0, -1.5, -2.0, -3.0, -4.0, -6.0])


def pack_weight(w, fmt):
    k, n = w.shape
    w = f64(np.asarray(w, np.float32).astype(ml_dtypes.bfloat16)).reshape(k // 32, 32, n)
    amax = np.abs(w).max(1)
    if fmt == "e4m3":
        byte = np.frexp(amax)[1] - 1 + 127 - 7
    else:
        mant, ex = np.frexp(amax / 6.0)
        byte = np.where(mant > 0.5, ex, ex - 1) + 127
    byte = np.clip(np.where(amax > 0, byte, 1), 1, 254)
    scaled = (w * np.exp2(127.0 - byte)[:, None, :]).reshape(k, n).astype(np.float32)
    by_word = np.ascontiguousarray(scaled.reshape(k // 512, 128, 4, n).transpose(0, 1, 3, 2))
    if fmt == "e4m3":
        words = by_word.astype(ml_dtypes.float8_e4m3fn).view(np.uint8)
    else:
        c = by_word.astype(ml_dtypes.float4_e2m1fn).view(np.uint8) & 0xF
        words = (c[..., 0::2] | (c[..., 1::2] << 4)).reshape(k // 512, 128, 2 * n)
    return np.ascontiguousarray(words), np.ascontiguousarray(byte.astype(np.uint8).reshape(k // 512, 16, n))


def unpack_weight(words, scales, fmt):
    g, _, n = scales.shape
    words = np.ascontiguousarray(words).reshape(g, 128, n, -1)
    if fmt == "e4m3":
        vals = words.view(ml_dtypes.float8_e4m3fn).astype(np.float64)
    else:
        nib = np.empty((g, 128, n, 4), np.uint8)
        nib[..., 0::2] = words & 0xF
        nib[..., 1::2] = words >> 4
        vals = E2M1[nib]
    vals = vals * np.repeat(np.exp2(scales.astype(np.float64) - 127.0), 8, axis=1)[..., None]
    return vals.transpose(0, 1, 3, 2).reshape(g * 512, n)


def bf(x):
    return np.asarray(x, np.float32).astype(ml_dtypes.bfloat16)


def planes(Y):
    r, m = Y.shape
    b = f64(bf(Y)).reshape(r // 32, 32, m)
    amax = np.abs(b).max(1)
    byte = np.clip(np.where(amax > 0, np.frexp(amax)[1] - 1 + 127 - 7, 1), 1, 254)
    codes = (b * np.exp2(127.0 - byte)[:, None, :]).reshape(r, m).astype(np.float32).astype(ml_dtypes.float8_e4m3fn).view(np.uint8)
    words = codes.reshape(r // 512, 128, 4, m).transpose(0, 1, 3, 2)
    return np.ascontiguousarray(words), np.ascontiguousarray(byte.astype(np.uint8).reshape(r // 512, 16, m))


D, T, I, C, Q, E = 512, 2048, 512, 1024, 256, 512


def setup_inputs():
    n = np.random.standard_normal
    idx = np.random.permutation(T)[:I]
    idx2 = np.stack([np.random.randint(0, C, I) for _ in range(8)])
    fd = mx_kscale(D)
    fi = mx_kscale(I)
    keysp = pack_weight(n((D, T)) / fd[:, None], "e2m1")
    return {
        "query": (n((D, Q)) * 0.25 / np.sqrt(D) * fd[:, None]).astype(np.float32),
        "keys_words": keysp[0],
        "keys_scales": keysp[1],
        "vbook": (n((E, C))).astype(np.float32),
        "size": (np.random.uniform(0.5, 2.0, (1, I)) * fi).astype(np.float32),
        "vsc": (np.random.uniform(0.5, 2.0, (I, 1)) / fi[:, None]).astype(np.float32),
        "offs": striped(idx),
        "offs2": striped8(idx2),
    }


def reference(query, keys_words, keys_scales, vbook, size, vsc, offs, offs2):
    idx = unstriped(offs)
    idx2 = unstriped8(offs2)
    keysu = unpack_weight(keys_words, keys_scales, "e2m1")
    queryq = mxq(f64(query), 0, "e4m3")
    keysidxg = keysu[:, idx]
    a = queryq.T @ keysidxg
    p = np.exp(a - np.max(a, axis=1, keepdims=True))
    w = p * f64(size) / np.sum(p, axis=1, keepdims=True)
    wt = w.T
    v = pick8(f64(vbook), idx2, 64).T
    vv = v * f64(vsc)
    vvq = mxq(vv, 0, "e4m3")
    wtq = mxq(wt, 0, "e4m3")
    o = vvq.T @ wtq
    words, scales = planes(o)
    return o, words, scales

@@ -1,0 +1,216 @@
+from contextlib import ExitStack
+
+import concourse.mybir as mybir
+from concourse.masks import make_identity
+
+D, T, I, C, Q, E = 512, 2048, 512, 1024, 256, 512
+FLOPS = 2 * D * Q * I + 2 * I * E * Q
+
+F32 = mybir.dt.float32
+BF16 = mybir.dt.bfloat16
+I32 = mybir.dt.int32
+U32 = mybir.dt.uint32
+U16 = mybir.dt.uint16
+U8 = mybir.dt.uint8
+FP8X4 = mybir.dt.float8_e4m3fn_x4
+FP4X4 = mybir.dt.float4_e2m1fn_x4
+MULT = mybir.AluOpType.mult
+MAX = mybir.AluOpType.max
+EXP = mybir.ActivationFunctionType.Exp
+AX = mybir.AxisListType.X
+
+P = 128
+PACK = 4
+HALVES = Q // P
+
+
+def tile_attend_pqvalues_pl_kernel(tc, query, keys_words, keys_scales, vbook, size, vsc, offs, offs2, out_0, out_1, out_2):
+    nc = tc.nc
+    with ExitStack() as ctx:
+        sb = ctx.enter_context(tc.tile_pool(name="sb", bufs=1))
+        ps = ctx.enter_context(tc.psum_pool(name="ps", bufs=1))
+
+        def sbt(name, shape, dtype):
+            return sb.tile(shape, dtype, name=name, align_bytes=64)
+
+        def bank(name, shape, tag):
+            return ps.tile(shape, F32, name=name, tag=tag)
+
+        key_list = sbt("key_list", [P, I // 16], U16)
+        code_lists = sbt("code_lists", [P, I // 16], U16)
+        key_words = sbt("key_words", [P, T], U16)
+        key_scales = sbt("key_scales", [P, T], U8)
+        ident = sbt("ident", [P, P], F32)
+        vsc_cols = sbt("vsc_cols", [P, PACK], F32)
+        size_cols = sbt("size_cols", [P, PACK], F32)
+        books = [sbt("book%d" % t, [P, C], F32) for t in range(PACK)]
+        q_raw = [sbt("q_raw%d" % h, [P, PACK, P], F32) for h in range(HALVES)]
+
+        warm_in = sbt("warm_in", [P, 1], F32)
+        nc.vector.memset(key_scales[:].bitcast(I32), 0)
+        nc.gpsimd.memset(warm_in[:], 0.0)
+        make_identity(nc, ident[:])
+
+        book_rows = vbook.rearrange("(p t) c -> p t c", t=PACK)
+        q_rows = query.rearrange("(p t) q -> p t q", t=PACK)
+        nc.sync.dma_start(key_list[:], offs)
+        nc.sync.dma_start(code_lists[:], offs2)
+        nc.sync.dma_start(vsc_cols[:], vsc.rearrange("(s r) o -> s (r o)", r=PACK))
+        for quad in range(4):
+            nc.sync.dma_start(key_scales[32 * quad : 32 * quad + 4, :].bitcast(I32), keys_scales[0, 4 * quad : 4 * quad + 4, :].bitcast(I32))
+        nc.sync.dma_start(key_words[:].bitcast(I32), keys_words[0].bitcast(I32))
+        nc.sync.dma_start(books[0][:], book_rows[:, 0, :])
+        nc.sync.dma_start(q_raw[0][:], q_rows[:, :, 0:P])
+        nc.sync.dma_start(books[1][:], book_rows[:, 1, :])
+        nc.sync.dma_start(q_raw[1][:], q_rows[:, :, P : 2 * P])
+        nc.sync.dma_start(books[2][:], book_rows[:, 2, :])
+        nc.sync.dma_start(books[3][:], book_rows[:, 3, :])
+        nc.sync.dma_start(size_cols[:], size.rearrange("o (s r) -> s (o r)", r=PACK))
+
+        warm = sbt("warm", [P, 1], F32)
+        nc.scalar.activation(warm[:], warm_in[:], EXP)
+
+        def spread(cols, name, tag):
+            rows = bank(name, [P, PACK, P], tag)
+            for r in range(PACK):
+                nc.tensor.transpose(rows[:, r, :], cols[:, r : r + 1].to_broadcast([P, P]), ident[:])
+            return rows
+
+        vsc_bank = spread(vsc_cols, "vsc_bank", "vsc")
+        vsc_row = sbt("vsc_row", [P, I], F32)
+        nc.scalar.copy(vsc_row[:].rearrange("p (s r) -> p s r", r=PACK), vsc_bank[:].rearrange("p r s -> p s r"))
+        size_bank = spread(size_cols, "size_bank", "size")
+
+        kg_scales = sbt("kg_scales", [P, I], U8)
+        kg_words = sbt("kg_words", [P, I], U16)
+        nc.vector.tensor_copy(kg_scales[:], key_scales[:].indirect(key_list[:]))
+        nc.vector.tensor_copy(kg_words[:], key_words[:].indirect(key_list[:]))
+
+        vv = [sbt("vv%d" % t, [P, I], F32) for t in range(PACK)]
+        vv_bf = [sbt("vv_bf%d" % t, [P, I], BF16) for t in range(PACK)]
+        vv_in = sbt("vv_in", [P, E * PACK], BF16)
+        vv_codes = sbt("vv_codes", [P, E], U32)
+        vv_scales = sbt("vv_scales", [P, E], U8)
+
+        def gather_values(t):
+            nc.vector.tensor_tensor(vv[t][:], books[t][:].indirect(code_lists[:]), vsc_row[:], MULT)
+
+        def turn_values(t):
+            nc.scalar.copy(
+                vv_bf[t][:].rearrange("p (u s e) -> p u s e", u=2, e=2),
+                vv[t][:].rearrange("p (s u e) -> p u s e", u=2, e=2),
+            )
+            words = vv_bf[t][:].bitcast(F32)
+            turned = bank("v_turned%d" % t, [P, 2, P], "v%d" % (t % 2))
+            for u in range(2):
+                nc.tensor.transpose(turned[:, u, :], words[:, u * P : (u + 1) * P], ident[:])
+            nc.scalar.copy(vv_in[:, t * I : (t + 1) * I].bitcast(F32).rearrange("s (p u) -> s p u", u=2), turned[:].rearrange("s u p -> s p u"))
+
+        def quantise_values():
+            nc.vector.quantize_mx(out=vv_codes[:].bitcast(FP8X4), scales=vv_scales[:], in_=vv_in[:])
+
+        q_in = [sbt("q_in%d" % h, [P, P * PACK], BF16) for h in range(HALVES)]
+        q_codes = [sbt("q_codes%d" % h, [P, P], U32) for h in range(HALVES)]
+        q_scales = [sbt("q_scales%d" % h, [P, P], U8) for h in range(HALVES)]
+        scores = [None] * HALVES
+
+        def score(h):
+            nc.scalar.copy(
+                q_in[h][:].rearrange("p (c j t) -> p c t j", j=4, t=PACK),
+                q_raw[h][:].rearrange("p t (c j) -> p c t j", j=4),
+            )
+            nc.vector.quantize_mx(out=q_codes[h][:].bitcast(FP8X4), scales=q_scales[h][:], in_=q_in[h][:])
+            scores[h] = bank("scores%d" % h, [P, I], "s%d" % h)
+            nc.tensor.matmul_mx(
+                out=scores[h][:],
+                lhsT=q_codes[h][:].bitcast(FP8X4),
+                lhsT_scale=q_scales[h][:],
+                rhs=kg_words[:].bitcast(FP4X4),
+                rhs_scale=kg_scales[:],
+                start=True,
+                stop=True,
+            )
+
+        neg_max = [sbt("neg_max%d" % h, [P, 1], F32) for h in range(HALVES)]
+        row_sum = [sbt("row_sum%d" % h, [P, 1], F32) for h in range(HALVES)]
+        inv_sum = [sbt("inv_sum%d" % h, [P, 1], F32) for h in range(HALVES)]
+        p_exp = [sbt("p_exp%d" % h, [P, I], F32) for h in range(HALVES)]
+        w_bf = [sbt("w_bf%d" % h, [P, I], BF16) for h in range(HALVES)]
+        w_in = [sbt("w_in%d" % h, [P, P * PACK], BF16) for h in range(HALVES)]
+        w_codes = [sbt("w_codes%d" % h, [P, P], U32) for h in range(HALVES)]
+        w_scales = [sbt("w_scales%d" % h, [P, P], U8) for h in range(HALVES)]
+
+        def exponentiate(h):
+            nc.vector.tensor_reduce(neg_max[h][:], scores[h][:], AX, MAX, negate=True)
+            nc.scalar.activation(p_exp[h][:], scores[h][:], EXP, bias=neg_max[h][:], accum_out=row_sum[h][:])
+
+        def weigh(h):
+            nc.vector.reciprocal(inv_sum[h][:], row_sum[h][:])
+            nc.vector.scalar_tensor_tensor(
+                w_bf[h][:].rearrange("q (s r) -> q s r", r=PACK),
+                p_exp[h][:].rearrange("q (s r) -> q s r", r=PACK),
+                inv_sum[h][:],
+                size_bank[:].rearrange("q r s -> q s r"),
+                MULT,
+                MULT,
+            )
+            words = w_bf[h][:].bitcast(F32)
+            turned = bank("w_turned%d" % h, [P, 2, P], "w%d" % h)
+            for u in range(2):
+                nc.tensor.transpose(turned[:, u, :], words[:, u : 2 * P : 2], ident[:])
+            nc.scalar.copy(w_in[h][:].bitcast(F32).rearrange("s (q u) -> s q u", u=2), turned[:].rearrange("s u q -> s q u"))
+
+        def quantise_weights(h):
+            nc.vector.quantize_mx(out=w_codes[h][:].bitcast(FP8X4), scales=w_scales[h][:], in_=w_in[h][:])
+
+        gather_values(0)
+        score(0)
+        gather_values(1)
+        score(1)
+        turn_values(0)
+        exponentiate(0)
+        exponentiate(1)
+        gather_values(2)
+        turn_values(1)
+        gather_values(3)
+        turn_values(2)
+        weigh(0)
+        turn_values(3)
+        weigh(1)
+        quantise_values()
+        for h in range(HALVES):
+            quantise_weights(h)
+
+        o_codes = sbt("o_codes", [P, Q], U32)
+        o_scales = sbt("o_scales", [P, Q], U8)
+        out_rows = out_0.rearrange("(p t) q -> p t q", t=PACK)
+        for h in range(HALVES):
+            cols = slice(h * P, (h + 1) * P)
+            acc = bank("acc%d" % h, [P, PACK, P], "s%d" % h)
+            for t in range(PACK):
+                nc.tensor.matmul_mx(
+                    out=acc[:, t, :],
+                    lhsT=vv_codes[:, t * P : (t + 1) * P].bitcast(FP8X4),
+                    lhsT_scale=vv_scales[:, t * P : (t + 1) * P],
+                    rhs=w_codes[h][:].bitcast(FP8X4),
+                    rhs_scale=w_scales[h][:],
+                    start=True,
+                    stop=True,
+                )
+            o_f32 = sbt("o_f32_%d" % h, [P, PACK, P], F32)
+            o_in = sbt("o_in%d" % h, [P, P * PACK], BF16)
+            if h == 0:
+                nc.scalar.copy(o_f32[:], acc[:])
+                nc.scalar.copy(
+                    o_in[:].rearrange("p (c j t) -> p c t j", j=4, t=PACK),
+                    o_f32[:].rearrange("p t (c j) -> p c t j", j=4),
+                )
+            else:
+                nc.vector.tensor_copy(o_in[:].rearrange("p (q t) -> p q t", t=PACK), acc[:].rearrange("p t q -> p q t"))
+                nc.scalar.copy(o_f32[:], acc[:])
+            nc.sync.dma_start(out_rows[:, :, cols], o_f32[:])
+            nc.vector.quantize_mx(out=o_codes[:, cols].bitcast(FP8X4), scales=o_scales[:, cols], in_=o_in[:])
+        nc.sync.dma_start(out_1[0].rearrange("p c r -> p (c r)").bitcast(I32), o_codes[:].bitcast(I32))
+        for quad in range(4):
+            queue = nc.scalar if quad % 2 == 0 else nc.sync
+            queue.dma_start(out_2[0, 4 * quad : 4 * quad + 4, :].bitcast(I32), o_scales[32 * quad : 32 * quad + 4, :].bitcast(I32))

@@ -17,6 +17,7 @@ FP4X4 = mybir.dt.float4_e2m1fn_x4
 MULT = mybir.AluOpType.mult
 MAX = mybir.AluOpType.max
 EXP = mybir.ActivationFunctionType.Exp
+COPY = mybir.ActivationFunctionType.Copy
 AX = mybir.AxisListType.X
 
 P = 128
@@ -30,8 +31,8 @@ def tile_attend_pqvalues_pl_kernel(tc, query, keys_words, keys_scales, vbook, si
         sb = ctx.enter_context(tc.tile_pool(name="sb", bufs=1))
         ps = ctx.enter_context(tc.psum_pool(name="ps", bufs=1))
 
-        def sbt(name, shape, dtype):
-            return sb.tile(shape, dtype, name=name, align_bytes=64)
+        def sbt(name, shape, dtype, tag=None):
+            return sb.tile(shape, dtype, name=name, tag=tag or name, align_bytes=64)
 
         def bank(name, shape, tag):
             return ps.tile(shape, F32, name=name, tag=tag)
@@ -54,18 +55,18 @@ def tile_attend_pqvalues_pl_kernel(tc, query, keys_words, keys_scales, vbook, si
         book_rows = vbook.rearrange("(p t) c -> p t c", t=PACK)
         q_rows = query.rearrange("(p t) q -> p t q", t=PACK)
         nc.sync.dma_start(key_list[:], offs)
-        nc.sync.dma_start(code_lists[:], offs2)
         nc.sync.dma_start(vsc_cols[:], vsc.rearrange("(s r) o -> s (r o)", r=PACK))
+        nc.sync.dma_start(key_words[:].bitcast(I32), keys_words[0].bitcast(I32))
+        nc.sync.dma_start(code_lists[:], offs2)
+        nc.sync.dma_start(size_cols[:], size.rearrange("o (s r) -> s (o r)", r=PACK))
         for quad in range(4):
             nc.sync.dma_start(key_scales[32 * quad : 32 * quad + 4, :].bitcast(I32), keys_scales[0, 4 * quad : 4 * quad + 4, :].bitcast(I32))
-        nc.sync.dma_start(key_words[:].bitcast(I32), keys_words[0].bitcast(I32))
         nc.sync.dma_start(books[0][:], book_rows[:, 0, :])
         nc.sync.dma_start(q_raw[0][:], q_rows[:, :, 0:P])
-        nc.sync.dma_start(books[1][:], book_rows[:, 1, :])
         nc.sync.dma_start(q_raw[1][:], q_rows[:, :, P : 2 * P])
+        nc.sync.dma_start(books[1][:], book_rows[:, 1, :])
         nc.sync.dma_start(books[2][:], book_rows[:, 2, :])
         nc.sync.dma_start(books[3][:], book_rows[:, 3, :])
-        nc.sync.dma_start(size_cols[:], size.rearrange("o (s r) -> s (o r)", r=PACK))
 
         warm = sbt("warm", [P, 1], F32)
         nc.scalar.activation(warm[:], warm_in[:], EXP)
@@ -79,20 +80,22 @@ def tile_attend_pqvalues_pl_kernel(tc, query, keys_words, keys_scales, vbook, si
         vsc_bank = spread(vsc_cols, "vsc_bank", "vsc")
         vsc_row = sbt("vsc_row", [P, I], F32)
         nc.scalar.copy(vsc_row[:].rearrange("p (s r) -> p s r", r=PACK), vsc_bank[:].rearrange("p r s -> p s r"))
-        size_bank = spread(size_cols, "size_bank", "size")
 
         kg_scales = sbt("kg_scales", [P, I], U8)
         kg_words = sbt("kg_words", [P, I], U16)
         nc.vector.tensor_copy(kg_scales[:], key_scales[:].indirect(key_list[:]))
         nc.vector.tensor_copy(kg_words[:], key_words[:].indirect(key_list[:]))
 
-        vv = [sbt("vv%d" % t, [P, I], F32) for t in range(PACK)]
+        vv = [None] * PACK
         vv_bf = [sbt("vv_bf%d" % t, [P, I], BF16) for t in range(PACK)]
-        vv_in = sbt("vv_in", [P, E * PACK], BF16)
-        vv_codes = sbt("vv_codes", [P, E], U32)
-        vv_scales = sbt("vv_scales", [P, E], U8)
+        groups = [(0,), (1,), (2,), (3,)]
+        place = {t: (g, j) for g, planes in enumerate(groups) for j, t in enumerate(planes)}
+        vv_in = [sbt("vv_in%d" % g, [P, len(planes) * I], BF16) for g, planes in enumerate(groups)]
+        vv_codes = [sbt("vv_codes%d" % g, [P, len(planes) * P], U32) for g, planes in enumerate(groups)]
+        vv_scales = [sbt("vv_scales%d" % g, [P, len(planes) * P], U8) for g, planes in enumerate(groups)]
 
         def gather_values(t):
+            vv[t] = sbt("vv%d" % t, [P, I], F32, tag=("vv0", "vv1", "vv1", "row_sum")[t])
             nc.vector.tensor_tensor(vv[t][:], books[t][:].indirect(code_lists[:]), vsc_row[:], MULT)
 
         def turn_values(t):
@@ -104,10 +107,11 @@ def tile_attend_pqvalues_pl_kernel(tc, query, keys_words, keys_scales, vbook, si
             turned = bank("v_turned%d" % t, [P, 2, P], "v%d" % (t % 2))
             for u in range(2):
                 nc.tensor.transpose(turned[:, u, :], words[:, u * P : (u + 1) * P], ident[:])
-            nc.scalar.copy(vv_in[:, t * I : (t + 1) * I].bitcast(F32).rearrange("s (p u) -> s p u", u=2), turned[:].rearrange("s u p -> s p u"))
+            g, j = place[t]
+            nc.scalar.copy(vv_in[g][:, j * I : (j + 1) * I].bitcast(F32).rearrange("s (p u) -> s p u", u=2), turned[:].rearrange("s u p -> s p u"))
 
-        def quantise_values():
-            nc.vector.quantize_mx(out=vv_codes[:].bitcast(FP8X4), scales=vv_scales[:], in_=vv_in[:])
+        def quantise_values(g):
+            nc.vector.quantize_mx(out=vv_codes[g][:].bitcast(FP8X4), scales=vv_scales[g][:], in_=vv_in[g][:])
 
         q_in = [sbt("q_in%d" % h, [P, P * PACK], BF16) for h in range(HALVES)]
         q_codes = [sbt("q_codes%d" % h, [P, P], U32) for h in range(HALVES)]
@@ -132,84 +136,94 @@ def tile_attend_pqvalues_pl_kernel(tc, query, keys_words, keys_scales, vbook, si
             )
 
         neg_max = [sbt("neg_max%d" % h, [P, 1], F32) for h in range(HALVES)]
-        row_sum = [sbt("row_sum%d" % h, [P, 1], F32) for h in range(HALVES)]
-        inv_sum = [sbt("inv_sum%d" % h, [P, 1], F32) for h in range(HALVES)]
+        row_sum = sbt("row_sum", [P, HALVES], F32)
+        inv_sum = sbt("inv_sum", [P, HALVES], F32)
         p_exp = [sbt("p_exp%d" % h, [P, I], F32) for h in range(HALVES)]
-        w_bf = [sbt("w_bf%d" % h, [P, I], BF16) for h in range(HALVES)]
         w_in = [sbt("w_in%d" % h, [P, P * PACK], BF16) for h in range(HALVES)]
         w_codes = [sbt("w_codes%d" % h, [P, P], U32) for h in range(HALVES)]
         w_scales = [sbt("w_scales%d" % h, [P, P], U8) for h in range(HALVES)]
 
         def exponentiate(h):
             nc.vector.tensor_reduce(neg_max[h][:], scores[h][:], AX, MAX, negate=True)
-            nc.scalar.activation(p_exp[h][:], scores[h][:], EXP, bias=neg_max[h][:], accum_out=row_sum[h][:])
+            nc.scalar.activation(p_exp[h][:].rearrange("q (r s) -> q r s", r=PACK), scores[h][:].rearrange("q (s r) -> q r s", r=PACK), EXP, bias=neg_max[h][:], accum_out=row_sum[:, h : h + 1])
+
+        p_turned = [None] * HALVES
+
+        def invert_sums():
+            nc.vector.reciprocal(inv_sum[:], row_sum[:])
+
+        def normalise(h):
+            p_norm = sbt("p_norm%d" % h, [P, I], F32)
+            nc.scalar.activation(p_norm[:], p_exp[h][:], COPY, scale=inv_sum[:, h : h + 1])
+            p_turned[h] = bank("p_turned%d" % h, [P, PACK, P], "w%d" % h)
+            for r in range(PACK):
+                nc.tensor.transpose(p_turned[h][:, r, :], p_norm[:, r * P : (r + 1) * P], ident[:])
 
         def weigh(h):
-            nc.vector.reciprocal(inv_sum[h][:], row_sum[h][:])
-            nc.vector.scalar_tensor_tensor(
-                w_bf[h][:].rearrange("q (s r) -> q s r", r=PACK),
-                p_exp[h][:].rearrange("q (s r) -> q s r", r=PACK),
-                inv_sum[h][:],
-                size_bank[:].rearrange("q r s -> q s r"),
-                MULT,
+            nc.vector.tensor_tensor(
+                w_in[h][:].rearrange("s (q r) -> s q r", r=PACK),
+                p_turned[h][:].rearrange("s r q -> s q r"),
+                size_cols[:].unsqueeze(1).to_broadcast([P, P, PACK]),
                 MULT,
             )
-            words = w_bf[h][:].bitcast(F32)
-            turned = bank("w_turned%d" % h, [P, 2, P], "w%d" % h)
-            for u in range(2):
-                nc.tensor.transpose(turned[:, u, :], words[:, u : 2 * P : 2], ident[:])
-            nc.scalar.copy(w_in[h][:].bitcast(F32).rearrange("s (q u) -> s q u", u=2), turned[:].rearrange("s u q -> s q u"))
 
         def quantise_weights(h):
             nc.vector.quantize_mx(out=w_codes[h][:].bitcast(FP8X4), scales=w_scales[h][:], in_=w_in[h][:])
 
         gather_values(0)
         score(0)
-        gather_values(1)
         score(1)
+        gather_values(1)
         turn_values(0)
         exponentiate(0)
         exponentiate(1)
-        gather_values(2)
         turn_values(1)
-        gather_values(3)
+        gather_values(2)
+        invert_sums()
         turn_values(2)
-        weigh(0)
+        quantise_values(0)
+        quantise_values(1)
+        normalise(0)
+        normalise(1)
+        gather_values(3)
         turn_values(3)
+        quantise_values(2)
+        weigh(0)
         weigh(1)
-        quantise_values()
-        for h in range(HALVES):
-            quantise_weights(h)
+        quantise_weights(0)
+        quantise_weights(1)
+        quantise_values(3)
 
         o_codes = sbt("o_codes", [P, Q], U32)
         o_scales = sbt("o_scales", [P, Q], U8)
         out_rows = out_0.rearrange("(p t) q -> p t q", t=PACK)
-        for h in range(HALVES):
-            cols = slice(h * P, (h + 1) * P)
-            acc = bank("acc%d" % h, [P, PACK, P], "s%d" % h)
-            for t in range(PACK):
+        acc = [bank("acc%d" % h, [P, PACK, P], "s%d" % h) for h in range(HALVES)]
+        for t in range(PACK):
+            for h in range(HALVES):
                 nc.tensor.matmul_mx(
-                    out=acc[:, t, :],
-                    lhsT=vv_codes[:, t * P : (t + 1) * P].bitcast(FP8X4),
-                    lhsT_scale=vv_scales[:, t * P : (t + 1) * P],
+                    out=acc[h][:, t, :],
+                    lhsT=vv_codes[t][:].bitcast(FP8X4),
+                    lhsT_scale=vv_scales[t][:],
                     rhs=w_codes[h][:].bitcast(FP8X4),
                     rhs_scale=w_scales[h][:],
                     start=True,
                     stop=True,
                 )
-            o_f32 = sbt("o_f32_%d" % h, [P, PACK, P], F32)
-            o_in = sbt("o_in%d" % h, [P, P * PACK], BF16)
-            if h == 0:
-                nc.scalar.copy(o_f32[:], acc[:])
-                nc.scalar.copy(
-                    o_in[:].rearrange("p (c j t) -> p c t j", j=4, t=PACK),
-                    o_f32[:].rearrange("p t (c j) -> p c t j", j=4),
-                )
-            else:
-                nc.vector.tensor_copy(o_in[:].rearrange("p (q t) -> p q t", t=PACK), acc[:].rearrange("p t q -> p q t"))
-                nc.scalar.copy(o_f32[:], acc[:])
-            nc.sync.dma_start(out_rows[:, :, cols], o_f32[:])
-            nc.vector.quantize_mx(out=o_codes[:, cols].bitcast(FP8X4), scales=o_scales[:, cols], in_=o_in[:])
+        o_f32 = [sbt("o_f32_%d" % h, [P, PACK, P], F32) for h in range(HALVES)]
+        o_in = [sbt("o_in%d" % h, [P, P * PACK], BF16) for h in range(HALVES)]
+        nc.scalar.copy(o_f32[0][:], acc[0][:])
+        nc.sync.dma_start(out_rows[:, :, 0:P], o_f32[0][:])
+        nc.vector.tensor_copy(o_in[1][:].rearrange("p (q t) -> p q t", t=PACK), acc[1][:].rearrange("p t q -> p q t"))
+        for pair in (slice(0, 2), slice(2, 4)):
+            nc.scalar.copy(o_f32[1][:, pair, :], acc[1][:, pair, :])
+            nc.sync.dma_start(out_rows[:, pair, P : 2 * P], o_f32[1][:, pair, :])
+        nc.vector.tensor_copy(
+            o_in[0][:].rearrange("p (c j t) -> p c t j", j=4, t=PACK),
+            o_f32[0][:].rearrange("p t (c j) -> p c t j", j=4),
+        )
+        for h in (1, 0):
+            cols = slice(h * P, (h + 1) * P)
+            nc.vector.quantize_mx(out=o_codes[:, cols].bitcast(FP8X4), scales=o_scales[:, cols], in_=o_in[h][:])
         nc.sync.dma_start(out_1[0].rearrange("p c r -> p (c r)").bitcast(I32), o_codes[:].bitcast(I32))
         for quad in range(4):
             queue = nc.scalar if quad % 2 == 0 else nc.sync

@@ -61,9 +61,9 @@ def tile_attend_pqvalues_pl_kernel(tc, query, keys_words, keys_scales, vbook, si
         nc.sync.dma_start(size_cols[:], size.rearrange("o (s r) -> s (o r)", r=PACK))
         for quad in range(4):
             nc.sync.dma_start(key_scales[32 * quad : 32 * quad + 4, :].bitcast(I32), keys_scales[0, 4 * quad : 4 * quad + 4, :].bitcast(I32))
-        nc.sync.dma_start(books[0][:], book_rows[:, 0, :])
         nc.sync.dma_start(q_raw[0][:], q_rows[:, :, 0:P])
         nc.sync.dma_start(q_raw[1][:], q_rows[:, :, P : 2 * P])
+        nc.sync.dma_start(books[0][:], book_rows[:, 0, :])
         nc.sync.dma_start(books[1][:], book_rows[:, 1, :])
         nc.sync.dma_start(books[2][:], book_rows[:, 2, :])
         nc.sync.dma_start(books[3][:], book_rows[:, 3, :])
@@ -87,6 +87,7 @@ def tile_attend_pqvalues_pl_kernel(tc, query, keys_words, keys_scales, vbook, si
         nc.vector.tensor_copy(kg_words[:], key_words[:].indirect(key_list[:]))
 
         vv = [None] * PACK
+        pieces = (1, 1, 1, 1)
         vv_bf = [sbt("vv_bf%d" % t, [P, I], BF16) for t in range(PACK)]
         groups = [(0,), (1,), (2,), (3,)]
         place = {t: (g, j) for g, planes in enumerate(groups) for j, t in enumerate(planes)}
@@ -95,14 +96,19 @@ def tile_attend_pqvalues_pl_kernel(tc, query, keys_words, keys_scales, vbook, si
         vv_scales = [sbt("vv_scales%d" % g, [P, len(planes) * P], U8) for g, planes in enumerate(groups)]
 
         def gather_values(t):
-            vv[t] = sbt("vv%d" % t, [P, I], F32, tag=("vv0", "vv1", "vv1", "row_sum")[t])
-            nc.vector.tensor_tensor(vv[t][:], books[t][:].indirect(code_lists[:]), vsc_row[:], MULT)
+            vv[t] = sbt("vv%d" % t, [P, I], F32, tag="row_sum" if t == 2 else None)
+            n = I // pieces[t]
+            for k in range(pieces[t]):
+                slots = slice(k * n, (k + 1) * n)
+                nc.vector.tensor_tensor(vv[t][:, slots], books[t][:].indirect(code_lists[:, k * n // 16 : (k + 1) * n // 16]), vsc_row[:, slots], MULT)
 
         def turn_values(t):
-            nc.scalar.copy(
-                vv_bf[t][:].rearrange("p (u s e) -> p u s e", u=2, e=2),
-                vv[t][:].rearrange("p (s u e) -> p u s e", u=2, e=2),
-            )
+            m = P // pieces[t]
+            for k in range(pieces[t]):
+                nc.scalar.copy(
+                    vv_bf[t][:].rearrange("p (u s e) -> p u s e", u=2, e=2)[:, :, k * m : (k + 1) * m, :],
+                    vv[t][:].rearrange("p (s u e) -> p u s e", u=2, e=2)[:, :, k * m : (k + 1) * m, :],
+                )
             words = vv_bf[t][:].bitcast(F32)
             turned = bank("v_turned%d" % t, [P, 2, P], "v%d" % (t % 2))
             for u in range(2):
@@ -170,53 +176,64 @@ def tile_attend_pqvalues_pl_kernel(tc, query, keys_words, keys_scales, vbook, si
         def quantise_weights(h):
             nc.vector.quantize_mx(out=w_codes[h][:].bitcast(FP8X4), scales=w_scales[h][:], in_=w_in[h][:])
 
-        gather_values(0)
         score(0)
         score(1)
-        gather_values(1)
-        turn_values(0)
+        gather_values(0)
         exponentiate(0)
         exponentiate(1)
-        turn_values(1)
-        gather_values(2)
+        turn_values(0)
+        gather_values(1)
         invert_sums()
-        turn_values(2)
-        quantise_values(0)
-        quantise_values(1)
+        turn_values(1)
         normalise(0)
         normalise(1)
+        gather_values(2)
+        turn_values(2)
         gather_values(3)
         turn_values(3)
-        quantise_values(2)
+        quantise_values(0)
+        quantise_values(1)
         weigh(0)
         weigh(1)
         quantise_weights(0)
         quantise_weights(1)
+        quantise_values(2)
         quantise_values(3)
 
         o_codes = sbt("o_codes", [P, Q], U32)
         o_scales = sbt("o_scales", [P, Q], U8)
         out_rows = out_0.rearrange("(p t) q -> p t q", t=PACK)
-        acc = [bank("acc%d" % h, [P, PACK, P], "s%d" % h) for h in range(HALVES)]
+        acc_early = bank("acc_early", [P, PACK - 1, P], "s0")
+        acc_last = bank("acc_last", [P, P], "vsc")
+        acc1 = bank("acc1", [P, PACK, P], "s1")
+
+        def product(out, t, h):
+            nc.tensor.matmul_mx(
+                out=out,
+                lhsT=vv_codes[t][:].bitcast(FP8X4),
+                lhsT_scale=vv_scales[t][:],
+                rhs=w_codes[h][:].bitcast(FP8X4),
+                rhs_scale=w_scales[h][:],
+                start=True,
+                stop=True,
+            )
+
+        for t in range(PACK - 1):
+            product(acc_early[:, t, :], t, 0)
         for t in range(PACK):
-            for h in range(HALVES):
-                nc.tensor.matmul_mx(
-                    out=acc[h][:, t, :],
-                    lhsT=vv_codes[t][:].bitcast(FP8X4),
-                    lhsT_scale=vv_scales[t][:],
-                    rhs=w_codes[h][:].bitcast(FP8X4),
-                    rhs_scale=w_scales[h][:],
-                    start=True,
-                    stop=True,
-                )
+            product(acc1[:, t, :], t, 1)
+        product(acc_last[:], PACK - 1, 0)
         o_f32 = [sbt("o_f32_%d" % h, [P, PACK, P], F32) for h in range(HALVES)]
         o_in = [sbt("o_in%d" % h, [P, P * PACK], BF16) for h in range(HALVES)]
-        nc.scalar.copy(o_f32[0][:], acc[0][:])
-        nc.sync.dma_start(out_rows[:, :, 0:P], o_f32[0][:])
-        nc.vector.tensor_copy(o_in[1][:].rearrange("p (q t) -> p q t", t=PACK), acc[1][:].rearrange("p t q -> p q t"))
+        nc.scalar.copy(o_f32[0][:, 0 : PACK - 1, :], acc_early[:])
+        nc.sync.dma_start(out_rows[:, 0 : PACK - 1, 0:P], o_f32[0][:, 0 : PACK - 1, :])
+        nc.scalar.copy(o_f32[0][:, PACK - 1, :], acc_last[:])
+        nc.sync.dma_start(out_rows[:, PACK - 1, 0:P], o_f32[0][:, PACK - 1, :])
+        nc.vector.tensor_copy(o_in[1][:].rearrange("p (q t) -> p q t", t=PACK), acc1[:].rearrange("p t q -> p q t"))
         for pair in (slice(0, 2), slice(2, 4)):
-            nc.scalar.copy(o_f32[1][:, pair, :], acc[1][:, pair, :])
-            nc.sync.dma_start(out_rows[:, pair, P : 2 * P], o_f32[1][:, pair, :])
+            nc.scalar.copy(o_f32[1][:, pair, :], acc1[:, pair, :])
+            queue = nc.sync if pair.start == 0 else nc.scalar
+            queue.dma_start(out_rows[:, pair, P : 2 * P], o_f32[1][:, pair, :])
         nc.vector.tensor_copy(
             o_in[0][:].rearrange("p (c j t) -> p c t j", j=4, t=PACK),
             o_f32[0][:].rearrange("p t (c j) -> p c t j", j=4),
@@ -226,5 +243,5 @@ def tile_attend_pqvalues_pl_kernel(tc, query, keys_words, keys_scales, vbook, si
             nc.vector.quantize_mx(out=o_codes[:, cols].bitcast(FP8X4), scales=o_scales[:, cols], in_=o_in[h][:])
         nc.sync.dma_start(out_1[0].rearrange("p c r -> p (c r)").bitcast(I32), o_codes[:].bitcast(I32))
         for quad in range(4):
-            queue = nc.scalar if quad % 2 == 0 else nc.sync
+            queue = nc.scalar if quad == 3 else nc.sync
             queue.dma_start(out_2[0, 4 * quad : 4 * quad + 4, :].bitcast(I32), o_scales[32 * quad : 32 * quad + 4, :].bitcast(I32))

@@ -54,63 +54,83 @@ def tile_attend_pqvalues_pl_kernel(tc, query, keys_words, keys_scales, vbook, si
 
         book_rows = vbook.rearrange("(p t) c -> p t c", t=PACK)
         q_rows = query.rearrange("(p t) q -> p t q", t=PACK)
+
+        def load_scale_rows():
+            for quad in range(4):
+                nc.sync.dma_start(key_scales[32 * quad : 32 * quad + 4, :].bitcast(I32), keys_scales[0, 4 * quad : 4 * quad + 4, :].bitcast(I32))
+
+        def load_queries(h):
+            nc.sync.dma_start(q_raw[h][:], q_rows[:, :, h * P : (h + 1) * P])
+
+        def load_book(t):
+            nc.sync.dma_start(books[t][:], book_rows[:, t, :])
+
         nc.sync.dma_start(key_list[:], offs)
         nc.sync.dma_start(vsc_cols[:], vsc.rearrange("(s r) o -> s (r o)", r=PACK))
         nc.sync.dma_start(key_words[:].bitcast(I32), keys_words[0].bitcast(I32))
         nc.sync.dma_start(code_lists[:], offs2)
+        load_queries(0)
+        load_scale_rows()
+        load_queries(1)
+        load_book(0)
+        load_book(1)
+        load_book(2)
+        load_book(3)
         nc.sync.dma_start(size_cols[:], size.rearrange("o (s r) -> s (o r)", r=PACK))
-        for quad in range(4):
-            nc.sync.dma_start(key_scales[32 * quad : 32 * quad + 4, :].bitcast(I32), keys_scales[0, 4 * quad : 4 * quad + 4, :].bitcast(I32))
-        nc.sync.dma_start(q_raw[0][:], q_rows[:, :, 0:P])
-        nc.sync.dma_start(q_raw[1][:], q_rows[:, :, P : 2 * P])
-        nc.sync.dma_start(books[0][:], book_rows[:, 0, :])
-        nc.sync.dma_start(books[1][:], book_rows[:, 1, :])
-        nc.sync.dma_start(books[2][:], book_rows[:, 2, :])
-        nc.sync.dma_start(books[3][:], book_rows[:, 3, :])
 
         warm = sbt("warm", [P, 1], F32)
         nc.scalar.activation(warm[:], warm_in[:], EXP)
 
-        def spread(cols, name, tag):
-            rows = bank(name, [P, PACK, P], tag)
-            for r in range(PACK):
-                nc.tensor.transpose(rows[:, r, :], cols[:, r : r + 1].to_broadcast([P, P]), ident[:])
-            return rows
+        q_in = [sbt("q_in%d" % h, [P, P * PACK], BF16) for h in range(HALVES)]
+        q_codes = [sbt("q_codes%d" % h, [P, P], U32) for h in range(HALVES)]
+        q_scales = [sbt("q_scales%d" % h, [P, P], U8) for h in range(HALVES)]
 
-        vsc_bank = spread(vsc_cols, "vsc_bank", "vsc")
-        vsc_row = sbt("vsc_row", [P, I], F32)
-        nc.scalar.copy(vsc_row[:].rearrange("p (s r) -> p s r", r=PACK), vsc_bank[:].rearrange("p r s -> p s r"))
+        def round_queries(h):
+            nc.scalar.copy(
+                q_in[h][:].rearrange("p (c j t) -> p c t j", j=4, t=PACK),
+                q_raw[h][:].rearrange("p t (c j) -> p c t j", j=4),
+            )
+
+        def quantise_queries(h):
+            nc.vector.quantize_mx(out=q_codes[h][:].bitcast(FP8X4), scales=q_scales[h][:], in_=q_in[h][:])
+
+        held = {}
+
+        def spread_vsc():
+            vsc_bank = bank("vsc_bank", [P, PACK, P], "a")
+            for r in range(PACK):
+                nc.tensor.transpose(vsc_bank[:, r, :], vsc_cols[:, r : r + 1].to_broadcast([P, P]), ident[:])
+            held["vsc_row"] = sbt("vsc_row", [P, I], F32, tag="q_raw0")
+            nc.scalar.copy(held["vsc_row"][:].rearrange("p (s r) -> p s r", r=PACK), vsc_bank[:].rearrange("p r s -> p s r"))
 
         kg_scales = sbt("kg_scales", [P, I], U8)
         kg_words = sbt("kg_words", [P, I], U16)
-        nc.vector.tensor_copy(kg_scales[:], key_scales[:].indirect(key_list[:]))
-        nc.vector.tensor_copy(kg_words[:], key_words[:].indirect(key_list[:]))
+
+        def gather_key_words():
+            nc.vector.tensor_copy(kg_words[:], key_words[:].indirect(key_list[:]))
+
+        def gather_key_scales():
+            nc.vector.tensor_copy(kg_scales[:], key_scales[:].indirect(key_list[:]))
 
         vv = [None] * PACK
-        pieces = (1, 1, 1, 1)
         vv_bf = [sbt("vv_bf%d" % t, [P, I], BF16) for t in range(PACK)]
-        groups = [(0,), (1,), (2,), (3,)]
+        groups = [(0, 1), (2,), (3,)]
         place = {t: (g, j) for g, planes in enumerate(groups) for j, t in enumerate(planes)}
         vv_in = [sbt("vv_in%d" % g, [P, len(planes) * I], BF16) for g, planes in enumerate(groups)]
         vv_codes = [sbt("vv_codes%d" % g, [P, len(planes) * P], U32) for g, planes in enumerate(groups)]
         vv_scales = [sbt("vv_scales%d" % g, [P, len(planes) * P], U8) for g, planes in enumerate(groups)]
 
-        def gather_values(t):
-            vv[t] = sbt("vv%d" % t, [P, I], F32, tag="row_sum" if t == 2 else None)
-            n = I // pieces[t]
-            for k in range(pieces[t]):
-                slots = slice(k * n, (k + 1) * n)
-                nc.vector.tensor_tensor(vv[t][:, slots], books[t][:].indirect(code_lists[:, k * n // 16 : (k + 1) * n // 16]), vsc_row[:, slots], MULT)
+        def gather_values(t, tag=None):
+            vv[t] = sbt("vv%d" % t, [P, I], F32, tag=tag)
+            nc.vector.tensor_tensor(vv[t][:], books[t][:].indirect(code_lists[:]), held["vsc_row"][:], MULT)
 
         def turn_values(t):
-            m = P // pieces[t]
-            for k in range(pieces[t]):
-                nc.scalar.copy(
-                    vv_bf[t][:].rearrange("p (u s e) -> p u s e", u=2, e=2)[:, :, k * m : (k + 1) * m, :],
-                    vv[t][:].rearrange("p (s u e) -> p u s e", u=2, e=2)[:, :, k * m : (k + 1) * m, :],
-                )
+            nc.scalar.copy(
+                vv_bf[t][:].rearrange("p (u s e) -> p u s e", u=2, e=2),
+                vv[t][:].rearrange("p (s u e) -> p u s e", u=2, e=2),
+            )
             words = vv_bf[t][:].bitcast(F32)
-            turned = bank("v_turned%d" % t, [P, 2, P], "v%d" % (t % 2))
+            turned = bank("v_turned%d" % t, [P, 2, P], "cd"[t % 2])
             for u in range(2):
                 nc.tensor.transpose(turned[:, u, :], words[:, u * P : (u + 1) * P], ident[:])
             g, j = place[t]
@@ -119,18 +139,10 @@ def tile_attend_pqvalues_pl_kernel(tc, query, keys_words, keys_scales, vbook, si
         def quantise_values(g):
             nc.vector.quantize_mx(out=vv_codes[g][:].bitcast(FP8X4), scales=vv_scales[g][:], in_=vv_in[g][:])
 
-        q_in = [sbt("q_in%d" % h, [P, P * PACK], BF16) for h in range(HALVES)]
-        q_codes = [sbt("q_codes%d" % h, [P, P], U32) for h in range(HALVES)]
-        q_scales = [sbt("q_scales%d" % h, [P, P], U8) for h in range(HALVES)]
         scores = [None] * HALVES
 
         def score(h):
-            nc.scalar.copy(
-                q_in[h][:].rearrange("p (c j t) -> p c t j", j=4, t=PACK),
-                q_raw[h][:].rearrange("p t (c j) -> p c t j", j=4),
-            )
-            nc.vector.quantize_mx(out=q_codes[h][:].bitcast(FP8X4), scales=q_scales[h][:], in_=q_in[h][:])
-            scores[h] = bank("scores%d" % h, [P, I], "s%d" % h)
+            scores[h] = bank("scores%d" % h, [P, I], "ab"[h])
             nc.tensor.matmul_mx(
                 out=scores[h][:],
                 lhsT=q_codes[h][:].bitcast(FP8X4),
@@ -141,16 +153,19 @@ def tile_attend_pqvalues_pl_kernel(tc, query, keys_words, keys_scales, vbook, si
                 stop=True,
             )
 
-        neg_max = [sbt("neg_max%d" % h, [P, 1], F32) for h in range(HALVES)]
+        neg_max = [None] * HALVES
         row_sum = sbt("row_sum", [P, HALVES], F32)
         inv_sum = sbt("inv_sum", [P, HALVES], F32)
         p_exp = [sbt("p_exp%d" % h, [P, I], F32) for h in range(HALVES)]
-        w_in = [sbt("w_in%d" % h, [P, P * PACK], BF16) for h in range(HALVES)]
-        w_codes = [sbt("w_codes%d" % h, [P, P], U32) for h in range(HALVES)]
+        w_in = [None] * HALVES
+        w_codes = [None] * HALVES
         w_scales = [sbt("w_scales%d" % h, [P, P], U8) for h in range(HALVES)]
 
-        def exponentiate(h):
+        def row_max(h, tag=None):
+            neg_max[h] = sbt("neg_max%d" % h, [P, 1], F32, tag=tag)
             nc.vector.tensor_reduce(neg_max[h][:], scores[h][:], AX, MAX, negate=True)
+
+        def exponentiate(h):
             nc.scalar.activation(p_exp[h][:].rearrange("q (r s) -> q r s", r=PACK), scores[h][:].rearrange("q (s r) -> q r s", r=PACK), EXP, bias=neg_max[h][:], accum_out=row_sum[:, h : h + 1])
 
         p_turned = [None] * HALVES
@@ -161,11 +176,12 @@ def tile_attend_pqvalues_pl_kernel(tc, query, keys_words, keys_scales, vbook, si
         def normalise(h):
             p_norm = sbt("p_norm%d" % h, [P, I], F32)
             nc.scalar.activation(p_norm[:], p_exp[h][:], COPY, scale=inv_sum[:, h : h + 1])
-            p_turned[h] = bank("p_turned%d" % h, [P, PACK, P], "w%d" % h)
+            p_turned[h] = bank("p_turned%d" % h, [P, PACK, P], "ef"[h])
             for r in range(PACK):
                 nc.tensor.transpose(p_turned[h][:, r, :], p_norm[:, r * P : (r + 1) * P], ident[:])
 
-        def weigh(h):
+        def weigh(h, tag=None):
+            w_in[h] = sbt("w_in%d" % h, [P, P * PACK], BF16, tag=tag)
             nc.vector.tensor_tensor(
                 w_in[h][:].rearrange("s (q r) -> s q r", r=PACK),
                 p_turned[h][:].rearrange("s r q -> s q r"),
@@ -173,75 +189,90 @@ def tile_attend_pqvalues_pl_kernel(tc, query, keys_words, keys_scales, vbook, si
                 MULT,
             )
 
-        def quantise_weights(h):
+        def quantise_weights(h, tag=None):
+            w_codes[h] = sbt("w_codes%d" % h, [P, P], U32, tag=tag)
             nc.vector.quantize_mx(out=w_codes[h][:].bitcast(FP8X4), scales=w_scales[h][:], in_=w_in[h][:])
 
-        score(0)
-        score(1)
-        gather_values(0)
-        exponentiate(0)
-        exponentiate(1)
-        turn_values(0)
-        gather_values(1)
-        invert_sums()
-        turn_values(1)
-        normalise(0)
-        normalise(1)
-        gather_values(2)
-        turn_values(2)
-        gather_values(3)
-        turn_values(3)
-        quantise_values(0)
-        quantise_values(1)
-        weigh(0)
-        weigh(1)
-        quantise_weights(0)
-        quantise_weights(1)
-        quantise_values(2)
-        quantise_values(3)
-
-        o_codes = sbt("o_codes", [P, Q], U32)
-        o_scales = sbt("o_scales", [P, Q], U8)
-        out_rows = out_0.rearrange("(p t) q -> p t q", t=PACK)
-        acc_early = bank("acc_early", [P, PACK - 1, P], "s0")
-        acc_last = bank("acc_last", [P, P], "vsc")
-        acc1 = bank("acc1", [P, PACK, P], "s1")
-
         def product(out, t, h):
+            g, j = place[t]
             nc.tensor.matmul_mx(
                 out=out,
-                lhsT=vv_codes[t][:].bitcast(FP8X4),
-                lhsT_scale=vv_scales[t][:],
+                lhsT=vv_codes[g][:, j * P : (j + 1) * P].bitcast(FP8X4),
+                lhsT_scale=vv_scales[g][:, j * P : (j + 1) * P],
                 rhs=w_codes[h][:].bitcast(FP8X4),
                 rhs_scale=w_scales[h][:],
                 start=True,
                 stop=True,
             )
 
+        gather_key_words()
+        round_queries(0)
+        quantise_queries(0)
+        spread_vsc()
+        gather_key_scales()
+        round_queries(1)
+        quantise_queries(1)
+        score(0)
+        score(1)
+        gather_values(0)
+        row_max(0, tag="book0")
+        turn_values(0)
+        exponentiate(0)
+        row_max(1)
+        exponentiate(1)
+        gather_values(1, tag="q_codes1")
+        invert_sums()
+        turn_values(1)
+        normalise(0)
+        gather_values(2, tag="row_sum")
+        turn_values(2)
+        normalise(1)
+        quantise_values(0)
+        gather_values(3)
+        turn_values(3)
+        weigh(0)
+        quantise_values(1)
+        quantise_weights(0)
+        weigh(1)
+        quantise_values(2)
+        quantise_weights(1)
+
+        o_codes = sbt("o_codes", [P, Q], U32)
+        o_scales = sbt("o_scales", [P, Q], U8)
+        out_rows = out_0.rearrange("(p t) q -> p t q", t=PACK)
+        out_words = out_1[0].rearrange("p c r -> p (c r)").bitcast(I32)
+        acc_early = bank("acc_early", [P, PACK - 1, P], "a")
+        acc_last = bank("acc_last", [P, P], "g")
+        acc_pairs = [bank("acc_pair%d" % u, [P, 2, P], "bh"[u]) for u in range(2)]
         for t in range(PACK - 1):
             product(acc_early[:, t, :], t, 0)
-        for t in range(PACK):
-            product(acc1[:, t, :], t, 1)
         product(acc_last[:], PACK - 1, 0)
+        for t in range(PACK):
+            product(acc_pairs[t // 2][:, t % 2, :], t, 1)
         o_f32 = [sbt("o_f32_%d" % h, [P, PACK, P], F32) for h in range(HALVES)]
         o_in = [sbt("o_in%d" % h, [P, P * PACK], BF16) for h in range(HALVES)]
+
+        def quantise_result(h):
+            cols = slice(h * P, (h + 1) * P)
+            nc.vector.quantize_mx(out=o_codes[:, cols].bitcast(FP8X4), scales=o_scales[:, cols], in_=o_in[h][:])
+
         nc.scalar.copy(o_f32[0][:, 0 : PACK - 1, :], acc_early[:])
-        nc.sync.dma_start(out_rows[:, 0 : PACK - 1, 0:P], o_f32[0][:, 0 : PACK - 1, :])
         nc.scalar.copy(o_f32[0][:, PACK - 1, :], acc_last[:])
-        nc.sync.dma_start(out_rows[:, PACK - 1, 0:P], o_f32[0][:, PACK - 1, :])
-        nc.vector.tensor_copy(o_in[1][:].rearrange("p (q t) -> p q t", t=PACK), acc1[:].rearrange("p t q -> p q t"))
-        for pair in (slice(0, 2), slice(2, 4)):
-            nc.scalar.copy(o_f32[1][:, pair, :], acc1[:, pair, :])
-            queue = nc.sync if pair.start == 0 else nc.scalar
-            queue.dma_start(out_rows[:, pair, P : 2 * P], o_f32[1][:, pair, :])
+        nc.sync.dma_start(out_rows[:, :, 0:P], o_f32[0][:])
         nc.vector.tensor_copy(
             o_in[0][:].rearrange("p (c j t) -> p c t j", j=4, t=PACK),
             o_f32[0][:].rearrange("p t (c j) -> p c t j", j=4),
         )
-        for h in (1, 0):
-            cols = slice(h * P, (h + 1) * P)
-            nc.vector.quantize_mx(out=o_codes[:, cols].bitcast(FP8X4), scales=o_scales[:, cols], in_=o_in[h][:])
-        nc.sync.dma_start(out_1[0].rearrange("p c r -> p (c r)").bitcast(I32), o_codes[:].bitcast(I32))
+        pair_words = o_in[1][:].rearrange("p (q u e) -> p u q e", u=2, e=2)
+        nc.scalar.copy(o_f32[1][:, 0:2, :], acc_pairs[0][:])
+        nc.sync.dma_start(out_rows[:, 0:2, P : 2 * P], o_f32[1][:, 0:2, :])
+        nc.scalar.copy(pair_words[:, 0, :, :], acc_pairs[0][:].rearrange("p e q -> p q e"))
+        nc.vector.tensor_copy(pair_words[:, 1, :, :], acc_pairs[1][:].rearrange("p e q -> p q e"))
+        nc.scalar.copy(o_f32[1][:, 2:4, :], acc_pairs[1][:])
+        nc.scalar.dma_start(out_rows[:, 2:4, P : 2 * P], o_f32[1][:, 2:4, :])
+        quantise_result(0)
+        quantise_result(1)
+        nc.sync.dma_start(out_words, o_codes[:].bitcast(I32))
         for quad in range(4):
             queue = nc.scalar if quad == 3 else nc.sync
             queue.dma_start(out_2[0, 4 * quad : 4 * quad + 4, :].bitcast(I32), o_scales[32 * quad : 32 * quad + 4, :].bitcast(I32))

@@ -56,8 +56,8 @@ def tile_attend_pqvalues_pl_kernel(tc, query, keys_words, keys_scales, vbook, si
         q_rows = query.rearrange("(p t) q -> p t q", t=PACK)
 
         def load_scale_rows():
-            for quad in range(4):
-                nc.sync.dma_start(key_scales[32 * quad : 32 * quad + 4, :].bitcast(I32), keys_scales[0, 4 * quad : 4 * quad + 4, :].bitcast(I32))
+            for row in range(4):
+                nc.sync.dma_start(key_scales[row:P:32, :].bitcast(I32), keys_scales[0, row:16:4, :].bitcast(I32))
 
         def load_queries(h):
             nc.sync.dma_start(q_raw[h][:], q_rows[:, :, h * P : (h + 1) * P])
@@ -273,6 +273,6 @@ def tile_attend_pqvalues_pl_kernel(tc, query, keys_words, keys_scales, vbook, si
         quantise_result(0)
         quantise_result(1)
         nc.sync.dma_start(out_words, o_codes[:].bitcast(I32))
-        for quad in range(4):
-            queue = nc.scalar if quad == 3 else nc.sync
-            queue.dma_start(out_2[0, 4 * quad : 4 * quad + 4, :].bitcast(I32), o_scales[32 * quad : 32 * quad + 4, :].bitcast(I32))
+        for row in range(4):
+            queue = nc.scalar if row == 3 else nc.sync
+            queue.dma_start(out_2[0, row:16:4, :].bitcast(I32), o_scales[row:P:32, :].bitcast(I32))

@@ -23,6 +23,16 @@ AX = mybir.AxisListType.X
 P = 128
 PACK = 4
 HALVES = Q // P
+GROUPS = [(0, 1), (2,), (3,)]
+
+REUSE = {
+    "vsc_row": "q_raw0",
+    "neg_max0": "book0",
+    "vv1a": "q1_codes",
+    "vv1": "q1_scales",
+    "vv2": "vv1a",
+}
+OVERLAY = {}
 
 
 def tile_attend_pqvalues_pl_kernel(tc, query, keys_words, keys_scales, vbook, size, vsc, offs, offs2, out_0, out_1, out_2):
@@ -30,12 +40,22 @@ def tile_attend_pqvalues_pl_kernel(tc, query, keys_words, keys_scales, vbook, si
     with ExitStack() as ctx:
         sb = ctx.enter_context(tc.tile_pool(name="sb", bufs=1))
         ps = ctx.enter_context(tc.psum_pool(name="ps", bufs=1))
+        shared = ctx.enter_context(tc.tile_pool(name="shared", bufs=1))
+        tiles = {}
+        tags = {}
 
-        def sbt(name, shape, dtype, tag=None):
-            return sb.tile(shape, dtype, name=name, tag=tag or name, align_bytes=64)
+        def sbt(name, shape, dtype):
+            if name in OVERLAY and name not in tiles:
+                tags[name] = name
+                tiles[name] = shared.tile(shape, dtype, name=name, tag=name, align_bytes=64, offset=OVERLAY[name])
+            if name not in tiles:
+                tags[name] = tags[REUSE[name]] if name in REUSE else name
+                tiles[name] = sb.tile(shape, dtype, name=name, tag=tags[name], align_bytes=64)
+            return tiles[name]
 
         def bank(name, shape, tag):
-            return ps.tile(shape, F32, name=name, tag=tag)
+            tiles[name] = ps.tile(shape, F32, name=name, tag=tag)
+            return tiles[name]
 
         key_list = sbt("key_list", [P, I // 16], U16)
         code_lists = sbt("code_lists", [P, I // 16], U16)
@@ -56,8 +76,8 @@ def tile_attend_pqvalues_pl_kernel(tc, query, keys_words, keys_scales, vbook, si
         q_rows = query.rearrange("(p t) q -> p t q", t=PACK)
 
         def load_scale_rows():
-            for row in range(4):
-                nc.sync.dma_start(key_scales[row:P:32, :].bitcast(I32), keys_scales[0, row:16:4, :].bitcast(I32))
+            for quad in range(4):
+                nc.sync.dma_start(key_scales[32 * quad : 32 * quad + 4, :].bitcast(I32), keys_scales[0, 4 * quad : 4 * quad + 4, :].bitcast(I32))
 
         def load_queries(h):
             nc.sync.dma_start(q_raw[h][:], q_rows[:, :, h * P : (h + 1) * P])
@@ -81,126 +101,116 @@ def tile_attend_pqvalues_pl_kernel(tc, query, keys_words, keys_scales, vbook, si
         warm = sbt("warm", [P, 1], F32)
         nc.scalar.activation(warm[:], warm_in[:], EXP)
 
-        q_in = [sbt("q_in%d" % h, [P, P * PACK], BF16) for h in range(HALVES)]
-        q_codes = [sbt("q_codes%d" % h, [P, P], U32) for h in range(HALVES)]
-        q_scales = [sbt("q_scales%d" % h, [P, P], U8) for h in range(HALVES)]
+        def quantise(name, source, width):
+            codes = sbt(name + "_codes", [P, width], U32)
+            scales = sbt(name + "_scales", [P, width], U8)
+            nc.vector.quantize_mx(out=codes[:].bitcast(FP8X4), scales=scales[:], in_=source[:])
 
         def round_queries(h):
+            q_in = sbt("q_in%d" % h, [P, P * PACK], BF16)
             nc.scalar.copy(
-                q_in[h][:].rearrange("p (c j t) -> p c t j", j=4, t=PACK),
+                q_in[:].rearrange("p (c j t) -> p c t j", j=4, t=PACK),
                 q_raw[h][:].rearrange("p t (c j) -> p c t j", j=4),
             )
 
         def quantise_queries(h):
-            nc.vector.quantize_mx(out=q_codes[h][:].bitcast(FP8X4), scales=q_scales[h][:], in_=q_in[h][:])
-
-        held = {}
+            quantise("q%d" % h, tiles["q_in%d" % h], P)
 
         def spread_vsc():
             vsc_bank = bank("vsc_bank", [P, PACK, P], "a")
             for r in range(PACK):
                 nc.tensor.transpose(vsc_bank[:, r, :], vsc_cols[:, r : r + 1].to_broadcast([P, P]), ident[:])
-            held["vsc_row"] = sbt("vsc_row", [P, I], F32, tag="q_raw0")
-            nc.scalar.copy(held["vsc_row"][:].rearrange("p (s r) -> p s r", r=PACK), vsc_bank[:].rearrange("p r s -> p s r"))
-
-        kg_scales = sbt("kg_scales", [P, I], U8)
-        kg_words = sbt("kg_words", [P, I], U16)
+            vsc_row = sbt("vsc_row", [P, I], F32)
+            nc.scalar.copy(vsc_row[:].rearrange("p (s r) -> p s r", r=PACK), vsc_bank[:].rearrange("p r s -> p s r"))
 
         def gather_key_words():
-            nc.vector.tensor_copy(kg_words[:], key_words[:].indirect(key_list[:]))
+            nc.vector.tensor_copy(sbt("kg_words", [P, I], U16)[:], key_words[:].indirect(key_list[:]))
 
         def gather_key_scales():
-            nc.vector.tensor_copy(kg_scales[:], key_scales[:].indirect(key_list[:]))
+            nc.vector.tensor_copy(sbt("kg_scales", [P, I], U8)[:], key_scales[:].indirect(key_list[:]))
 
-        vv = [None] * PACK
-        vv_bf = [sbt("vv_bf%d" % t, [P, I], BF16) for t in range(PACK)]
-        groups = [(0, 1), (2,), (3,)]
-        place = {t: (g, j) for g, planes in enumerate(groups) for j, t in enumerate(planes)}
-        vv_in = [sbt("vv_in%d" % g, [P, len(planes) * I], BF16) for g, planes in enumerate(groups)]
-        vv_codes = [sbt("vv_codes%d" % g, [P, len(planes) * P], U32) for g, planes in enumerate(groups)]
-        vv_scales = [sbt("vv_scales%d" % g, [P, len(planes) * P], U8) for g, planes in enumerate(groups)]
+        place = {t: (g, j) for g, planes in enumerate(GROUPS) for j, t in enumerate(planes)}
 
-        def gather_values(t, tag=None):
-            vv[t] = sbt("vv%d" % t, [P, I], F32, tag=tag)
-            nc.vector.tensor_tensor(vv[t][:], books[t][:].indirect(code_lists[:]), held["vsc_row"][:], MULT)
+        def gather_values(t, lo=0, hi=I, part=""):
+            vv = sbt("vv%d%s" % (t, part), [P, I], F32)
+            nc.vector.tensor_tensor(vv[:, lo:hi], books[t][:].indirect(code_lists[:, lo // 16 : hi // 16]), tiles["vsc_row"][:, lo:hi], MULT)
+
+        def round_values(t, lo=0, hi=I, part=""):
+            vv_bf = sbt("vv_bf%d" % t, [P, I], BF16)
+            nc.scalar.copy(
+                vv_bf[:].rearrange("p (u s e) -> p u s e", u=2, e=2)[:, :, lo // PACK : hi // PACK, :],
+                tiles["vv%d%s" % (t, part)][:, lo:hi].rearrange("p (s u e) -> p u s e", u=2, e=2),
+            )
 
         def turn_values(t):
-            nc.scalar.copy(
-                vv_bf[t][:].rearrange("p (u s e) -> p u s e", u=2, e=2),
-                vv[t][:].rearrange("p (s u e) -> p u s e", u=2, e=2),
-            )
-            words = vv_bf[t][:].bitcast(F32)
-            turned = bank("v_turned%d" % t, [P, 2, P], "cd"[t % 2])
+            words = tiles["vv_bf%d" % t][:].bitcast(F32)
+            turned = bank("v_turned%d" % t, [P, 2, P], "cdcd"[t])
             for u in range(2):
                 nc.tensor.transpose(turned[:, u, :], words[:, u * P : (u + 1) * P], ident[:])
+
+        def fetch_values(t):
             g, j = place[t]
-            nc.scalar.copy(vv_in[g][:, j * I : (j + 1) * I].bitcast(F32).rearrange("s (p u) -> s p u", u=2), turned[:].rearrange("s u p -> s p u"))
+            vv_in = sbt("vv_in%d" % g, [P, len(GROUPS[g]) * I], BF16)
+            nc.scalar.copy(
+                vv_in[:, j * I : (j + 1) * I].bitcast(F32).rearrange("s (p u) -> s p u", u=2),
+                tiles["v_turned%d" % t][:].rearrange("s u p -> s p u"),
+            )
 
         def quantise_values(g):
-            nc.vector.quantize_mx(out=vv_codes[g][:].bitcast(FP8X4), scales=vv_scales[g][:], in_=vv_in[g][:])
-
-        scores = [None] * HALVES
+            quantise("v%d" % g, tiles["vv_in%d" % g], len(GROUPS[g]) * P)
 
         def score(h):
-            scores[h] = bank("scores%d" % h, [P, I], "ab"[h])
             nc.tensor.matmul_mx(
-                out=scores[h][:],
-                lhsT=q_codes[h][:].bitcast(FP8X4),
-                lhsT_scale=q_scales[h][:],
-                rhs=kg_words[:].bitcast(FP4X4),
-                rhs_scale=kg_scales[:],
+                out=bank("scores%d" % h, [P, I], "ab"[h])[:],
+                lhsT=tiles["q%d_codes" % h][:].bitcast(FP8X4),
+                lhsT_scale=tiles["q%d_scales" % h][:],
+                rhs=tiles["kg_words"][:].bitcast(FP4X4),
+                rhs_scale=tiles["kg_scales"][:],
                 start=True,
                 stop=True,
             )
 
-        neg_max = [None] * HALVES
-        row_sum = sbt("row_sum", [P, HALVES], F32)
-        inv_sum = sbt("inv_sum", [P, HALVES], F32)
-        p_exp = [sbt("p_exp%d" % h, [P, I], F32) for h in range(HALVES)]
-        w_in = [None] * HALVES
-        w_codes = [None] * HALVES
-        w_scales = [sbt("w_scales%d" % h, [P, P], U8) for h in range(HALVES)]
-
-        def row_max(h, tag=None):
-            neg_max[h] = sbt("neg_max%d" % h, [P, 1], F32, tag=tag)
-            nc.vector.tensor_reduce(neg_max[h][:], scores[h][:], AX, MAX, negate=True)
+        def row_max(h):
+            nc.vector.tensor_reduce(sbt("neg_max%d" % h, [P, 1], F32)[:], tiles["scores%d" % h][:], AX, MAX, negate=True)
 
         def exponentiate(h):
-            nc.scalar.activation(p_exp[h][:].rearrange("q (r s) -> q r s", r=PACK), scores[h][:].rearrange("q (s r) -> q r s", r=PACK), EXP, bias=neg_max[h][:], accum_out=row_sum[:, h : h + 1])
-
-        p_turned = [None] * HALVES
+            nc.scalar.activation(
+                sbt("p_exp%d" % h, [P, I], F32)[:].rearrange("q (r s) -> q r s", r=PACK),
+                tiles["scores%d" % h][:].rearrange("q (s r) -> q r s", r=PACK),
+                EXP,
+                bias=tiles["neg_max%d" % h][:],
+                accum_out=sbt("row_sum", [P, HALVES], F32)[:, h : h + 1],
+            )
 
         def invert_sums():
-            nc.vector.reciprocal(inv_sum[:], row_sum[:])
+            nc.vector.reciprocal(sbt("inv_sum", [P, HALVES], F32)[:], tiles["row_sum"][:])
 
         def normalise(h):
             p_norm = sbt("p_norm%d" % h, [P, I], F32)
-            nc.scalar.activation(p_norm[:], p_exp[h][:], COPY, scale=inv_sum[:, h : h + 1])
-            p_turned[h] = bank("p_turned%d" % h, [P, PACK, P], "ef"[h])
+            nc.scalar.activation(p_norm[:], tiles["p_exp%d" % h][:], COPY, scale=tiles["inv_sum"][:, h : h + 1])
+            p_turned = bank("p_turned%d" % h, [P, PACK, P], "ef"[h])
             for r in range(PACK):
-                nc.tensor.transpose(p_turned[h][:, r, :], p_norm[:, r * P : (r + 1) * P], ident[:])
+                nc.tensor.transpose(p_turned[:, r, :], p_norm[:, r * P : (r + 1) * P], ident[:])
 
-        def weigh(h, tag=None):
-            w_in[h] = sbt("w_in%d" % h, [P, P * PACK], BF16, tag=tag)
+        def weigh(h):
             nc.vector.tensor_tensor(
-                w_in[h][:].rearrange("s (q r) -> s q r", r=PACK),
-                p_turned[h][:].rearrange("s r q -> s q r"),
+                sbt("w_in%d" % h, [P, P * PACK], BF16)[:].rearrange("s (q r) -> s q r", r=PACK),
+                tiles["p_turned%d" % h][:].rearrange("s r q -> s q r"),
                 size_cols[:].unsqueeze(1).to_broadcast([P, P, PACK]),
                 MULT,
             )
 
-        def quantise_weights(h, tag=None):
-            w_codes[h] = sbt("w_codes%d" % h, [P, P], U32, tag=tag)
-            nc.vector.quantize_mx(out=w_codes[h][:].bitcast(FP8X4), scales=w_scales[h][:], in_=w_in[h][:])
+        def quantise_weights(h):
+            quantise("w%d" % h, tiles["w_in%d" % h], P)
 
         def product(out, t, h):
             g, j = place[t]
             nc.tensor.matmul_mx(
                 out=out,
-                lhsT=vv_codes[g][:, j * P : (j + 1) * P].bitcast(FP8X4),
-                lhsT_scale=vv_scales[g][:, j * P : (j + 1) * P],
-                rhs=w_codes[h][:].bitcast(FP8X4),
-                rhs_scale=w_scales[h][:],
+                lhsT=tiles["v%d_codes" % g][:, j * P : (j + 1) * P].bitcast(FP8X4),
+                lhsT_scale=tiles["v%d_scales" % g][:, j * P : (j + 1) * P],
+                rhs=tiles["w%d_codes" % h][:].bitcast(FP8X4),
+                rhs_scale=tiles["w%d_scales" % h][:],
                 start=True,
                 stop=True,
             )
@@ -215,21 +225,33 @@ def tile_attend_pqvalues_pl_kernel(tc, query, keys_words, keys_scales, vbook, si
         score(0)
         score(1)
         gather_values(0)
-        row_max(0, tag="book0")
+        row_max(0)
+        round_values(0)
         turn_values(0)
         exponentiate(0)
         row_max(1)
         exponentiate(1)
-        gather_values(1, tag="q_codes1")
+        gather_values(1, 0, P, "a")
+        round_values(1, 0, P, "a")
+        fetch_values(0)
+        gather_values(1, P, I)
         invert_sums()
+        round_values(1, P, I)
         turn_values(1)
         normalise(0)
-        gather_values(2, tag="row_sum")
-        turn_values(2)
         normalise(1)
+        fetch_values(1)
+        gather_values(2)
+        round_values(2)
+        turn_values(2)
         quantise_values(0)
-        gather_values(3)
+        gather_values(3, 0, 384)
+        round_values(3, 0, 384)
+        gather_values(3, 384, I)
+        round_values(3, 384, I)
         turn_values(3)
+        fetch_values(2)
+        fetch_values(3)
         weigh(0)
         quantise_values(1)
         quantise_weights(0)
@@ -273,6 +295,6 @@ def tile_attend_pqvalues_pl_kernel(tc, query, keys_words, keys_scales, vbook, si
         quantise_result(0)
         quantise_result(1)
         nc.sync.dma_start(out_words, o_codes[:].bitcast(I32))
-        for row in range(4):
-            queue = nc.scalar if row == 3 else nc.sync
-            queue.dma_start(out_2[0, row:16:4, :].bitcast(I32), o_scales[row:P:32, :].bitcast(I32))
+        for quad in range(4):
+            queue = nc.scalar if quad == 3 else nc.sync
+            queue.dma_start(out_2[0, 4 * quad : 4 * quad + 4, :].bitcast(I32), o_scales[32 * quad : 32 * quad + 4, :].bitcast(I32))

@@ -23,16 +23,27 @@ AX = mybir.AxisListType.X
 P = 128
 PACK = 4
 HALVES = Q // P
-GROUPS = [(0, 1), (2,), (3,)]
+RESULT_BANKS = ["ab", "gh"]
+GROUPS = [(0,), (1, 2), (3,)]
 
 REUSE = {
-    "vsc_row": "q_raw0",
-    "neg_max0": "book0",
-    "vv1a": "q1_codes",
-    "vv1": "q1_scales",
-    "vv2": "vv1a",
+    "vv_bf0": "q_in1",
+    "neg_max0": "q_raw1",
+    "o_f32_0": "vv_bf3",
 }
-OVERLAY = {}
+OVERLAY = {
+    "book3": 0,
+    "vv_in1": 0,
+    "w_in0": 2048,
+    "w_in1": 3072,
+    "book1": 4096,
+    "p_exp0": 4096,
+    "p_exp1": 6144,
+    "book2": 8192,
+    "vv_in0": 8192,
+    "vv_bf1": 9216,
+    "inv_sum": 10240,
+}
 
 
 def tile_attend_pqvalues_pl_kernel(tc, query, keys_words, keys_scales, vbook, size, vsc, offs, offs2, out_0, out_1, out_2):
@@ -69,11 +80,27 @@ def tile_attend_pqvalues_pl_kernel(tc, query, keys_words, keys_scales, vbook, si
 
         warm_in = sbt("warm_in", [P, 1], F32)
         nc.vector.memset(key_scales[:].bitcast(I32), 0)
-        nc.gpsimd.memset(warm_in[:], 0.0)
-        make_identity(nc, ident[:])
+        nc.vector.memset(ident[:], 0.0)
+        nc.vector.memset(warm_in[:], 0.0)
+        make_identity(nc, ident[:], nomemset=True)
 
         book_rows = vbook.rearrange("(p t) c -> p t c", t=PACK)
         q_rows = query.rearrange("(p t) q -> p t q", t=PACK)
+
+        def load_key_list():
+            nc.sync.dma_start(key_list[:], offs)
+
+        def load_code_lists():
+            nc.sync.dma_start(code_lists[:], offs2)
+
+        def load_words():
+            nc.sync.dma_start(key_words[:].bitcast(I32), keys_words[0].bitcast(I32))
+
+        def load_vsc():
+            nc.sync.dma_start(vsc_cols[:], vsc.rearrange("(s r) o -> s (r o)", r=PACK))
+
+        def load_size():
+            nc.sync.dma_start(size_cols[:], size.rearrange("o (s r) -> s (o r)", r=PACK))
 
         def load_scale_rows():
             for quad in range(4):
@@ -85,18 +112,18 @@ def tile_attend_pqvalues_pl_kernel(tc, query, keys_words, keys_scales, vbook, si
         def load_book(t):
             nc.sync.dma_start(books[t][:], book_rows[:, t, :])
 
-        nc.sync.dma_start(key_list[:], offs)
-        nc.sync.dma_start(vsc_cols[:], vsc.rearrange("(s r) o -> s (r o)", r=PACK))
-        nc.sync.dma_start(key_words[:].bitcast(I32), keys_words[0].bitcast(I32))
-        nc.sync.dma_start(code_lists[:], offs2)
+        load_key_list()
+        load_vsc()
+        load_size()
+        load_words()
         load_queries(0)
         load_scale_rows()
-        load_queries(1)
+        load_code_lists()
         load_book(0)
+        load_queries(1)
         load_book(1)
         load_book(2)
         load_book(3)
-        nc.sync.dma_start(size_cols[:], size.rearrange("o (s r) -> s (o r)", r=PACK))
 
         warm = sbt("warm", [P, 1], F32)
         nc.scalar.activation(warm[:], warm_in[:], EXP)
@@ -106,9 +133,16 @@ def tile_attend_pqvalues_pl_kernel(tc, query, keys_words, keys_scales, vbook, si
             scales = sbt(name + "_scales", [P, width], U8)
             nc.vector.quantize_mx(out=codes[:].bitcast(FP8X4), scales=scales[:], in_=source[:])
 
-        def round_queries(h):
+        def copy_on(engine, out, source):
+            if engine == "S":
+                nc.scalar.copy(out, source)
+            else:
+                nc.vector.tensor_copy(out, source)
+
+        def round_queries(h, engine):
             q_in = sbt("q_in%d" % h, [P, P * PACK], BF16)
-            nc.scalar.copy(
+            copy_on(
+                engine,
                 q_in[:].rearrange("p (c j t) -> p c t j", j=4, t=PACK),
                 q_raw[h][:].rearrange("p t (c j) -> p c t j", j=4),
             )
@@ -116,12 +150,16 @@ def tile_attend_pqvalues_pl_kernel(tc, query, keys_words, keys_scales, vbook, si
         def quantise_queries(h):
             quantise("q%d" % h, tiles["q_in%d" % h], P)
 
-        def spread_vsc():
-            vsc_bank = bank("vsc_bank", [P, PACK, P], "a")
+        def spread(name, cols, tag):
+            row = bank(name, [P, PACK, P], tag)
             for r in range(PACK):
-                nc.tensor.transpose(vsc_bank[:, r, :], vsc_cols[:, r : r + 1].to_broadcast([P, P]), ident[:])
-            vsc_row = sbt("vsc_row", [P, I], F32)
-            nc.scalar.copy(vsc_row[:].rearrange("p (s r) -> p s r", r=PACK), vsc_bank[:].rearrange("p r s -> p s r"))
+                nc.tensor.transpose(row[:, r, :], cols[:, r : r + 1].to_broadcast([P, P]), ident[:])
+
+        def copy_row(name, source):
+            nc.scalar.copy(
+                sbt(name, [P, I], F32)[:].rearrange("p (s r) -> p s r", r=PACK),
+                tiles[source][:].rearrange("p r s -> p s r"),
+            )
 
         def gather_key_words():
             nc.vector.tensor_copy(sbt("kg_words", [P, I], U16)[:], key_words[:].indirect(key_list[:]))
@@ -131,29 +169,63 @@ def tile_attend_pqvalues_pl_kernel(tc, query, keys_words, keys_scales, vbook, si
 
         place = {t: (g, j) for g, planes in enumerate(GROUPS) for j, t in enumerate(planes)}
 
-        def gather_values(t, lo=0, hi=I, part=""):
-            vv = sbt("vv%d%s" % (t, part), [P, I], F32)
-            nc.vector.tensor_tensor(vv[:, lo:hi], books[t][:].indirect(code_lists[:, lo // 16 : hi // 16]), tiles["vsc_row"][:, lo:hi], MULT)
+        def gather_values(t, engine, lo=0, hi=I):
+            out = sbt("vg%d" % t, [P, I], F32)[:, lo:hi]
+            window = books[t][:].indirect(code_lists[:, lo // 16 : hi // 16])
+            if engine == "S":
+                nc.scalar.activation(out, window, COPY)
+            else:
+                nc.vector.tensor_copy(out, window)
 
-        def round_values(t, lo=0, hi=I, part=""):
-            vv_bf = sbt("vv_bf%d" % t, [P, I], BF16)
-            nc.scalar.copy(
-                vv_bf[:].rearrange("p (u s e) -> p u s e", u=2, e=2)[:, :, lo // PACK : hi // PACK, :],
-                tiles["vv%d%s" % (t, part)][:, lo:hi].rearrange("p (s u e) -> p u s e", u=2, e=2),
+        def gather_scaled(t):
+            nc.vector.tensor_tensor(sbt("vg%d" % t, [P, I], F32)[:], books[t][:].indirect(code_lists[:]), tiles["vsc_row"][:], MULT)
+
+        def round_turned(t):
+            nc.scalar.copy(value_slot(t).rearrange("s (p r) -> s p r", r=PACK), tiles["v_turned%d" % t][:].rearrange("s r p -> s p r"))
+
+        def scale_pairs(t, engine, lo=0, hi=I):
+            s = slice(lo // PACK, hi // PACK)
+            if engine == "G":
+                factor = tiles["vsc_row"][:, lo:hi].rearrange("p (s u e) -> p u s e", u=2, e=2)
+            else:
+                factor = tiles["vsc_bank"][:, :, s].rearrange("p (u e) s -> p u s e", u=2)
+            (nc.gpsimd if engine == "G" else nc.vector).tensor_tensor(
+                sbt("vv_bf%d" % t, [P, I], BF16)[:].rearrange("p (u s e) -> p u s e", u=2, e=2)[:, :, s, :],
+                tiles["vg%d" % t][:, lo:hi].rearrange("p (s u e) -> p u s e", u=2, e=2),
+                factor,
+                MULT,
             )
 
-        def turn_values(t):
-            words = tiles["vv_bf%d" % t][:].bitcast(F32)
-            turned = bank("v_turned%d" % t, [P, 2, P], "cdcd"[t])
+        def turn_pairs(name, source, tag):
+            words = tiles[source][:].bitcast(F32)
+            turned = bank(name, [P, 2, P], tag)
             for u in range(2):
                 nc.tensor.transpose(turned[:, u, :], words[:, u * P : (u + 1) * P], ident[:])
 
-        def fetch_values(t):
+        def fetch_pairs(out, name, engine):
+            copy_on(engine, out.bitcast(F32).rearrange("s (p u) -> s p u", u=2), tiles[name][:].rearrange("s u p -> s p u"))
+
+        def value_slot(t):
             g, j = place[t]
-            vv_in = sbt("vv_in%d" % g, [P, len(GROUPS[g]) * I], BF16)
-            nc.scalar.copy(
-                vv_in[:, j * I : (j + 1) * I].bitcast(F32).rearrange("s (p u) -> s p u", u=2),
-                tiles["v_turned%d" % t][:].rearrange("s u p -> s p u"),
+            return sbt("vv_in%d" % g, [P, len(GROUPS[g]) * I], BF16)[:, j * I : (j + 1) * I]
+
+        def turn_value_pairs(t, tag):
+            turn_pairs("v_turned%d" % t, "vv_bf%d" % t, tag)
+
+        def fetch_values(t, engine):
+            fetch_pairs(value_slot(t), "v_turned%d" % t, engine)
+
+        def turn_floats(t, tag):
+            turned = bank("v_turned%d" % t, [P, PACK, P], tag)
+            for r in range(PACK):
+                nc.tensor.transpose(turned[:, r, :], tiles["vg%d" % t][:, r:I:PACK], ident[:])
+
+        def scale_turned(t):
+            nc.vector.tensor_tensor(
+                value_slot(t).rearrange("s (p r) -> s p r", r=PACK),
+                tiles["v_turned%d" % t][:].rearrange("s r p -> s p r"),
+                vsc_cols[:].unsqueeze(1).to_broadcast([P, P, PACK]),
+                MULT,
             )
 
         def quantise_values(g):
@@ -175,8 +247,8 @@ def tile_attend_pqvalues_pl_kernel(tc, query, keys_words, keys_scales, vbook, si
 
         def exponentiate(h):
             nc.scalar.activation(
-                sbt("p_exp%d" % h, [P, I], F32)[:].rearrange("q (r s) -> q r s", r=PACK),
-                tiles["scores%d" % h][:].rearrange("q (s r) -> q r s", r=PACK),
+                sbt("p_exp%d" % h, [P, I], F32)[:].rearrange("q (u s e) -> q u s e", u=2, e=2),
+                tiles["scores%d" % h][:].rearrange("q (s u e) -> q u s e", u=2, e=2),
                 EXP,
                 bias=tiles["neg_max%d" % h][:],
                 accum_out=sbt("row_sum", [P, HALVES], F32)[:, h : h + 1],
@@ -185,28 +257,35 @@ def tile_attend_pqvalues_pl_kernel(tc, query, keys_words, keys_scales, vbook, si
         def invert_sums():
             nc.vector.reciprocal(sbt("inv_sum", [P, HALVES], F32)[:], tiles["row_sum"][:])
 
-        def normalise(h):
-            p_norm = sbt("p_norm%d" % h, [P, I], F32)
-            nc.scalar.activation(p_norm[:], tiles["p_exp%d" % h][:], COPY, scale=tiles["inv_sum"][:, h : h + 1])
-            p_turned = bank("p_turned%d" % h, [P, PACK, P], "ef"[h])
-            for r in range(PACK):
-                nc.tensor.transpose(p_turned[:, r, :], p_norm[:, r * P : (r + 1) * P], ident[:])
-
         def weigh(h):
-            nc.vector.tensor_tensor(
-                sbt("w_in%d" % h, [P, P * PACK], BF16)[:].rearrange("s (q r) -> s q r", r=PACK),
-                tiles["p_turned%d" % h][:].rearrange("s r q -> s q r"),
-                size_cols[:].unsqueeze(1).to_broadcast([P, P, PACK]),
-                MULT,
-            )
+            w_bf = sbt("w_bf%d" % h, [P, I], BF16)
+            for u in range(2):
+                run = slice(u * 2 * P, (u + 1) * 2 * P)
+                nc.vector.scalar_tensor_tensor(
+                    w_bf[:, run].rearrange("q (s e) -> q s e", e=2),
+                    tiles["p_exp%d" % h][:, run].rearrange("q (s e) -> q s e", e=2),
+                    tiles["inv_sum"][:, h : h + 1],
+                    tiles["size_bank"][:, 2 * u : 2 * u + 2, :].rearrange("q e s -> q s e"),
+                    MULT,
+                    MULT,
+                )
+
+        def turn_weights(h):
+            turn_pairs("w_turned%d" % h, "w_bf%d" % h, "gh"[h])
+
+        def fetch_weights(h, engine):
+            fetch_pairs(sbt("w_in%d" % h, [P, I], BF16)[:], "w_turned%d" % h, engine)
 
         def quantise_weights(h):
             quantise("w%d" % h, tiles["w_in%d" % h], P)
 
-        def product(out, t, h):
+        def product(t, h, late):
+            name = "acc%d%d" % (late, h)
+            if name not in tiles:
+                bank(name, [P, 3 - late, P], RESULT_BANKS[late][h])
             g, j = place[t]
             nc.tensor.matmul_mx(
-                out=out,
+                out=tiles[name][:, t - 2 * late, :],
                 lhsT=tiles["v%d_codes" % g][:, j * P : (j + 1) * P].bitcast(FP8X4),
                 lhsT_scale=tiles["v%d_scales" % g][:, j * P : (j + 1) * P],
                 rhs=tiles["w%d_codes" % h][:].bitcast(FP8X4),
@@ -215,86 +294,100 @@ def tile_attend_pqvalues_pl_kernel(tc, query, keys_words, keys_scales, vbook, si
                 stop=True,
             )
 
-        gather_key_words()
-        round_queries(0)
-        quantise_queries(0)
-        spread_vsc()
-        gather_key_scales()
-        round_queries(1)
-        quantise_queries(1)
-        score(0)
-        score(1)
-        gather_values(0)
-        row_max(0)
-        round_values(0)
-        turn_values(0)
-        exponentiate(0)
-        row_max(1)
-        exponentiate(1)
-        gather_values(1, 0, P, "a")
-        round_values(1, 0, P, "a")
-        fetch_values(0)
-        gather_values(1, P, I)
-        invert_sums()
-        round_values(1, P, I)
-        turn_values(1)
-        normalise(0)
-        normalise(1)
-        fetch_values(1)
-        gather_values(2)
-        round_values(2)
-        turn_values(2)
-        quantise_values(0)
-        gather_values(3, 0, 384)
-        round_values(3, 0, 384)
-        gather_values(3, 384, I)
-        round_values(3, 384, I)
-        turn_values(3)
-        fetch_values(2)
-        fetch_values(3)
-        weigh(0)
-        quantise_values(1)
-        quantise_weights(0)
-        weigh(1)
-        quantise_values(2)
-        quantise_weights(1)
-
-        o_codes = sbt("o_codes", [P, Q], U32)
-        o_scales = sbt("o_scales", [P, Q], U8)
         out_rows = out_0.rearrange("(p t) q -> p t q", t=PACK)
         out_words = out_1[0].rearrange("p c r -> p (c r)").bitcast(I32)
-        acc_early = bank("acc_early", [P, PACK - 1, P], "a")
-        acc_last = bank("acc_last", [P, P], "g")
-        acc_pairs = [bank("acc_pair%d" % u, [P, 2, P], "bh"[u]) for u in range(2)]
-        for t in range(PACK - 1):
-            product(acc_early[:, t, :], t, 0)
-        product(acc_last[:], PACK - 1, 0)
-        for t in range(PACK):
-            product(acc_pairs[t // 2][:, t % 2, :], t, 1)
-        o_f32 = [sbt("o_f32_%d" % h, [P, PACK, P], F32) for h in range(HALVES)]
-        o_in = [sbt("o_in%d" % h, [P, P * PACK], BF16) for h in range(HALVES)]
+
+        def copy_result(u, h, engine):
+            copy_on(engine, sbt("o_f32_%d" % u, [P, 3 - 2 * u, Q], F32)[:, :, h * P : (h + 1) * P], tiles["acc%d%d" % (u, h)][:, u:, :])
+
+        def store_result(u, queue):
+            queue.dma_start(out_rows[:, 3 * u : 3 + u, :], tiles["o_f32_%d" % u][:])
+
+        def round_result(u, h, engine):
+            copy_on(
+                engine,
+                sbt("o_in%d" % h, [P, P * PACK], BF16)[:].rearrange("p (q u e) -> p u q e", u=2, e=2)[:, u, :, :],
+                tiles["acc%d%d" % (u, h)][:, 0:2, :].rearrange("p e q -> p q e"),
+            )
 
         def quantise_result(h):
             cols = slice(h * P, (h + 1) * P)
-            nc.vector.quantize_mx(out=o_codes[:, cols].bitcast(FP8X4), scales=o_scales[:, cols], in_=o_in[h][:])
+            nc.vector.quantize_mx(
+                out=sbt("o_codes", [P, Q], U32)[:, cols].bitcast(FP8X4),
+                scales=sbt("o_scales", [P, Q], U8)[:, cols],
+                in_=tiles["o_in%d" % h][:],
+            )
 
-        nc.scalar.copy(o_f32[0][:, 0 : PACK - 1, :], acc_early[:])
-        nc.scalar.copy(o_f32[0][:, PACK - 1, :], acc_last[:])
-        nc.sync.dma_start(out_rows[:, :, 0:P], o_f32[0][:])
-        nc.vector.tensor_copy(
-            o_in[0][:].rearrange("p (c j t) -> p c t j", j=4, t=PACK),
-            o_f32[0][:].rearrange("p t (c j) -> p c t j", j=4),
-        )
-        pair_words = o_in[1][:].rearrange("p (q u e) -> p u q e", u=2, e=2)
-        nc.scalar.copy(o_f32[1][:, 0:2, :], acc_pairs[0][:])
-        nc.sync.dma_start(out_rows[:, 0:2, P : 2 * P], o_f32[1][:, 0:2, :])
-        nc.scalar.copy(pair_words[:, 0, :, :], acc_pairs[0][:].rearrange("p e q -> p q e"))
-        nc.vector.tensor_copy(pair_words[:, 1, :, :], acc_pairs[1][:].rearrange("p e q -> p q e"))
-        nc.scalar.copy(o_f32[1][:, 2:4, :], acc_pairs[1][:])
-        nc.scalar.dma_start(out_rows[:, 2:4, P : 2 * P], o_f32[1][:, 2:4, :])
+        def store_planes():
+            nc.sync.dma_start(out_words, tiles["o_codes"][:].bitcast(I32))
+            for quad in range(4):
+                queue = nc.scalar if quad == 3 else nc.sync
+                queue.dma_start(out_2[0, 4 * quad : 4 * quad + 4, :].bitcast(I32), tiles["o_scales"][32 * quad : 32 * quad + 4, :].bitcast(I32))
+
+        gather_key_words()
+        round_queries(0, "S")
+        quantise_queries(0)
+        spread("vsc_bank", vsc_cols, "c")
+        copy_row("vsc_row", "vsc_bank")
+        spread("size_bank", size_cols, "d")
+        gather_key_scales()
+        score(0)
+        gather_values(0, "S")
+        round_queries(1, "V")
+        quantise_queries(1)
+        scale_pairs(0, "G")
+        score(1)
+        row_max(0)
+        gather_values(1, "S")
+        exponentiate(0)
+        row_max(1)
+        exponentiate(1)
+        turn_value_pairs(0, "e")
+        gather_scaled(2)
+        invert_sums()
+        fetch_values(0, "V")
+        scale_pairs(1, "G")
+        turn_floats(2, "f")
+        weigh(0)
+        turn_value_pairs(1, "e")
+        turn_weights(0)
+        quantise_values(0)
+        weigh(1)
+        turn_weights(1)
+        gather_values(3, "S", 0, 256)
+        gather_values(3, "S", 256, I)
+        scale_pairs(3, "V", 0, 256)
+        scale_pairs(3, "V", 256, I)
+        fetch_weights(0, "S")
+        round_turned(2)
+        fetch_values(1, "S")
+        fetch_weights(1, "S")
+        turn_value_pairs(3, "f")
+        fetch_values(3, "S")
+        quantise_weights(0)
+        quantise_values(1)
+        product(0, 0, 0)
+        product(1, 0, 0)
+        product(2, 0, 0)
+        quantise_weights(1)
+        product(0, 1, 0)
+        product(1, 1, 0)
+        product(2, 1, 0)
+        quantise_values(2)
+        product(2, 0, 1)
+        product(2, 1, 1)
+        copy_result(0, 0, "S")
+        round_result(0, 0, "V")
+        copy_result(0, 1, "S")
+        round_result(0, 1, "S")
+        store_result(0, nc.sync)
+        product(3, 0, 1)
+        product(3, 1, 1)
+        round_result(1, 0, "V")
+        round_result(1, 1, "S")
+        copy_result(1, 0, "V")
+        copy_result(1, 1, "S")
         quantise_result(0)
         quantise_result(1)
-        nc.sync.dma_start(out_words, o_codes[:].bitcast(I32))
-        for quad in range(4):
-            queue = nc.scalar if quad == 3 else nc.sync
-            queue.dma_start(out_2[0, 4 * quad : 4 * quad + 4, :].bitcast(I32), o_scales[32 * quad : 32 * quad + 4, :].bitcast(I32))
+        store_result(1, nc.scalar)
+        store_planes()

@@ -23,7 +23,7 @@ AX = mybir.AxisListType.X
 P = 128
 PACK = 4
 HALVES = Q // P
-RESULT_BANKS = ["ab", "gh"]
+RESULT_BANKS = ["db", "gh"]
 GROUPS = [(0,), (1, 2), (3,)]
 
 REUSE = {
@@ -114,14 +114,14 @@ def tile_attend_pqvalues_pl_kernel(tc, query, keys_words, keys_scales, vbook, si
 
         load_key_list()
         load_vsc()
-        load_size()
         load_words()
+        load_code_lists()
         load_queries(0)
         load_scale_rows()
-        load_code_lists()
         load_book(0)
         load_queries(1)
         load_book(1)
+        load_size()
         load_book(2)
         load_book(3)
 
@@ -186,12 +186,12 @@ def tile_attend_pqvalues_pl_kernel(tc, query, keys_words, keys_scales, vbook, si
         def scale_pairs(t, engine, lo=0, hi=I):
             s = slice(lo // PACK, hi // PACK)
             if engine == "G":
-                factor = tiles["vsc_row"][:, lo:hi].rearrange("p (s u e) -> p u s e", u=2, e=2)
+                factor = tiles["vsc_row"][:, lo:hi].rearrange("p (s r) -> p s r", r=PACK)
             else:
-                factor = tiles["vsc_bank"][:, :, s].rearrange("p (u e) s -> p u s e", u=2)
+                factor = tiles["vsc_bank"][:, :, s].rearrange("p r s -> p s r")
             (nc.gpsimd if engine == "G" else nc.vector).tensor_tensor(
-                sbt("vv_bf%d" % t, [P, I], BF16)[:].rearrange("p (u s e) -> p u s e", u=2, e=2)[:, :, s, :],
-                tiles["vg%d" % t][:, lo:hi].rearrange("p (s u e) -> p u s e", u=2, e=2),
+                sbt("vv_bf%d" % t, [P, I], BF16)[:, lo:hi].rearrange("p (s r) -> p s r", r=PACK),
+                tiles["vg%d" % t][:, lo:hi].rearrange("p (s r) -> p s r", r=PACK),
                 factor,
                 MULT,
             )
@@ -200,7 +200,7 @@ def tile_attend_pqvalues_pl_kernel(tc, query, keys_words, keys_scales, vbook, si
             words = tiles[source][:].bitcast(F32)
             turned = bank(name, [P, 2, P], tag)
             for u in range(2):
-                nc.tensor.transpose(turned[:, u, :], words[:, u * P : (u + 1) * P], ident[:])
+                nc.tensor.transpose(turned[:, u, :], words[:, u : 2 * P : 2], ident[:])
 
         def fetch_pairs(out, name, engine):
             copy_on(engine, out.bitcast(F32).rearrange("s (p u) -> s p u", u=2), tiles[name][:].rearrange("s u p -> s p u"))
@@ -247,8 +247,8 @@ def tile_attend_pqvalues_pl_kernel(tc, query, keys_words, keys_scales, vbook, si
 
         def exponentiate(h):
             nc.scalar.activation(
-                sbt("p_exp%d" % h, [P, I], F32)[:].rearrange("q (u s e) -> q u s e", u=2, e=2),
-                tiles["scores%d" % h][:].rearrange("q (s u e) -> q u s e", u=2, e=2),
+                sbt("p_exp%d" % h, [P, I], F32)[:],
+                tiles["scores%d" % h][:],
                 EXP,
                 bias=tiles["neg_max%d" % h][:],
                 accum_out=sbt("row_sum", [P, HALVES], F32)[:, h : h + 1],
@@ -258,17 +258,14 @@ def tile_attend_pqvalues_pl_kernel(tc, query, keys_words, keys_scales, vbook, si
             nc.vector.reciprocal(sbt("inv_sum", [P, HALVES], F32)[:], tiles["row_sum"][:])
 
         def weigh(h):
-            w_bf = sbt("w_bf%d" % h, [P, I], BF16)
-            for u in range(2):
-                run = slice(u * 2 * P, (u + 1) * 2 * P)
-                nc.vector.scalar_tensor_tensor(
-                    w_bf[:, run].rearrange("q (s e) -> q s e", e=2),
-                    tiles["p_exp%d" % h][:, run].rearrange("q (s e) -> q s e", e=2),
-                    tiles["inv_sum"][:, h : h + 1],
-                    tiles["size_bank"][:, 2 * u : 2 * u + 2, :].rearrange("q e s -> q s e"),
-                    MULT,
-                    MULT,
-                )
+            nc.vector.scalar_tensor_tensor(
+                sbt("w_bf%d" % h, [P, I], BF16)[:].rearrange("q (s r) -> q s r", r=PACK),
+                tiles["p_exp%d" % h][:].rearrange("q (s r) -> q s r", r=PACK),
+                tiles["inv_sum"][:, h : h + 1],
+                tiles["size_bank"][:].rearrange("q r s -> q s r"),
+                MULT,
+                MULT,
+            )
 
         def turn_weights(h):
             turn_pairs("w_turned%d" % h, "w_bf%d" % h, "gh"[h])
@@ -329,7 +326,6 @@ def tile_attend_pqvalues_pl_kernel(tc, query, keys_words, keys_scales, vbook, si
         quantise_queries(0)
         spread("vsc_bank", vsc_cols, "c")
         copy_row("vsc_row", "vsc_bank")
-        spread("size_bank", size_cols, "d")
         gather_key_scales()
         score(0)
         gather_values(0, "S")
@@ -343,6 +339,7 @@ def tile_attend_pqvalues_pl_kernel(tc, query, keys_words, keys_scales, vbook, si
         row_max(1)
         exponentiate(1)
         turn_value_pairs(0, "e")
+        spread("size_bank", size_cols, "a")
         gather_scaled(2)
         invert_sums()
         fetch_values(0, "V")
@@ -351,8 +348,8 @@ def tile_attend_pqvalues_pl_kernel(tc, query, keys_words, keys_scales, vbook, si
         weigh(0)
         turn_value_pairs(1, "e")
         turn_weights(0)
-        quantise_values(0)
         weigh(1)
+        quantise_values(0)
         turn_weights(1)
         gather_values(3, "S", 0, 256)
         gather_values(3, "S", 256, I)

@@ -27,7 +27,6 @@ RESULT_BANKS = ["db", "gh"]
 GROUPS = [(0,), (1, 2), (3,)]
 
 REUSE = {
-    "vv_bf0": "q_in1",
     "neg_max0": "q_raw1",
     "o_f32_0": "vv_bf3",
 }
@@ -331,7 +330,7 @@ def tile_attend_pqvalues_pl_kernel(tc, query, keys_words, keys_scales, vbook, si
         gather_values(0, "S")
         round_queries(1, "V")
         quantise_queries(1)
-        scale_pairs(0, "G")
+        scale_pairs(0, "V")
         score(1)
         row_max(0)
         gather_values(1, "S")
@@ -343,7 +342,7 @@ def tile_attend_pqvalues_pl_kernel(tc, query, keys_words, keys_scales, vbook, si
         gather_scaled(2)
         invert_sums()
         fetch_values(0, "V")
-        scale_pairs(1, "G")
+        scale_pairs(1, "V")
         turn_floats(2, "f")
         weigh(0)
         turn_value_pairs(1, "e")

@@ -24,24 +24,25 @@ P = 128
 PACK = 4
 HALVES = Q // P
 RESULT_BANKS = ["db", "gh"]
-GROUPS = [(0,), (1, 2), (3,)]
+GROUPS = [(0,), (1,), (2,), (3,)]
 
 REUSE = {
-    "neg_max0": "q_raw1",
     "o_f32_0": "vv_bf3",
+    "q0_codes": "vsc_cols",
 }
 OVERLAY = {
-    "book3": 0,
-    "vv_in1": 0,
-    "w_in0": 2048,
-    "w_in1": 3072,
-    "book1": 4096,
-    "p_exp0": 4096,
-    "p_exp1": 6144,
-    "book2": 8192,
-    "vv_in0": 8192,
-    "vv_bf1": 9216,
-    "inv_sum": 10240,
+    "v0_codes": 576,
+    "book3": 1024,
+    "w_in0": 1088,
+    "vv_in1": 2112,
+    "w_in1": 3136,
+    "vv_in2": 4160,
+    "book0": 5184,
+    "neg_max0": 5184,
+    "neg_max1": 5248,
+    "book1": 9280,
+    "vv_in0": 9280,
+    "inv_sum": 10304,
 }
 
 
@@ -113,12 +114,12 @@ def tile_attend_pqvalues_pl_kernel(tc, query, keys_words, keys_scales, vbook, si
 
         load_key_list()
         load_vsc()
-        load_words()
         load_code_lists()
+        load_words()
         load_queries(0)
         load_scale_rows()
-        load_book(0)
         load_queries(1)
+        load_book(0)
         load_book(1)
         load_size()
         load_book(2)
@@ -163,8 +164,8 @@ def tile_attend_pqvalues_pl_kernel(tc, query, keys_words, keys_scales, vbook, si
         def gather_key_words():
             nc.vector.tensor_copy(sbt("kg_words", [P, I], U16)[:], key_words[:].indirect(key_list[:]))
 
-        def gather_key_scales():
-            nc.vector.tensor_copy(sbt("kg_scales", [P, I], U8)[:], key_scales[:].indirect(key_list[:]))
+        def gather_key_scales(lo, hi):
+            nc.vector.tensor_copy(sbt("kg_scales", [P, I], U8)[:, lo:hi], key_scales[:].indirect(key_list[:, lo // 16 : hi // 16]))
 
         place = {t: (g, j) for g, planes in enumerate(GROUPS) for j, t in enumerate(planes)}
 
@@ -176,15 +177,24 @@ def tile_attend_pqvalues_pl_kernel(tc, query, keys_words, keys_scales, vbook, si
             else:
                 nc.vector.tensor_copy(out, window)
 
-        def gather_scaled(t):
-            nc.vector.tensor_tensor(sbt("vg%d" % t, [P, I], F32)[:], books[t][:].indirect(code_lists[:]), tiles["vsc_row"][:], MULT)
+        def gather_scaled(t, lo=0, hi=I, part=""):
+            out = sbt("vg%d%s" % (t, part), [P, I], F32)[:, lo:hi]
+            nc.vector.tensor_tensor(out, books[t][:].indirect(code_lists[:, lo // 16 : hi // 16]), tiles["vsc_row"][:, lo:hi], MULT)
+
+        def round_values(t, engine, lo=0, hi=I, part=""):
+            out = sbt("vv_bf%d" % t, [P, I], BF16)[:, lo:hi]
+            source = tiles["vg%d%s" % (t, part)][:, lo:hi]
+            if engine == "G":
+                nc.gpsimd.tensor_copy(out, source)
+            else:
+                nc.scalar.copy(out, source)
 
         def round_turned(t):
             nc.scalar.copy(value_slot(t).rearrange("s (p r) -> s p r", r=PACK), tiles["v_turned%d" % t][:].rearrange("s r p -> s p r"))
 
         def scale_pairs(t, engine, lo=0, hi=I):
             s = slice(lo // PACK, hi // PACK)
-            if engine == "G":
+            if engine != "V":
                 factor = tiles["vsc_row"][:, lo:hi].rearrange("p (s r) -> p s r", r=PACK)
             else:
                 factor = tiles["vsc_bank"][:, :, s].rearrange("p r s -> p s r")
@@ -230,13 +240,15 @@ def tile_attend_pqvalues_pl_kernel(tc, query, keys_words, keys_scales, vbook, si
         def quantise_values(g):
             quantise("v%d" % g, tiles["vv_in%d" % g], len(GROUPS[g]) * P)
 
-        def score(h):
+        def score(h, lo, hi):
+            if "scores%d" % h not in tiles:
+                bank("scores%d" % h, [P, I], "ab"[h])
             nc.tensor.matmul_mx(
-                out=bank("scores%d" % h, [P, I], "ab"[h])[:],
+                out=tiles["scores%d" % h][:, lo:hi],
                 lhsT=tiles["q%d_codes" % h][:].bitcast(FP8X4),
                 lhsT_scale=tiles["q%d_scales" % h][:],
-                rhs=tiles["kg_words"][:].bitcast(FP4X4),
-                rhs_scale=tiles["kg_scales"][:],
+                rhs=tiles["kg_words"][:, lo:hi].bitcast(FP4X4),
+                rhs_scale=tiles["kg_scales"][:, lo:hi],
                 start=True,
                 stop=True,
             )
@@ -275,13 +287,13 @@ def tile_attend_pqvalues_pl_kernel(tc, query, keys_words, keys_scales, vbook, si
         def quantise_weights(h):
             quantise("w%d" % h, tiles["w_in%d" % h], P)
 
-        def product(t, h, late):
-            name = "acc%d%d" % (late, h)
+        def product(t, h):
+            name = "acc%d%d" % (t // 2, h)
             if name not in tiles:
-                bank(name, [P, 3 - late, P], RESULT_BANKS[late][h])
+                bank(name, [P, 2, P], RESULT_BANKS[t // 2][h])
             g, j = place[t]
             nc.tensor.matmul_mx(
-                out=tiles[name][:, t - 2 * late, :],
+                out=tiles[name][:, t % 2, :],
                 lhsT=tiles["v%d_codes" % g][:, j * P : (j + 1) * P].bitcast(FP8X4),
                 lhsT_scale=tiles["v%d_scales" % g][:, j * P : (j + 1) * P],
                 rhs=tiles["w%d_codes" % h][:].bitcast(FP8X4),
@@ -294,16 +306,22 @@ def tile_attend_pqvalues_pl_kernel(tc, query, keys_words, keys_scales, vbook, si
         out_words = out_1[0].rearrange("p c r -> p (c r)").bitcast(I32)
 
         def copy_result(u, h, engine):
-            copy_on(engine, sbt("o_f32_%d" % u, [P, 3 - 2 * u, Q], F32)[:, :, h * P : (h + 1) * P], tiles["acc%d%d" % (u, h)][:, u:, :])
+            copy_on(engine, sbt("o_f32_%d" % u, [P, 2, Q], F32)[:, :, h * P : (h + 1) * P], tiles["acc%d%d" % (u, h)][:])
 
         def store_result(u, queue):
-            queue.dma_start(out_rows[:, 3 * u : 3 + u, :], tiles["o_f32_%d" % u][:])
+            queue.dma_start(out_rows[:, 2 * u : 2 * u + 2, :], tiles["o_f32_%d" % u][:])
 
         def round_result(u, h, engine):
             copy_on(
                 engine,
                 sbt("o_in%d" % h, [P, P * PACK], BF16)[:].rearrange("p (q u e) -> p u q e", u=2, e=2)[:, u, :, :],
-                tiles["acc%d%d" % (u, h)][:, 0:2, :].rearrange("p e q -> p q e"),
+                tiles["acc%d%d" % (u, h)][:].rearrange("p e q -> p q e"),
+            )
+
+        def round_early(h):
+            nc.vector.tensor_copy(
+                sbt("o_in%d" % h, [P, P * PACK], BF16)[:].rearrange("p (q u e) -> p u q e", u=2, e=2)[:, 0, :, :],
+                tiles["o_f32_0"][:, 0:2, h * P : (h + 1) * P].rearrange("p e q -> p q e"),
             )
 
         def quantise_result(h):
@@ -321,64 +339,68 @@ def tile_attend_pqvalues_pl_kernel(tc, query, keys_words, keys_scales, vbook, si
                 queue.dma_start(out_2[0, 4 * quad : 4 * quad + 4, :].bitcast(I32), tiles["o_scales"][32 * quad : 32 * quad + 4, :].bitcast(I32))
 
         gather_key_words()
+        spread("vsc_bank", vsc_cols, "c")
         round_queries(0, "S")
         quantise_queries(0)
-        spread("vsc_bank", vsc_cols, "c")
         copy_row("vsc_row", "vsc_bank")
-        gather_key_scales()
-        score(0)
-        gather_values(0, "S")
-        round_queries(1, "V")
+        gather_key_scales(0, 256)
+        score(0, 0, 256)
+        round_queries(1, "S")
         quantise_queries(1)
-        scale_pairs(0, "V")
-        score(1)
+        gather_key_scales(256, I)
+        score(1, 0, 256)
+        score(0, 256, I)
+        score(1, 256, I)
+        gather_values(0, "S", 0, 256)
+        gather_values(0, "V", 256, I)
         row_max(0)
-        gather_values(1, "S")
         exponentiate(0)
         row_max(1)
         exponentiate(1)
+        scale_pairs(0, "G")
         turn_value_pairs(0, "e")
         spread("size_bank", size_cols, "a")
-        gather_scaled(2)
+        gather_scaled(1)
         invert_sums()
         fetch_values(0, "V")
-        scale_pairs(1, "V")
-        turn_floats(2, "f")
+        round_values(1, "G")
+        turn_value_pairs(1, "f")
+        gather_values(2, "S")
         weigh(0)
-        turn_value_pairs(1, "e")
         turn_weights(0)
+        scale_pairs(2, "G")
         weigh(1)
-        quantise_values(0)
         turn_weights(1)
+        turn_value_pairs(2, "e")
         gather_values(3, "S", 0, 256)
         gather_values(3, "S", 256, I)
         scale_pairs(3, "V", 0, 256)
         scale_pairs(3, "V", 256, I)
         fetch_weights(0, "S")
-        round_turned(2)
         fetch_values(1, "S")
         fetch_weights(1, "S")
-        turn_value_pairs(3, "f")
+        fetch_values(2, "S")
+        turn_value_pairs(3, "a")
         fetch_values(3, "S")
+        quantise_values(0)
         quantise_weights(0)
+        product(0, 0)
         quantise_values(1)
-        product(0, 0, 0)
-        product(1, 0, 0)
-        product(2, 0, 0)
+        product(1, 0)
         quantise_weights(1)
-        product(0, 1, 0)
-        product(1, 1, 0)
-        product(2, 1, 0)
+        product(0, 1)
+        product(1, 1)
         quantise_values(2)
-        product(2, 0, 1)
-        product(2, 1, 1)
+        product(2, 0)
+        product(2, 1)
+        quantise_values(3)
+        product(3, 0)
+        product(3, 1)
         copy_result(0, 0, "S")
-        round_result(0, 0, "V")
         copy_result(0, 1, "S")
-        round_result(0, 1, "S")
+        round_early(0)
+        round_early(1)
         store_result(0, nc.sync)
-        product(3, 0, 1)
-        product(3, 1, 1)
         round_result(1, 0, "V")
         round_result(1, 1, "S")
         copy_result(1, 0, "V")

@@ -23,12 +23,14 @@ AX = mybir.AxisListType.X
 P = 128
 PACK = 4
 HALVES = Q // P
-RESULT_BANKS = ["db", "gh"]
+RESULT_BANKS = ["ab", "gh"]
 GROUPS = [(0,), (1,), (2,), (3,)]
 
 REUSE = {
     "o_f32_0": "vv_bf3",
     "q0_codes": "vsc_cols",
+    "p_exp": "size_cols",
+    "vv_bf2": "vg1",
 }
 OVERLAY = {
     "v0_codes": 576,
@@ -38,8 +40,9 @@ OVERLAY = {
     "w_in1": 3136,
     "vv_in2": 4160,
     "book0": 5184,
-    "neg_max0": 5184,
-    "neg_max1": 5248,
+    "neg_max1": 5184,
+    "neg_max0": 5248,
+    "vg2": 5248,
     "book1": 9280,
     "vv_in0": 9280,
     "inv_sum": 10304,
@@ -120,9 +123,9 @@ def tile_attend_pqvalues_pl_kernel(tc, query, keys_words, keys_scales, vbook, si
         load_scale_rows()
         load_queries(1)
         load_book(0)
-        load_book(1)
-        load_size()
         load_book(2)
+        load_size()
+        load_book(1)
         load_book(3)
 
         warm = sbt("warm", [P, 1], F32)
@@ -169,8 +172,8 @@ def tile_attend_pqvalues_pl_kernel(tc, query, keys_words, keys_scales, vbook, si
 
         place = {t: (g, j) for g, planes in enumerate(GROUPS) for j, t in enumerate(planes)}
 
-        def gather_values(t, engine, lo=0, hi=I):
-            out = sbt("vg%d" % t, [P, I], F32)[:, lo:hi]
+        def gather_values(t, engine, lo=0, hi=I, part=""):
+            out = sbt("vg%d%s" % (t, part), [P, I], F32)[:, lo:hi]
             window = books[t][:].indirect(code_lists[:, lo // 16 : hi // 16])
             if engine == "S":
                 nc.scalar.activation(out, window, COPY)
@@ -192,7 +195,7 @@ def tile_attend_pqvalues_pl_kernel(tc, query, keys_words, keys_scales, vbook, si
         def round_turned(t):
             nc.scalar.copy(value_slot(t).rearrange("s (p r) -> s p r", r=PACK), tiles["v_turned%d" % t][:].rearrange("s r p -> s p r"))
 
-        def scale_pairs(t, engine, lo=0, hi=I):
+        def scale_pairs(t, engine, lo=0, hi=I, part=""):
             s = slice(lo // PACK, hi // PACK)
             if engine != "V":
                 factor = tiles["vsc_row"][:, lo:hi].rearrange("p (s r) -> p s r", r=PACK)
@@ -200,7 +203,7 @@ def tile_attend_pqvalues_pl_kernel(tc, query, keys_words, keys_scales, vbook, si
                 factor = tiles["vsc_bank"][:, :, s].rearrange("p r s -> p s r")
             (nc.gpsimd if engine == "G" else nc.vector).tensor_tensor(
                 sbt("vv_bf%d" % t, [P, I], BF16)[:, lo:hi].rearrange("p (s r) -> p s r", r=PACK),
-                tiles["vg%d" % t][:, lo:hi].rearrange("p (s r) -> p s r", r=PACK),
+                tiles["vg%d%s" % (t, part)][:, lo:hi].rearrange("p (s r) -> p s r", r=PACK),
                 factor,
                 MULT,
             )
@@ -258,7 +261,7 @@ def tile_attend_pqvalues_pl_kernel(tc, query, keys_words, keys_scales, vbook, si
 
         def exponentiate(h):
             nc.scalar.activation(
-                sbt("p_exp%d" % h, [P, I], F32)[:],
+                sbt("p_exp", [P, HALVES, I], F32)[:, h, :],
                 tiles["scores%d" % h][:],
                 EXP,
                 bias=tiles["neg_max%d" % h][:],
@@ -271,7 +274,7 @@ def tile_attend_pqvalues_pl_kernel(tc, query, keys_words, keys_scales, vbook, si
         def weigh(h):
             nc.vector.scalar_tensor_tensor(
                 sbt("w_bf%d" % h, [P, I], BF16)[:].rearrange("q (s r) -> q s r", r=PACK),
-                tiles["p_exp%d" % h][:].rearrange("q (s r) -> q s r", r=PACK),
+                tiles["p_exp"][:, h, :].rearrange("q (s r) -> q s r", r=PACK),
                 tiles["inv_sum"][:, h : h + 1],
                 tiles["size_bank"][:].rearrange("q r s -> q s r"),
                 MULT,
@@ -353,25 +356,27 @@ def tile_attend_pqvalues_pl_kernel(tc, query, keys_words, keys_scales, vbook, si
         score(1, 256, I)
         gather_values(0, "S", 0, 256)
         gather_values(0, "V", 256, I)
+        gather_values(2, "S", 0, 256, "a")
+        spread("size_bank", size_cols, "d")
         row_max(0)
         exponentiate(0)
         row_max(1)
         exponentiate(1)
         scale_pairs(0, "G")
-        turn_value_pairs(0, "e")
-        spread("size_bank", size_cols, "a")
+        turn_value_pairs(0, "a")
+        gather_values(2, "S", 256, I)
         gather_scaled(1)
         invert_sums()
         fetch_values(0, "V")
         round_values(1, "G")
         turn_value_pairs(1, "f")
-        gather_values(2, "S")
         weigh(0)
         turn_weights(0)
-        scale_pairs(2, "G")
+        scale_pairs(2, "G", 0, 256, "a")
+        scale_pairs(2, "G", 256, I)
         weigh(1)
         turn_weights(1)
-        turn_value_pairs(2, "e")
+        turn_value_pairs(2, "d")
         gather_values(3, "S", 0, 256)
         gather_values(3, "S", 256, I)
         scale_pairs(3, "V", 0, 256)
@@ -380,7 +385,7 @@ def tile_attend_pqvalues_pl_kernel(tc, query, keys_words, keys_scales, vbook, si
         fetch_values(1, "S")
         fetch_weights(1, "S")
         fetch_values(2, "S")
-        turn_value_pairs(3, "a")
+        turn_value_pairs(3, "e")
         fetch_values(3, "S")
         quantise_values(0)
         quantise_weights(0)

@@ -41,7 +41,6 @@ OVERLAY = {
     "vv_in2": 4160,
     "book0": 5184,
     "neg_max1": 5184,
-    "neg_max0": 5248,
     "vg2": 5248,
     "book1": 9280,
     "vv_in0": 9280,
@@ -208,11 +207,11 @@ def tile_attend_pqvalues_pl_kernel(tc, query, keys_words, keys_scales, vbook, si
                 MULT,
             )
 
-        def turn_pairs(name, source, tag):
+        def turn_pairs(name, source, tag, dealt=False):
             words = tiles[source][:].bitcast(F32)
             turned = bank(name, [P, 2, P], tag)
             for u in range(2):
-                nc.tensor.transpose(turned[:, u, :], words[:, u : 2 * P : 2], ident[:])
+                nc.tensor.transpose(turned[:, u, :], words[:, u * P : (u + 1) * P] if dealt else words[:, u : 2 * P : 2], ident[:])
 
         def fetch_pairs(out, name, engine):
             copy_on(engine, out.bitcast(F32).rearrange("s (p u) -> s p u", u=2), tiles[name][:].rearrange("s u p -> s p u"))
@@ -221,8 +220,17 @@ def tile_attend_pqvalues_pl_kernel(tc, query, keys_words, keys_scales, vbook, si
             g, j = place[t]
             return sbt("vv_in%d" % g, [P, len(GROUPS[g]) * I], BF16)[:, j * I : (j + 1) * I]
 
-        def turn_value_pairs(t, tag):
-            turn_pairs("v_turned%d" % t, "vv_bf%d" % t, tag)
+        def turn_value_pairs(t, tag, dealt=False):
+            turn_pairs("v_turned%d" % t, "vv_bf%d" % t, tag, dealt)
+
+        def scale_dealt(t, lo, hi):
+            s = slice(lo // PACK, hi // PACK)
+            nc.vector.tensor_tensor(
+                sbt("vv_bf%d" % t, [P, I], BF16)[:].rearrange("p (u s e) -> p u s e", u=2, e=2)[:, :, s, :],
+                tiles["vg%d" % t][:, lo:hi].rearrange("p (s u e) -> p u s e", u=2, e=2),
+                tiles["vsc_bank"][:, :, s].rearrange("p (u e) s -> p u s e", u=2),
+                MULT,
+            )
 
         def fetch_values(t, engine):
             fetch_pairs(value_slot(t), "v_turned%d" % t, engine)
@@ -256,15 +264,18 @@ def tile_attend_pqvalues_pl_kernel(tc, query, keys_words, keys_scales, vbook, si
                 stop=True,
             )
 
+        def neg_max(h):
+            return sbt("vg2", [P, I], F32)[:, I - 1 : I] if h == 0 else sbt("neg_max1", [P, 1], F32)[:]
+
         def row_max(h):
-            nc.vector.tensor_reduce(sbt("neg_max%d" % h, [P, 1], F32)[:], tiles["scores%d" % h][:], AX, MAX, negate=True)
+            nc.vector.tensor_reduce(neg_max(h), tiles["scores%d" % h][:], AX, MAX, negate=True)
 
         def exponentiate(h):
             nc.scalar.activation(
-                sbt("p_exp", [P, HALVES, I], F32)[:, h, :],
-                tiles["scores%d" % h][:],
+                sbt("p_exp", [P, HALVES, I], F32)[:, h, :].rearrange("q (u s e) -> q u s e", u=2, e=2),
+                tiles["scores%d" % h][:].rearrange("q (s u e) -> q u s e", u=2, e=2),
                 EXP,
-                bias=tiles["neg_max%d" % h][:],
+                bias=neg_max(h),
                 accum_out=sbt("row_sum", [P, HALVES], F32)[:, h : h + 1],
             )
 
@@ -272,17 +283,19 @@ def tile_attend_pqvalues_pl_kernel(tc, query, keys_words, keys_scales, vbook, si
             nc.vector.reciprocal(sbt("inv_sum", [P, HALVES], F32)[:], tiles["row_sum"][:])
 
         def weigh(h):
-            nc.vector.scalar_tensor_tensor(
-                sbt("w_bf%d" % h, [P, I], BF16)[:].rearrange("q (s r) -> q s r", r=PACK),
-                tiles["p_exp"][:, h, :].rearrange("q (s r) -> q s r", r=PACK),
-                tiles["inv_sum"][:, h : h + 1],
-                tiles["size_bank"][:].rearrange("q r s -> q s r"),
-                MULT,
-                MULT,
-            )
+            for u in range(2):
+                run = slice(u * 2 * P, (u + 1) * 2 * P)
+                nc.vector.scalar_tensor_tensor(
+                    sbt("w_bf%d" % h, [P, I], BF16)[:, run].rearrange("q (s e) -> q s e", e=2),
+                    tiles["p_exp"][:, h, run].rearrange("q (s e) -> q s e", e=2),
+                    tiles["inv_sum"][:, h : h + 1],
+                    tiles["size_bank"][:, 2 * u : 2 * u + 2, :].rearrange("q e s -> q s e"),
+                    MULT,
+                    MULT,
+                )
 
         def turn_weights(h):
-            turn_pairs("w_turned%d" % h, "w_bf%d" % h, "gh"[h])
+            turn_pairs("w_turned%d" % h, "w_bf%d" % h, "gh"[h], True)
 
         def fetch_weights(h, engine):
             fetch_pairs(sbt("w_in%d" % h, [P, I], BF16)[:], "w_turned%d" % h, engine)
@@ -335,10 +348,13 @@ def tile_attend_pqvalues_pl_kernel(tc, query, keys_words, keys_scales, vbook, si
                 in_=tiles["o_in%d" % h][:],
             )
 
+        def store_words(h):
+            cols = slice(h * P, (h + 1) * P)
+            nc.sync.dma_start(out_words[:, cols], tiles["o_codes"][:, cols].bitcast(I32))
+
         def store_planes():
-            nc.sync.dma_start(out_words, tiles["o_codes"][:].bitcast(I32))
             for quad in range(4):
-                queue = nc.scalar if quad == 3 else nc.sync
+                queue = nc.scalar if quad >= 2 else nc.sync
                 queue.dma_start(out_2[0, 4 * quad : 4 * quad + 4, :].bitcast(I32), tiles["o_scales"][32 * quad : 32 * quad + 4, :].bitcast(I32))
 
         gather_key_words()
@@ -346,17 +362,14 @@ def tile_attend_pqvalues_pl_kernel(tc, query, keys_words, keys_scales, vbook, si
         round_queries(0, "S")
         quantise_queries(0)
         copy_row("vsc_row", "vsc_bank")
-        gather_key_scales(0, 256)
-        score(0, 0, 256)
+        gather_key_scales(0, I)
+        score(0, 0, I)
         round_queries(1, "S")
         quantise_queries(1)
-        gather_key_scales(256, I)
-        score(1, 0, 256)
-        score(0, 256, I)
-        score(1, 256, I)
+        score(1, 0, I)
         gather_values(0, "S", 0, 256)
         gather_values(0, "V", 256, I)
-        gather_values(2, "S", 0, 256, "a")
+        gather_values(2, "S", 0, 256)
         spread("size_bank", size_cols, "d")
         row_max(0)
         exponentiate(0)
@@ -372,20 +385,17 @@ def tile_attend_pqvalues_pl_kernel(tc, query, keys_words, keys_scales, vbook, si
         turn_value_pairs(1, "f")
         weigh(0)
         turn_weights(0)
-        scale_pairs(2, "G", 0, 256, "a")
-        scale_pairs(2, "G", 256, I)
+        scale_pairs(2, "G")
         weigh(1)
         turn_weights(1)
         turn_value_pairs(2, "d")
-        gather_values(3, "S", 0, 256)
-        gather_values(3, "S", 256, I)
-        scale_pairs(3, "V", 0, 256)
-        scale_pairs(3, "V", 256, I)
+        gather_values(3, "S")
+        scale_dealt(3, 0, I)
         fetch_weights(0, "S")
         fetch_values(1, "S")
         fetch_weights(1, "S")
         fetch_values(2, "S")
-        turn_value_pairs(3, "e")
+        turn_value_pairs(3, "e", True)
         fetch_values(3, "S")
         quantise_values(0)
         quantise_weights(0)
@@ -413,4 +423,6 @@ def tile_attend_pqvalues_pl_kernel(tc, query, keys_words, keys_scales, vbook, si
         quantise_result(0)
         quantise_result(1)
         store_result(1, nc.scalar)
+        store_words(0)
+        store_words(1)
         store_planes()

@@ -23,28 +23,30 @@ AX = mybir.AxisListType.X
 P = 128
 PACK = 4
 HALVES = Q // P
-RESULT_BANKS = ["ab", "gh"]
-GROUPS = [(0,), (1,), (2,), (3,)]
+MID = I // 2
 
 REUSE = {
-    "o_f32_0": "vv_bf3",
     "q0_codes": "vsc_cols",
     "p_exp": "size_cols",
-    "vv_bf2": "vg1",
+    "vv_bf2": "book1",
+    "o_f32_0": "vv_bf3",
 }
+
+ALIGN = 64
+ROW = I * 2
+BOOK = C * 4
+BOOK3 = ROW
+BOOK0 = BOOK3 + ALIGN + BOOK
 OVERLAY = {
-    "v0_codes": 576,
-    "book3": 1024,
-    "w_in0": 1088,
-    "vv_in1": 2112,
-    "w_in1": 3136,
-    "vv_in2": 4160,
-    "book0": 5184,
-    "neg_max1": 5184,
-    "vg2": 5248,
-    "book1": 9280,
-    "vv_in0": 9280,
-    "inv_sum": 10304,
+    "book3": BOOK3,
+    "v0_codes": BOOK3 + ALIGN - P * 4,
+    "w_in0": BOOK3 + ALIGN,
+    "vv_in1": BOOK3 + ALIGN + ROW,
+    "w_in1": BOOK3 + ALIGN + 2 * ROW,
+    "vv_in2": BOOK3 + ALIGN + 3 * ROW,
+    "book0": BOOK0,
+    "neg_max1": BOOK0,
+    "vg2": BOOK0 + ALIGN,
 }
 
 
@@ -55,19 +57,18 @@ def tile_attend_pqvalues_pl_kernel(tc, query, keys_words, keys_scales, vbook, si
         ps = ctx.enter_context(tc.psum_pool(name="ps", bufs=1))
         shared = ctx.enter_context(tc.tile_pool(name="shared", bufs=1))
         tiles = {}
-        tags = {}
 
         def sbt(name, shape, dtype):
-            if name in OVERLAY and name not in tiles:
-                tags[name] = name
-                tiles[name] = shared.tile(shape, dtype, name=name, tag=name, align_bytes=64, offset=OVERLAY[name])
             if name not in tiles:
-                tags[name] = tags[REUSE[name]] if name in REUSE else name
-                tiles[name] = sb.tile(shape, dtype, name=name, tag=tags[name], align_bytes=64)
+                if name in OVERLAY:
+                    tiles[name] = shared.tile(shape, dtype, name=name, tag=name, align_bytes=ALIGN, offset=OVERLAY[name])
+                else:
+                    tiles[name] = sb.tile(shape, dtype, name=name, tag=REUSE.get(name, name), align_bytes=ALIGN)
             return tiles[name]
 
         def bank(name, shape, tag):
-            tiles[name] = ps.tile(shape, F32, name=name, tag=tag)
+            if name not in tiles:
+                tiles[name] = ps.tile(shape, F32, name=name, tag=tag)
             return tiles[name]
 
         key_list = sbt("key_list", [P, I // 16], U16)
@@ -79,8 +80,8 @@ def tile_attend_pqvalues_pl_kernel(tc, query, keys_words, keys_scales, vbook, si
         size_cols = sbt("size_cols", [P, PACK], F32)
         books = [sbt("book%d" % t, [P, C], F32) for t in range(PACK)]
         q_raw = [sbt("q_raw%d" % h, [P, PACK, P], F32) for h in range(HALVES)]
-
         warm_in = sbt("warm_in", [P, 1], F32)
+
         nc.vector.memset(key_scales[:].bitcast(I32), 0)
         nc.vector.memset(ident[:], 0.0)
         nc.vector.memset(warm_in[:], 0.0)
@@ -88,189 +89,72 @@ def tile_attend_pqvalues_pl_kernel(tc, query, keys_words, keys_scales, vbook, si
 
         book_rows = vbook.rearrange("(p t) c -> p t c", t=PACK)
         q_rows = query.rearrange("(p t) q -> p t q", t=PACK)
+        out_rows = out_0.rearrange("(p t) q -> p t q", t=PACK)
+        out_words = out_1[0].rearrange("p c r -> p (c r)").bitcast(I32)
 
-        def load_key_list():
-            nc.sync.dma_start(key_list[:], offs)
+        nc.sync.dma_start(key_list[:], offs)
+        nc.sync.dma_start(vsc_cols[:], vsc.rearrange("(s r) o -> s (r o)", r=PACK))
+        nc.sync.dma_start(code_lists[:], offs2)
+        nc.sync.dma_start(key_words[:].bitcast(I32), keys_words[0].bitcast(I32))
+        nc.sync.dma_start(q_raw[0][:], q_rows[:, :, 0:P])
+        for quad in range(4):
+            nc.sync.dma_start(key_scales[32 * quad : 32 * quad + 4, :].bitcast(I32), keys_scales[0, 4 * quad : 4 * quad + 4, :].bitcast(I32))
+        nc.sync.dma_start(q_raw[1][:], q_rows[:, :, P:Q])
+        nc.sync.dma_start(books[0][:], book_rows[:, 0, :])
+        nc.sync.dma_start(books[2][:], book_rows[:, 2, :])
+        nc.sync.dma_start(size_cols[:], size.rearrange("o (s r) -> s (o r)", r=PACK))
+        nc.sync.dma_start(books[1][:], book_rows[:, 1, :])
+        nc.sync.dma_start(books[3][:], book_rows[:, 3, :])
 
-        def load_code_lists():
-            nc.sync.dma_start(code_lists[:], offs2)
+        nc.scalar.activation(sbt("warm", [P, 1], F32)[:], warm_in[:], EXP)
 
-        def load_words():
-            nc.sync.dma_start(key_words[:].bitcast(I32), keys_words[0].bitcast(I32))
-
-        def load_vsc():
-            nc.sync.dma_start(vsc_cols[:], vsc.rearrange("(s r) o -> s (r o)", r=PACK))
-
-        def load_size():
-            nc.sync.dma_start(size_cols[:], size.rearrange("o (s r) -> s (o r)", r=PACK))
-
-        def load_scale_rows():
-            for quad in range(4):
-                nc.sync.dma_start(key_scales[32 * quad : 32 * quad + 4, :].bitcast(I32), keys_scales[0, 4 * quad : 4 * quad + 4, :].bitcast(I32))
-
-        def load_queries(h):
-            nc.sync.dma_start(q_raw[h][:], q_rows[:, :, h * P : (h + 1) * P])
-
-        def load_book(t):
-            nc.sync.dma_start(books[t][:], book_rows[:, t, :])
-
-        load_key_list()
-        load_vsc()
-        load_code_lists()
-        load_words()
-        load_queries(0)
-        load_scale_rows()
-        load_queries(1)
-        load_book(0)
-        load_book(2)
-        load_size()
-        load_book(1)
-        load_book(3)
-
-        warm = sbt("warm", [P, 1], F32)
-        nc.scalar.activation(warm[:], warm_in[:], EXP)
-
-        def quantise(name, source, width):
-            codes = sbt(name + "_codes", [P, width], U32)
-            scales = sbt(name + "_scales", [P, width], U8)
-            nc.vector.quantize_mx(out=codes[:].bitcast(FP8X4), scales=scales[:], in_=source[:])
-
-        def copy_on(engine, out, source):
-            if engine == "S":
-                nc.scalar.copy(out, source)
-            else:
-                nc.vector.tensor_copy(out, source)
-
-        def round_queries(h, engine):
-            q_in = sbt("q_in%d" % h, [P, P * PACK], BF16)
-            copy_on(
-                engine,
-                q_in[:].rearrange("p (c j t) -> p c t j", j=4, t=PACK),
-                q_raw[h][:].rearrange("p t (c j) -> p c t j", j=4),
-            )
-
-        def quantise_queries(h):
-            quantise("q%d" % h, tiles["q_in%d" % h], P)
+        def quantise(name, source):
+            codes = sbt(name + "_codes", [P, P], U32)
+            scales = sbt(name + "_scales", [P, P], U8)
+            nc.vector.quantize_mx(out=codes[:].bitcast(FP8X4), scales=scales[:], in_=tiles[source][:])
 
         def spread(name, cols, tag):
             row = bank(name, [P, PACK, P], tag)
             for r in range(PACK):
                 nc.tensor.transpose(row[:, r, :], cols[:, r : r + 1].to_broadcast([P, P]), ident[:])
 
-        def copy_row(name, source):
+        def round_queries(h):
             nc.scalar.copy(
-                sbt(name, [P, I], F32)[:].rearrange("p (s r) -> p s r", r=PACK),
-                tiles[source][:].rearrange("p r s -> p s r"),
+                sbt("q_in%d" % h, [P, P * PACK], BF16)[:].rearrange("p (c j t) -> p c t j", j=4, t=PACK),
+                q_raw[h][:].rearrange("p t (c j) -> p c t j", j=4),
             )
 
-        def gather_key_words():
-            nc.vector.tensor_copy(sbt("kg_words", [P, I], U16)[:], key_words[:].indirect(key_list[:]))
-
-        def gather_key_scales(lo, hi):
-            nc.vector.tensor_copy(sbt("kg_scales", [P, I], U8)[:, lo:hi], key_scales[:].indirect(key_list[:, lo // 16 : hi // 16]))
-
-        place = {t: (g, j) for g, planes in enumerate(GROUPS) for j, t in enumerate(planes)}
-
-        def gather_values(t, engine, lo=0, hi=I, part=""):
-            out = sbt("vg%d%s" % (t, part), [P, I], F32)[:, lo:hi]
-            window = books[t][:].indirect(code_lists[:, lo // 16 : hi // 16])
-            if engine == "S":
-                nc.scalar.activation(out, window, COPY)
-            else:
-                nc.vector.tensor_copy(out, window)
-
-        def gather_scaled(t, lo=0, hi=I, part=""):
-            out = sbt("vg%d%s" % (t, part), [P, I], F32)[:, lo:hi]
-            nc.vector.tensor_tensor(out, books[t][:].indirect(code_lists[:, lo // 16 : hi // 16]), tiles["vsc_row"][:, lo:hi], MULT)
-
-        def round_values(t, engine, lo=0, hi=I, part=""):
-            out = sbt("vv_bf%d" % t, [P, I], BF16)[:, lo:hi]
-            source = tiles["vg%d%s" % (t, part)][:, lo:hi]
-            if engine == "G":
-                nc.gpsimd.tensor_copy(out, source)
-            else:
-                nc.scalar.copy(out, source)
-
-        def round_turned(t):
-            nc.scalar.copy(value_slot(t).rearrange("s (p r) -> s p r", r=PACK), tiles["v_turned%d" % t][:].rearrange("s r p -> s p r"))
-
-        def scale_pairs(t, engine, lo=0, hi=I, part=""):
-            s = slice(lo // PACK, hi // PACK)
-            if engine != "V":
-                factor = tiles["vsc_row"][:, lo:hi].rearrange("p (s r) -> p s r", r=PACK)
-            else:
-                factor = tiles["vsc_bank"][:, :, s].rearrange("p r s -> p s r")
-            (nc.gpsimd if engine == "G" else nc.vector).tensor_tensor(
-                sbt("vv_bf%d" % t, [P, I], BF16)[:, lo:hi].rearrange("p (s r) -> p s r", r=PACK),
-                tiles["vg%d%s" % (t, part)][:, lo:hi].rearrange("p (s r) -> p s r", r=PACK),
-                factor,
-                MULT,
-            )
-
-        def turn_pairs(name, source, tag, dealt=False):
-            words = tiles[source][:].bitcast(F32)
-            turned = bank(name, [P, 2, P], tag)
-            for u in range(2):
-                nc.tensor.transpose(turned[:, u, :], words[:, u * P : (u + 1) * P] if dealt else words[:, u : 2 * P : 2], ident[:])
-
-        def fetch_pairs(out, name, engine):
-            copy_on(engine, out.bitcast(F32).rearrange("s (p u) -> s p u", u=2), tiles[name][:].rearrange("s u p -> s p u"))
-
-        def value_slot(t):
-            g, j = place[t]
-            return sbt("vv_in%d" % g, [P, len(GROUPS[g]) * I], BF16)[:, j * I : (j + 1) * I]
-
-        def turn_value_pairs(t, tag, dealt=False):
-            turn_pairs("v_turned%d" % t, "vv_bf%d" % t, tag, dealt)
-
-        def scale_dealt(t, lo, hi):
-            s = slice(lo // PACK, hi // PACK)
-            nc.vector.tensor_tensor(
-                sbt("vv_bf%d" % t, [P, I], BF16)[:].rearrange("p (u s e) -> p u s e", u=2, e=2)[:, :, s, :],
-                tiles["vg%d" % t][:, lo:hi].rearrange("p (s u e) -> p u s e", u=2, e=2),
-                tiles["vsc_bank"][:, :, s].rearrange("p (u e) s -> p u s e", u=2),
-                MULT,
-            )
-
-        def fetch_values(t, engine):
-            fetch_pairs(value_slot(t), "v_turned%d" % t, engine)
-
-        def turn_floats(t, tag):
-            turned = bank("v_turned%d" % t, [P, PACK, P], tag)
-            for r in range(PACK):
-                nc.tensor.transpose(turned[:, r, :], tiles["vg%d" % t][:, r:I:PACK], ident[:])
-
-        def scale_turned(t):
-            nc.vector.tensor_tensor(
-                value_slot(t).rearrange("s (p r) -> s p r", r=PACK),
-                tiles["v_turned%d" % t][:].rearrange("s r p -> s p r"),
-                vsc_cols[:].unsqueeze(1).to_broadcast([P, P, PACK]),
-                MULT,
-            )
-
-        def quantise_values(g):
-            quantise("v%d" % g, tiles["vv_in%d" % g], len(GROUPS[g]) * P)
-
-        def score(h, lo, hi):
-            if "scores%d" % h not in tiles:
-                bank("scores%d" % h, [P, I], "ab"[h])
+        def score(h):
             nc.tensor.matmul_mx(
-                out=tiles["scores%d" % h][:, lo:hi],
+                out=bank("scores%d" % h, [P, I], "ab"[h])[:],
                 lhsT=tiles["q%d_codes" % h][:].bitcast(FP8X4),
                 lhsT_scale=tiles["q%d_scales" % h][:],
-                rhs=tiles["kg_words"][:, lo:hi].bitcast(FP4X4),
-                rhs_scale=tiles["kg_scales"][:, lo:hi],
+                rhs=tiles["kg_words"][:].bitcast(FP4X4),
+                rhs_scale=tiles["kg_scales"][:],
                 start=True,
                 stop=True,
             )
 
+        def gathered(t):
+            return sbt("vg%d" % t, [P, I], F32)
+
+        def rounded(t):
+            return sbt("vv_bf%d" % t, [P, I], BF16)
+
+        def listed(t, lo, hi):
+            return books[t][:].indirect(code_lists[:, lo // 16 : hi // 16])
+
+        def gather_on_scalar(t, lo, hi):
+            nc.scalar.activation(gathered(t)[:, lo:hi], listed(t, lo, hi), COPY)
+
+        def scale_on_gpsimd(t):
+            nc.gpsimd.tensor_tensor(rounded(t)[:], gathered(t)[:], tiles["vsc_row"][:], MULT)
+
         def neg_max(h):
-            return sbt("vg2", [P, I], F32)[:, I - 1 : I] if h == 0 else sbt("neg_max1", [P, 1], F32)[:]
+            return gathered(2)[:, I - 1 : I] if h == 0 else sbt("neg_max1", [P, 1], F32)[:]
 
-        def row_max(h):
+        def softmax_numerator(h):
             nc.vector.tensor_reduce(neg_max(h), tiles["scores%d" % h][:], AX, MAX, negate=True)
-
-        def exponentiate(h):
             nc.scalar.activation(
                 sbt("p_exp", [P, HALVES, I], F32)[:, h, :].rearrange("q (u s e) -> q u s e", u=2, e=2),
                 tiles["scores%d" % h][:].rearrange("q (s u e) -> q u s e", u=2, e=2),
@@ -279,12 +163,9 @@ def tile_attend_pqvalues_pl_kernel(tc, query, keys_words, keys_scales, vbook, si
                 accum_out=sbt("row_sum", [P, HALVES], F32)[:, h : h + 1],
             )
 
-        def invert_sums():
-            nc.vector.reciprocal(sbt("inv_sum", [P, HALVES], F32)[:], tiles["row_sum"][:])
-
         def weigh(h):
             for u in range(2):
-                run = slice(u * 2 * P, (u + 1) * 2 * P)
+                run = slice(u * MID, (u + 1) * MID)
                 nc.vector.scalar_tensor_tensor(
                     sbt("w_bf%d" % h, [P, I], BF16)[:, run].rearrange("q (s e) -> q s e", e=2),
                     tiles["p_exp"][:, h, run].rearrange("q (s e) -> q s e", e=2),
@@ -294,135 +175,125 @@ def tile_attend_pqvalues_pl_kernel(tc, query, keys_words, keys_scales, vbook, si
                     MULT,
                 )
 
-        def turn_weights(h):
-            turn_pairs("w_turned%d" % h, "w_bf%d" % h, "gh"[h], True)
+        def turn_in_order(source, tag):
+            words = tiles[source][:].bitcast(F32)
+            turned = bank(source + "_turned", [P, 2, P], tag)
+            for u in range(2):
+                nc.tensor.transpose(turned[:, u, :], words[:, u : 2 * P : 2], ident[:])
 
-        def fetch_weights(h, engine):
-            fetch_pairs(sbt("w_in%d" % h, [P, I], BF16)[:], "w_turned%d" % h, engine)
+        def turn_dealt(source, tag):
+            words = tiles[source][:].bitcast(F32)
+            turned = bank(source + "_turned", [P, 2, P], tag)
+            for u in range(2):
+                nc.tensor.transpose(turned[:, u, :], words[:, u * P : (u + 1) * P], ident[:])
 
-        def quantise_weights(h):
-            quantise("w%d" % h, tiles["w_in%d" % h], P)
+        def fetch(copy, name, source):
+            copy(
+                sbt(name, [P, I], BF16)[:].bitcast(F32).rearrange("s (p u) -> s p u", u=2),
+                tiles[source + "_turned"][:].rearrange("s u p -> s p u"),
+            )
 
         def product(t, h):
-            name = "acc%d%d" % (t // 2, h)
-            if name not in tiles:
-                bank(name, [P, 2, P], RESULT_BANKS[t // 2][h])
-            g, j = place[t]
             nc.tensor.matmul_mx(
-                out=tiles[name][:, t % 2, :],
-                lhsT=tiles["v%d_codes" % g][:, j * P : (j + 1) * P].bitcast(FP8X4),
-                lhsT_scale=tiles["v%d_scales" % g][:, j * P : (j + 1) * P],
+                out=bank("acc%d%d" % (t // 2, h), [P, 2, P], ("ab", "gh")[t // 2][h])[:, t % 2, :],
+                lhsT=tiles["v%d_codes" % t][:].bitcast(FP8X4),
+                lhsT_scale=tiles["v%d_scales" % t][:],
                 rhs=tiles["w%d_codes" % h][:].bitcast(FP8X4),
                 rhs_scale=tiles["w%d_scales" % h][:],
                 start=True,
                 stop=True,
             )
 
-        out_rows = out_0.rearrange("(p t) q -> p t q", t=PACK)
-        out_words = out_1[0].rearrange("p c r -> p (c r)").bitcast(I32)
+        def result(u, h):
+            return sbt("o_f32_%d" % u, [P, 2, Q], F32)[:, :, h * P : (h + 1) * P]
 
-        def copy_result(u, h, engine):
-            copy_on(engine, sbt("o_f32_%d" % u, [P, 2, Q], F32)[:, :, h * P : (h + 1) * P], tiles["acc%d%d" % (u, h)][:])
+        def result_pair(u, h):
+            return sbt("o_in%d" % h, [P, P * PACK], BF16)[:].rearrange("p (q u e) -> p u q e", u=2, e=2)[:, u, :, :]
 
-        def store_result(u, queue):
-            queue.dma_start(out_rows[:, 2 * u : 2 * u + 2, :], tiles["o_f32_%d" % u][:])
-
-        def round_result(u, h, engine):
-            copy_on(
-                engine,
-                sbt("o_in%d" % h, [P, P * PACK], BF16)[:].rearrange("p (q u e) -> p u q e", u=2, e=2)[:, u, :, :],
-                tiles["acc%d%d" % (u, h)][:].rearrange("p e q -> p q e"),
-            )
-
-        def round_early(h):
-            nc.vector.tensor_copy(
-                sbt("o_in%d" % h, [P, P * PACK], BF16)[:].rearrange("p (q u e) -> p u q e", u=2, e=2)[:, 0, :, :],
-                tiles["o_f32_0"][:, 0:2, h * P : (h + 1) * P].rearrange("p e q -> p q e"),
-            )
-
-        def quantise_result(h):
-            cols = slice(h * P, (h + 1) * P)
-            nc.vector.quantize_mx(
-                out=sbt("o_codes", [P, Q], U32)[:, cols].bitcast(FP8X4),
-                scales=sbt("o_scales", [P, Q], U8)[:, cols],
-                in_=tiles["o_in%d" % h][:],
-            )
-
-        def store_words(h):
-            cols = slice(h * P, (h + 1) * P)
-            nc.sync.dma_start(out_words[:, cols], tiles["o_codes"][:, cols].bitcast(I32))
-
-        def store_planes():
-            for quad in range(4):
-                queue = nc.scalar if quad >= 2 else nc.sync
-                queue.dma_start(out_2[0, 4 * quad : 4 * quad + 4, :].bitcast(I32), tiles["o_scales"][32 * quad : 32 * quad + 4, :].bitcast(I32))
-
-        gather_key_words()
+        nc.vector.tensor_copy(sbt("kg_words", [P, I], U16)[:], key_words[:].indirect(key_list[:]))
         spread("vsc_bank", vsc_cols, "c")
-        round_queries(0, "S")
-        quantise_queries(0)
-        copy_row("vsc_row", "vsc_bank")
-        gather_key_scales(0, I)
-        score(0, 0, I)
-        round_queries(1, "S")
-        quantise_queries(1)
-        score(1, 0, I)
-        gather_values(0, "S", 0, 256)
-        gather_values(0, "V", 256, I)
-        gather_values(2, "S", 0, 256)
+        round_queries(0)
+        quantise("q0", "q_in0")
+        nc.scalar.copy(
+            sbt("vsc_row", [P, I], F32)[:].rearrange("p (s r) -> p s r", r=PACK),
+            tiles["vsc_bank"][:].rearrange("p r s -> p s r"),
+        )
+        nc.vector.tensor_copy(sbt("kg_scales", [P, I], U8)[:], key_scales[:].indirect(key_list[:]))
+        score(0)
+        round_queries(1)
+        quantise("q1", "q_in1")
+        score(1)
+
+        gather_on_scalar(0, 0, MID)
+        nc.vector.tensor_copy(gathered(0)[:, MID:I], listed(0, MID, I))
+        gather_on_scalar(2, 0, MID)
         spread("size_bank", size_cols, "d")
-        row_max(0)
-        exponentiate(0)
-        row_max(1)
-        exponentiate(1)
-        scale_pairs(0, "G")
-        turn_value_pairs(0, "a")
-        gather_values(2, "S", 256, I)
-        gather_scaled(1)
-        invert_sums()
-        fetch_values(0, "V")
-        round_values(1, "G")
-        turn_value_pairs(1, "f")
+        for h in range(HALVES):
+            softmax_numerator(h)
+        scale_on_gpsimd(0)
+        turn_in_order("vv_bf0", "a")
+
+        gather_on_scalar(2, MID, I)
+        nc.vector.tensor_tensor(gathered(1)[:], listed(1, 0, I), tiles["vsc_row"][:], MULT)
+        nc.vector.reciprocal(sbt("inv_sum", [P, HALVES], F32)[:], tiles["row_sum"][:])
+        fetch(nc.vector.tensor_copy, "vv_in0", "vv_bf0")
+        nc.gpsimd.tensor_copy(rounded(1)[:], gathered(1)[:])
+        turn_in_order("vv_bf1", "f")
         weigh(0)
-        turn_weights(0)
-        scale_pairs(2, "G")
+        turn_dealt("w_bf0", "g")
+        scale_on_gpsimd(2)
         weigh(1)
-        turn_weights(1)
-        turn_value_pairs(2, "d")
-        gather_values(3, "S")
-        scale_dealt(3, 0, I)
-        fetch_weights(0, "S")
-        fetch_values(1, "S")
-        fetch_weights(1, "S")
-        fetch_values(2, "S")
-        turn_value_pairs(3, "e", True)
-        fetch_values(3, "S")
-        quantise_values(0)
-        quantise_weights(0)
+        turn_dealt("w_bf1", "h")
+        turn_in_order("vv_bf2", "d")
+        gather_on_scalar(3, 0, MID)
+        gather_on_scalar(3, MID, I)
+        for lo in (0, MID):
+            s = slice(lo // PACK, (lo + MID) // PACK)
+            nc.vector.tensor_tensor(
+                rounded(3)[:].rearrange("p (u s e) -> p u s e", u=2, e=2)[:, :, s, :],
+                gathered(3)[:, lo : lo + MID].rearrange("p (s u e) -> p u s e", u=2, e=2),
+                tiles["vsc_bank"][:, :, s].rearrange("p (u e) s -> p u s e", u=2),
+                MULT,
+            )
+        fetch(nc.scalar.copy, "w_in0", "w_bf0")
+        fetch(nc.scalar.copy, "vv_in1", "vv_bf1")
+        fetch(nc.scalar.copy, "w_in1", "w_bf1")
+        fetch(nc.scalar.copy, "vv_in2", "vv_bf2")
+        turn_dealt("vv_bf3", "e")
+        fetch(nc.scalar.copy, "vv_in3", "vv_bf3")
+
+        quantise("v0", "vv_in0")
+        quantise("w0", "w_in0")
         product(0, 0)
-        quantise_values(1)
+        quantise("v1", "vv_in1")
         product(1, 0)
-        quantise_weights(1)
+        quantise("w1", "w_in1")
         product(0, 1)
         product(1, 1)
-        quantise_values(2)
-        product(2, 0)
-        product(2, 1)
-        quantise_values(3)
-        product(3, 0)
-        product(3, 1)
-        copy_result(0, 0, "S")
-        copy_result(0, 1, "S")
-        round_early(0)
-        round_early(1)
-        store_result(0, nc.sync)
-        round_result(1, 0, "V")
-        round_result(1, 1, "S")
-        copy_result(1, 0, "V")
-        copy_result(1, 1, "S")
-        quantise_result(0)
-        quantise_result(1)
-        store_result(1, nc.scalar)
-        store_words(0)
-        store_words(1)
-        store_planes()
+        for t in range(2, PACK):
+            quantise("v%d" % t, "vv_in%d" % t)
+            for h in range(HALVES):
+                product(t, h)
+
+        for h in range(HALVES):
+            nc.scalar.copy(result(0, h), tiles["acc0%d" % h][:])
+        for h in range(HALVES):
+            nc.vector.tensor_copy(result_pair(0, h), result(0, h).rearrange("p e q -> p q e"))
+        nc.sync.dma_start(out_rows[:, 0:2, :], tiles["o_f32_0"][:])
+        copies = (nc.vector.tensor_copy, nc.scalar.copy)
+        for h in range(HALVES):
+            copies[h](result_pair(1, h), tiles["acc1%d" % h][:].rearrange("p e q -> p q e"))
+        for h in range(HALVES):
+            copies[h](result(1, h), tiles["acc1%d" % h][:])
+        o_codes = sbt("o_codes", [P, Q], U32)
+        o_scales = sbt("o_scales", [P, Q], U8)
+        for h in range(HALVES):
+            cols = slice(h * P, (h + 1) * P)
+            nc.vector.quantize_mx(out=o_codes[:, cols].bitcast(FP8X4), scales=o_scales[:, cols], in_=tiles["o_in%d" % h][:])
+        nc.scalar.dma_start(out_rows[:, 2:PACK, :], tiles["o_f32_1"][:])
+        for h in range(HALVES):
+            cols = slice(h * P, (h + 1) * P)
+            nc.sync.dma_start(out_words[:, cols], o_codes[:, cols].bitcast(I32))
+        for quad in range(4):
+            queue = nc.scalar if quad >= 2 else nc.sync
+            queue.dma_start(out_2[0, 4 * quad : 4 * quad + 4, :].bitcast(I32), o_scales[32 * quad : 32 * quad + 4, :].bitcast(I32))

@@ -27,7 +27,6 @@ MID = I // 2
 
 REUSE = {
     "q0_codes": "vsc_cols",
-    "p_exp": "size_cols",
     "vv_bf2": "book1",
     "o_f32_0": "vv_bf3",
 }
@@ -160,7 +159,7 @@ def tile_attend_pqvalues_pl_kernel(tc, query, keys_words, keys_scales, vbook, si
                 tiles["scores%d" % h][:].rearrange("q (s u e) -> q u s e", u=2, e=2),
                 EXP,
                 bias=neg_max(h),
-                accum_out=sbt("row_sum", [P, HALVES], F32)[:, h : h + 1],
+                accum_out=size_cols[:, h : h + 1],
             )
 
         def weigh(h):
@@ -235,7 +234,7 @@ def tile_attend_pqvalues_pl_kernel(tc, query, keys_words, keys_scales, vbook, si
 
         gather_on_scalar(2, MID, I)
         nc.vector.tensor_tensor(gathered(1)[:], listed(1, 0, I), tiles["vsc_row"][:], MULT)
-        nc.vector.reciprocal(sbt("inv_sum", [P, HALVES], F32)[:], tiles["row_sum"][:])
+        nc.vector.reciprocal(sbt("inv_sum", [P, HALVES], F32)[:], size_cols[:, 0:HALVES])
         fetch(nc.vector.tensor_copy, "vv_in0", "vv_bf0")
         nc.gpsimd.tensor_copy(rounded(1)[:], gathered(1)[:])
         turn_in_order("vv_bf1", "f")
@@ -270,10 +269,12 @@ def tile_attend_pqvalues_pl_kernel(tc, query, keys_words, keys_scales, vbook, si
         quantise("w1", "w_in1")
         product(0, 1)
         product(1, 1)
-        for t in range(2, PACK):
-            quantise("v%d" % t, "vv_in%d" % t)
-            for h in range(HALVES):
-                product(t, h)
+        quantise("v2", "vv_in2")
+        product(2, 0)
+        product(2, 1)
+        quantise("v3", "vv_in3")
+        product(3, 1)
+        product(3, 0)
 
         for h in range(HALVES):
             nc.scalar.copy(result(0, h), tiles["acc0%d" % h][:])
@@ -283,17 +284,15 @@ def tile_attend_pqvalues_pl_kernel(tc, query, keys_words, keys_scales, vbook, si
         copies = (nc.vector.tensor_copy, nc.scalar.copy)
         for h in range(HALVES):
             copies[h](result_pair(1, h), tiles["acc1%d" % h][:].rearrange("p e q -> p q e"))
-        for h in range(HALVES):
+        for h in (1, 0):
             copies[h](result(1, h), tiles["acc1%d" % h][:])
+            (nc.sync, nc.scalar)[h].dma_start(out_rows[:, 2:PACK, h * P : (h + 1) * P], result(1, h))
         o_codes = sbt("o_codes", [P, Q], U32)
         o_scales = sbt("o_scales", [P, Q], U8)
-        for h in range(HALVES):
+        for h in (1, 0):
             cols = slice(h * P, (h + 1) * P)
             nc.vector.quantize_mx(out=o_codes[:, cols].bitcast(FP8X4), scales=o_scales[:, cols], in_=tiles["o_in%d" % h][:])
-        nc.scalar.dma_start(out_rows[:, 2:PACK, :], tiles["o_f32_1"][:])
-        for h in range(HALVES):
-            cols = slice(h * P, (h + 1) * P)
-            nc.sync.dma_start(out_words[:, cols], o_codes[:, cols].bitcast(I32))
+        nc.sync.dma_start(out_words, o_codes[:].bitcast(I32))
         for quad in range(4):
             queue = nc.scalar if quad >= 2 else nc.sync
             queue.dma_start(out_2[0, 4 * quad : 4 * quad + 4, :].bitcast(I32), o_scales[32 * quad : 32 * quad + 4, :].bitcast(I32))

@@ -93,8 +93,8 @@ def tile_attend_pqvalues_pl_kernel(tc, query, keys_words, keys_scales, vbook, si
 
         nc.sync.dma_start(key_list[:], offs)
         nc.sync.dma_start(vsc_cols[:], vsc.rearrange("(s r) o -> s (r o)", r=PACK))
-        nc.sync.dma_start(code_lists[:], offs2)
         nc.sync.dma_start(key_words[:].bitcast(I32), keys_words[0].bitcast(I32))
+        nc.sync.dma_start(code_lists[:], offs2)
         nc.sync.dma_start(q_raw[0][:], q_rows[:, :, 0:P])
         for quad in range(4):
             nc.sync.dma_start(key_scales[32 * quad : 32 * quad + 4, :].bitcast(I32), keys_scales[0, 4 * quad : 4 * quad + 4, :].bitcast(I32))

@@ -24,28 +24,33 @@ P = 128
 PACK = 4
 HALVES = Q // P
 MID = I // 2
-
-REUSE = {
-    "q0_codes": "vsc_cols",
-    "vv_bf2": "book1",
-    "o_f32_0": "vv_bf3",
-}
-
 ALIGN = 64
 ROW = I * 2
-BOOK = C * 4
-BOOK3 = ROW
-BOOK0 = BOOK3 + ALIGN + BOOK
+
+REUSE = {
+    "q_in": "vsc_cols",
+    "vg0": "q_raw",
+    "o_f32_0": "vv_bf3",
+}
 OVERLAY = {
-    "book3": BOOK3,
-    "v0_codes": BOOK3 + ALIGN - P * 4,
-    "w_in0": BOOK3 + ALIGN,
-    "vv_in1": BOOK3 + ALIGN + ROW,
-    "w_in1": BOOK3 + ALIGN + 2 * ROW,
-    "vv_in2": BOOK3 + ALIGN + 3 * ROW,
-    "book0": BOOK0,
-    "neg_max1": BOOK0,
-    "vg2": BOOK0 + ALIGN,
+    "book3": ALIGN,
+    "w_in0": 0,
+    "vv_in1": ROW,
+    "w_in1": 2 * ROW,
+    "vv_in2": 3 * ROW,
+    "v0_codes": 3 * ROW + ROW // 2 + ROW // 2 - ROW // 2 + ROW // 2,
+    "book0": 18 * ROW,
+    "neg_max1": 18 * ROW,
+    "vg2": 18 * ROW + ALIGN,
+    "key_words": 3 * ROW,
+    "size_cols": 5 * ROW - ALIGN,
+    "key_scales": 13 * ROW,
+    "kg_words": 13 * ROW,
+    "book2": 14 * ROW,
+    "book1": 5 * ROW,
+    "inv_sum": 5 * ROW,
+    "vv_bf2": 5 * ROW + ALIGN,
+    "vv_in0": 6 * ROW + ALIGN,
 }
 
 
@@ -78,39 +83,35 @@ def tile_attend_pqvalues_pl_kernel(tc, query, keys_words, keys_scales, vbook, si
         vsc_cols = sbt("vsc_cols", [P, PACK], F32)
         size_cols = sbt("size_cols", [P, PACK], F32)
         books = [sbt("book%d" % t, [P, C], F32) for t in range(PACK)]
-        q_raw = [sbt("q_raw%d" % h, [P, PACK, P], F32) for h in range(HALVES)]
+        q_raw = sbt("q_raw", [P, PACK, Q], F32)
         warm_in = sbt("warm_in", [P, 1], F32)
 
-        nc.vector.memset(key_scales[:].bitcast(I32), 0)
+        nc.vector.memset(key_scales[32:64, :].bitcast(I32), 0)
+        nc.vector.memset(key_scales[64:P, :].bitcast(I32), 0)
+        key_plane = sbt("key_plane", [P, I], U8)
+        nc.vector.memset(key_plane[:].bitcast(I32), 0)
         nc.vector.memset(ident[:], 0.0)
         nc.vector.memset(warm_in[:], 0.0)
         make_identity(nc, ident[:], nomemset=True)
 
         book_rows = vbook.rearrange("(p t) c -> p t c", t=PACK)
-        q_rows = query.rearrange("(p t) q -> p t q", t=PACK)
         out_rows = out_0.rearrange("(p t) q -> p t q", t=PACK)
         out_words = out_1[0].rearrange("p c r -> p (c r)").bitcast(I32)
 
+        nc.sync.dma_start(key_scales[0:32, :].bitcast(I32), keys_scales[0].bitcast(I32).unsqueeze(1).to_broadcast([16, 2, T // 4]))
         nc.sync.dma_start(key_list[:], offs)
         nc.sync.dma_start(vsc_cols[:], vsc.rearrange("(s r) o -> s (r o)", r=PACK))
         nc.sync.dma_start(key_words[:].bitcast(I32), keys_words[0].bitcast(I32))
-        nc.sync.dma_start(code_lists[:], offs2)
-        nc.sync.dma_start(q_raw[0][:], q_rows[:, :, 0:P])
-        for quad in range(4):
-            nc.sync.dma_start(key_scales[32 * quad : 32 * quad + 4, :].bitcast(I32), keys_scales[0, 4 * quad : 4 * quad + 4, :].bitcast(I32))
-        nc.sync.dma_start(q_raw[1][:], q_rows[:, :, P:Q])
+        nc.sync.dma_start(q_raw[:], query.rearrange("(p t) q -> p t q", t=PACK))
         nc.sync.dma_start(books[0][:], book_rows[:, 0, :])
-        nc.sync.dma_start(books[2][:], book_rows[:, 2, :])
-        nc.sync.dma_start(size_cols[:], size.rearrange("o (s r) -> s (o r)", r=PACK))
-        nc.sync.dma_start(books[1][:], book_rows[:, 1, :])
-        nc.sync.dma_start(books[3][:], book_rows[:, 3, :])
+        nc.sync.dma_start(code_lists[:], offs2)
 
         nc.scalar.activation(sbt("warm", [P, 1], F32)[:], warm_in[:], EXP)
 
         def quantise(name, source):
             codes = sbt(name + "_codes", [P, P], U32)
             scales = sbt(name + "_scales", [P, P], U8)
-            nc.vector.quantize_mx(out=codes[:].bitcast(FP8X4), scales=scales[:], in_=tiles[source][:])
+            nc.vector.quantize_mx(out=codes[:].bitcast(FP8X4), scales=scales[:], in_=source)
 
         def spread(name, cols, tag):
             row = bank(name, [P, PACK, P], tag)
@@ -119,8 +120,8 @@ def tile_attend_pqvalues_pl_kernel(tc, query, keys_words, keys_scales, vbook, si
 
         def round_queries(h):
             nc.scalar.copy(
-                sbt("q_in%d" % h, [P, P * PACK], BF16)[:].rearrange("p (c j t) -> p c t j", j=4, t=PACK),
-                q_raw[h][:].rearrange("p t (c j) -> p c t j", j=4),
+                sbt("q_in", [P, HALVES, P * PACK], BF16)[:, h, :].rearrange("p (c j t) -> p c t j", j=4, t=PACK),
+                q_raw[:, :, h * P : (h + 1) * P].rearrange("p t (c j) -> p c t j", j=4),
             )
 
         def score(h):
@@ -129,7 +130,7 @@ def tile_attend_pqvalues_pl_kernel(tc, query, keys_words, keys_scales, vbook, si
                 lhsT=tiles["q%d_codes" % h][:].bitcast(FP8X4),
                 lhsT_scale=tiles["q%d_scales" % h][:],
                 rhs=tiles["kg_words"][:].bitcast(FP4X4),
-                rhs_scale=tiles["kg_scales"][:],
+                rhs_scale=key_plane[:],
                 start=True,
                 stop=True,
             )
@@ -140,34 +141,53 @@ def tile_attend_pqvalues_pl_kernel(tc, query, keys_words, keys_scales, vbook, si
         def rounded(t):
             return sbt("vv_bf%d" % t, [P, I], BF16)
 
-        def listed(t, lo, hi):
-            return books[t][:].indirect(code_lists[:, lo // 16 : hi // 16])
+        def run(k):
+            return slice(k * MID, (k + 1) * MID)
 
-        def gather_on_scalar(t, lo, hi):
-            nc.scalar.activation(gathered(t)[:, lo:hi], listed(t, lo, hi), COPY)
+        def listed(t, k):
+            return books[t][:].indirect(code_lists[:, k * MID // 16 : (k + 1) * MID // 16])
 
-        def scale_on_gpsimd(t):
-            nc.gpsimd.tensor_tensor(rounded(t)[:], gathered(t)[:], tiles["vsc_row"][:], MULT)
+        def gather_on_scalar(t, k):
+            nc.scalar.activation(gathered(t)[:, run(k)], listed(t, k), COPY)
+
+        def gather_on_vector(t, k):
+            nc.vector.tensor_tensor(gathered(t)[:, run(k)], listed(t, k), tiles["vsc_row"][:, run(k)], MULT)
+
+        def round_on_gpsimd(t, k):
+            nc.gpsimd.tensor_copy(rounded(t)[:, run(k)], gathered(t)[:, run(k)])
+
+        def scale_on_gpsimd(t, k):
+            nc.gpsimd.tensor_tensor(rounded(t)[:, run(k)], gathered(t)[:, run(k)], tiles["vsc_row"][:, run(k)], MULT)
+
+        def scale_on_vector(t, k):
+            s = slice(k * MID // PACK, (k + 1) * MID // PACK)
+            nc.vector.tensor_tensor(
+                rounded(t)[:].rearrange("p (u s e) -> p u s e", u=2, e=2)[:, :, s, :],
+                gathered(t)[:, run(k)].rearrange("p (s u e) -> p u s e", u=2, e=2),
+                tiles["vsc_bank"][:, :, s].rearrange("p (u e) s -> p u s e", u=2),
+                MULT,
+            )
 
         def neg_max(h):
             return gathered(2)[:, I - 1 : I] if h == 0 else sbt("neg_max1", [P, 1], F32)[:]
 
-        def softmax_numerator(h):
+        def row_max(h):
             nc.vector.tensor_reduce(neg_max(h), tiles["scores%d" % h][:], AX, MAX, negate=True)
+
+        def numerator(h):
             nc.scalar.activation(
                 sbt("p_exp", [P, HALVES, I], F32)[:, h, :].rearrange("q (u s e) -> q u s e", u=2, e=2),
                 tiles["scores%d" % h][:].rearrange("q (s u e) -> q u s e", u=2, e=2),
                 EXP,
                 bias=neg_max(h),
-                accum_out=size_cols[:, h : h + 1],
+                accum_out=sbt("row_sum", [P, HALVES], F32)[:, h : h + 1],
             )
 
         def weigh(h):
             for u in range(2):
-                run = slice(u * MID, (u + 1) * MID)
                 nc.vector.scalar_tensor_tensor(
-                    sbt("w_bf%d" % h, [P, I], BF16)[:, run].rearrange("q (s e) -> q s e", e=2),
-                    tiles["p_exp"][:, h, run].rearrange("q (s e) -> q s e", e=2),
+                    sbt("w_bf%d" % h, [P, I], BF16)[:, run(u)].rearrange("q (s e) -> q s e", e=2),
+                    tiles["p_exp"][:, h, run(u)].rearrange("q (s e) -> q s e", e=2),
                     tiles["inv_sum"][:, h : h + 1],
                     tiles["size_bank"][:, 2 * u : 2 * u + 2, :].rearrange("q e s -> q s e"),
                     MULT,
@@ -194,7 +214,7 @@ def tile_attend_pqvalues_pl_kernel(tc, query, keys_words, keys_scales, vbook, si
 
         def product(t, h):
             nc.tensor.matmul_mx(
-                out=bank("acc%d%d" % (t // 2, h), [P, 2, P], ("ab", "gh")[t // 2][h])[:, t % 2, :],
+                out=bank("acc%d%d" % (t // 2, h), [P, 2, P], ("hd", "ec")[t // 2][h])[:, t % 2, :],
                 lhsT=tiles["v%d_codes" % t][:].bitcast(FP8X4),
                 lhsT_scale=tiles["v%d_scales" % t][:],
                 rhs=tiles["w%d_codes" % h][:].bitcast(FP8X4),
@@ -209,70 +229,73 @@ def tile_attend_pqvalues_pl_kernel(tc, query, keys_words, keys_scales, vbook, si
         def result_pair(u, h):
             return sbt("o_in%d" % h, [P, P * PACK], BF16)[:].rearrange("p (q u e) -> p u q e", u=2, e=2)[:, u, :, :]
 
-        nc.vector.tensor_copy(sbt("kg_words", [P, I], U16)[:], key_words[:].indirect(key_list[:]))
-        spread("vsc_bank", vsc_cols, "c")
-        round_queries(0)
-        quantise("q0", "q_in0")
-        nc.scalar.copy(
-            sbt("vsc_row", [P, I], F32)[:].rearrange("p (s r) -> p s r", r=PACK),
-            tiles["vsc_bank"][:].rearrange("p r s -> p s r"),
-        )
+        def copy_vsc_row():
+            nc.scalar.copy(
+                sbt("vsc_row", [P, I], F32)[:].rearrange("p (s r) -> p s r", r=PACK),
+                tiles["vsc_bank"][:].rearrange("p r s -> p s r"),
+            )
+
         nc.vector.tensor_copy(sbt("kg_scales", [P, I], U8)[:], key_scales[:].indirect(key_list[:]))
-        score(0)
-        round_queries(1)
-        quantise("q1", "q_in1")
-        score(1)
-
-        gather_on_scalar(0, 0, MID)
-        nc.vector.tensor_copy(gathered(0)[:, MID:I], listed(0, MID, I))
-        gather_on_scalar(2, 0, MID)
-        spread("size_bank", size_cols, "d")
+        for quad in range(4):
+            nc.sync.dma_start(key_plane[32 * quad : 32 * quad + 4, :].bitcast(I32), tiles["kg_scales"][8 * quad : 8 * quad + 8 : 2, :].bitcast(I32))
+        nc.vector.tensor_copy(sbt("kg_words", [P, I], U16)[:], key_words[:].indirect(key_list[:]))
+        nc.sync.dma_start(books[2][:], book_rows[:, 2, :])
+        nc.sync.dma_start(books[1][:], book_rows[:, 1, :])
+        nc.sync.dma_start(size_cols[:], size.rearrange("o (s r) -> s (o r)", r=PACK))
+        nc.sync.dma_start(books[3][:], book_rows[:, 3, :])
+        spread("vsc_bank", vsc_cols, "c")
+        copy_vsc_row()
         for h in range(HALVES):
-            softmax_numerator(h)
-        scale_on_gpsimd(0)
-        turn_in_order("vv_bf0", "a")
+            round_queries(h)
+            quantise("q%d" % h, tiles["q_in"][:, h, :])
+            score(h)
 
-        gather_on_scalar(2, MID, I)
-        nc.vector.tensor_tensor(gathered(1)[:], listed(1, 0, I), tiles["vsc_row"][:], MULT)
-        nc.vector.reciprocal(sbt("inv_sum", [P, HALVES], F32)[:], size_cols[:, 0:HALVES])
+        gather_on_scalar(0, 0)
+        gather_on_vector(0, 1)
+        gather_on_scalar(2, 0)
+        for h in range(HALVES):
+            row_max(h)
+            numerator(h)
+        scale_on_gpsimd(0, 0)
+        round_on_gpsimd(0, 1)
+        spread("size_bank", size_cols, "a")
+        turn_in_order("vv_bf0", "d")
+
+        nc.vector.tensor_tensor(gathered(1)[:], books[1][:].indirect(code_lists[:]), tiles["vsc_row"][:], MULT)
+        gather_on_scalar(2, 1)
+        gather_on_scalar(3, 0)
+        gather_on_scalar(3, 1)
+        nc.vector.reciprocal(sbt("inv_sum", [P, HALVES], F32)[:], tiles["row_sum"][:])
         fetch(nc.vector.tensor_copy, "vv_in0", "vv_bf0")
         nc.gpsimd.tensor_copy(rounded(1)[:], gathered(1)[:])
-        turn_in_order("vv_bf1", "f")
+        nc.gpsimd.tensor_tensor(rounded(2)[:], gathered(2)[:], tiles["vsc_row"][:], MULT)
+        turn_in_order("vv_bf1", "b")
         weigh(0)
-        turn_dealt("w_bf0", "g")
-        scale_on_gpsimd(2)
+        turn_dealt("w_bf0", "e")
         weigh(1)
-        turn_dealt("w_bf1", "h")
-        turn_in_order("vv_bf2", "d")
-        gather_on_scalar(3, 0, MID)
-        gather_on_scalar(3, MID, I)
-        for lo in (0, MID):
-            s = slice(lo // PACK, (lo + MID) // PACK)
-            nc.vector.tensor_tensor(
-                rounded(3)[:].rearrange("p (u s e) -> p u s e", u=2, e=2)[:, :, s, :],
-                gathered(3)[:, lo : lo + MID].rearrange("p (s u e) -> p u s e", u=2, e=2),
-                tiles["vsc_bank"][:, :, s].rearrange("p (u e) s -> p u s e", u=2),
-                MULT,
-            )
-        fetch(nc.scalar.copy, "w_in0", "w_bf0")
+        turn_dealt("w_bf1", "f")
+        turn_in_order("vv_bf2", "a")
+        scale_on_vector(3, 0)
+        scale_on_vector(3, 1)
+        turn_dealt("vv_bf3", "g")
         fetch(nc.scalar.copy, "vv_in1", "vv_bf1")
+        fetch(nc.scalar.copy, "w_in0", "w_bf0")
         fetch(nc.scalar.copy, "w_in1", "w_bf1")
         fetch(nc.scalar.copy, "vv_in2", "vv_bf2")
-        turn_dealt("vv_bf3", "e")
         fetch(nc.scalar.copy, "vv_in3", "vv_bf3")
 
-        quantise("v0", "vv_in0")
-        quantise("w0", "w_in0")
+        quantise("v0", tiles["vv_in0"][:])
+        quantise("w0", tiles["w_in0"][:])
         product(0, 0)
-        quantise("v1", "vv_in1")
+        quantise("v1", tiles["vv_in1"][:])
         product(1, 0)
-        quantise("w1", "w_in1")
+        quantise("w1", tiles["w_in1"][:])
         product(0, 1)
         product(1, 1)
-        quantise("v2", "vv_in2")
+        quantise("v2", tiles["vv_in2"][:])
         product(2, 0)
         product(2, 1)
-        quantise("v3", "vv_in3")
+        quantise("v3", tiles["vv_in3"][:])
         product(3, 1)
         product(3, 0)
 

@@ -34,11 +34,9 @@ REUSE = {
 }
 OVERLAY = {
     "book3": ALIGN,
-    "w_in0": 0,
-    "vv_in1": ROW,
-    "w_in1": 2 * ROW,
+    "vv_in01": 0,
+    "w_in0": 2 * ROW,
     "vv_in2": 3 * ROW,
-    "v0_codes": 3 * ROW + ROW // 2 + ROW // 2 - ROW // 2 + ROW // 2,
     "book0": 18 * ROW,
     "neg_max1": 18 * ROW,
     "vg2": 18 * ROW + ALIGN,
@@ -50,7 +48,6 @@ OVERLAY = {
     "book1": 5 * ROW,
     "inv_sum": 5 * ROW,
     "vv_bf2": 5 * ROW + ALIGN,
-    "vv_in0": 6 * ROW + ALIGN,
 }
 
 
@@ -159,12 +156,11 @@ def tile_attend_pqvalues_pl_kernel(tc, query, keys_words, keys_scales, vbook, si
         def scale_on_gpsimd(t, k):
             nc.gpsimd.tensor_tensor(rounded(t)[:, run(k)], gathered(t)[:, run(k)], tiles["vsc_row"][:, run(k)], MULT)
 
-        def scale_on_vector(t, k):
-            s = slice(k * MID // PACK, (k + 1) * MID // PACK)
+        def scale_on_vector(t, u):
             nc.vector.tensor_tensor(
-                rounded(t)[:].rearrange("p (u s e) -> p u s e", u=2, e=2)[:, :, s, :],
-                gathered(t)[:, run(k)].rearrange("p (s u e) -> p u s e", u=2, e=2),
-                tiles["vsc_bank"][:, :, s].rearrange("p (u e) s -> p u s e", u=2),
+                rounded(t)[:].rearrange("p (u s e) -> p u s e", u=2, e=2)[:, u, :, :],
+                gathered(t)[:].rearrange("p (s u e) -> p u s e", u=2, e=2)[:, u, :, :],
+                tiles["vsc_bank"][:, 2 * u : 2 * u + 2, :].rearrange("p e s -> p s e"),
                 MULT,
             )
 
@@ -194,9 +190,8 @@ def tile_attend_pqvalues_pl_kernel(tc, query, keys_words, keys_scales, vbook, si
                     MULT,
                 )
 
-        def turn_in_order(source, tag):
+        def turn_in_order(source, turned):
             words = tiles[source][:].bitcast(F32)
-            turned = bank(source + "_turned", [P, 2, P], tag)
             for u in range(2):
                 nc.tensor.transpose(turned[:, u, :], words[:, u : 2 * P : 2], ident[:])
 
@@ -214,7 +209,7 @@ def tile_attend_pqvalues_pl_kernel(tc, query, keys_words, keys_scales, vbook, si
 
         def product(t, h):
             nc.tensor.matmul_mx(
-                out=bank("acc%d%d" % (t // 2, h), [P, 2, P], ("hd", "ec")[t // 2][h])[:, t % 2, :],
+                out=bank("acc%d%d" % (t // 2, h), [P, 2, P], ("hd", "eb")[t // 2][h])[:, t % 2, :],
                 lhsT=tiles["v%d_codes" % t][:].bitcast(FP8X4),
                 lhsT_scale=tiles["v%d_scales" % t][:],
                 rhs=tiles["w%d_codes" % h][:].bitcast(FP8X4),
@@ -259,35 +254,37 @@ def tile_attend_pqvalues_pl_kernel(tc, query, keys_words, keys_scales, vbook, si
         scale_on_gpsimd(0, 0)
         round_on_gpsimd(0, 1)
         spread("size_bank", size_cols, "a")
-        turn_in_order("vv_bf0", "d")
+        early = bank("early_turned", [P, 2, 2, P], "b")
+        turn_in_order("vv_bf0", early[:, 0, :, :])
 
         nc.vector.tensor_tensor(gathered(1)[:], books[1][:].indirect(code_lists[:]), tiles["vsc_row"][:], MULT)
         gather_on_scalar(2, 1)
-        gather_on_scalar(3, 0)
-        gather_on_scalar(3, 1)
+        nc.scalar.activation(gathered(3)[:], books[3][:].indirect(code_lists[:]), COPY)
         nc.vector.reciprocal(sbt("inv_sum", [P, HALVES], F32)[:], tiles["row_sum"][:])
-        fetch(nc.vector.tensor_copy, "vv_in0", "vv_bf0")
         nc.gpsimd.tensor_copy(rounded(1)[:], gathered(1)[:])
         nc.gpsimd.tensor_tensor(rounded(2)[:], gathered(2)[:], tiles["vsc_row"][:], MULT)
-        turn_in_order("vv_bf1", "b")
+        turn_in_order("vv_bf1", early[:, 1, :, :])
         weigh(0)
         turn_dealt("w_bf0", "e")
         weigh(1)
         turn_dealt("w_bf1", "f")
-        turn_in_order("vv_bf2", "a")
-        scale_on_vector(3, 0)
-        scale_on_vector(3, 1)
+        turn_in_order("vv_bf2", bank("vv_bf2_turned", [P, 2, P], "a"))
+        for u in range(2):
+            scale_on_vector(3, u)
         turn_dealt("vv_bf3", "g")
-        fetch(nc.scalar.copy, "vv_in1", "vv_bf1")
+        nc.scalar.copy(
+            sbt("vv_in01", [P, 2, I], BF16)[:].rearrange("s t c -> s (t c)").bitcast(F32).rearrange("s (t p u) -> s t p u", t=2, u=2),
+            early[:].rearrange("s t u p -> s t p u"),
+        )
         fetch(nc.scalar.copy, "w_in0", "w_bf0")
         fetch(nc.scalar.copy, "w_in1", "w_bf1")
         fetch(nc.scalar.copy, "vv_in2", "vv_bf2")
         fetch(nc.scalar.copy, "vv_in3", "vv_bf3")
 
-        quantise("v0", tiles["vv_in0"][:])
+        quantise("v0", tiles["vv_in01"][:, 0, :])
         quantise("w0", tiles["w_in0"][:])
         product(0, 0)
-        quantise("v1", tiles["vv_in1"][:])
+        quantise("v1", tiles["vv_in01"][:, 1, :])
         product(1, 0)
         quantise("w1", tiles["w_in1"][:])
         product(0, 1)

from contextlib import ExitStack

import concourse.mybir as mybir
from concourse.masks import make_identity

D, T, I, C, Q, E = 512, 2048, 512, 1024, 256, 512
FLOPS = 2 * D * Q * I + 2 * I * E * Q

F32 = mybir.dt.float32
BF16 = mybir.dt.bfloat16
I32 = mybir.dt.int32
U32 = mybir.dt.uint32
U16 = mybir.dt.uint16
U8 = mybir.dt.uint8
FP8X4 = mybir.dt.float8_e4m3fn_x4
FP4X4 = mybir.dt.float4_e2m1fn_x4
MULT = mybir.AluOpType.mult
MAX = mybir.AluOpType.max
EXP = mybir.ActivationFunctionType.Exp
COPY = mybir.ActivationFunctionType.Copy
AX = mybir.AxisListType.X

P = 128
PACK = 4
HALVES = Q // P
MID = I // 2
ALIGN = 64
ROW = I * 2

REUSE = {
    "q_in": "vsc_cols",
    "vg0": "q_raw",
    "o_f32_0": "vv_bf3",
}
OVERLAY = {
    "book3": ALIGN,
    "vv_in01": 0,
    "w_in0": 2 * ROW,
    "vv_in2": 3 * ROW,
    "book0": 18 * ROW,
    "neg_max1": 18 * ROW,
    "vg2": 18 * ROW + ALIGN,
    "key_words": 3 * ROW,
    "size_cols": 5 * ROW - ALIGN,
    "key_scales": 13 * ROW,
    "kg_words": 13 * ROW,
    "book2": 14 * ROW,
    "book1": 5 * ROW,
    "inv_sum": 5 * ROW,
    "vv_bf2": 5 * ROW + ALIGN,
}


def tile_attend_pqvalues_pl_kernel(tc, query, keys_words, keys_scales, vbook, size, vsc, offs, offs2, out_0, out_1, out_2):
    nc = tc.nc
    with ExitStack() as ctx:
        sb = ctx.enter_context(tc.tile_pool(name="sb", bufs=1))
        ps = ctx.enter_context(tc.psum_pool(name="ps", bufs=1))
        shared = ctx.enter_context(tc.tile_pool(name="shared", bufs=1))
        tiles = {}

        def sbt(name, shape, dtype):
            if name not in tiles:
                if name in OVERLAY:
                    tiles[name] = shared.tile(shape, dtype, name=name, tag=name, align_bytes=ALIGN, offset=OVERLAY[name])
                else:
                    tiles[name] = sb.tile(shape, dtype, name=name, tag=REUSE.get(name, name), align_bytes=ALIGN)
            return tiles[name]

        def bank(name, shape, tag):
            if name not in tiles:
                tiles[name] = ps.tile(shape, F32, name=name, tag=tag)
            return tiles[name]

        key_list = sbt("key_list", [P, I // 16], U16)
        code_lists = sbt("code_lists", [P, I // 16], U16)
        key_words = sbt("key_words", [P, T], U16)
        key_scales = sbt("key_scales", [P, T], U8)
        ident = sbt("ident", [P, P], F32)
        vsc_cols = sbt("vsc_cols", [P, PACK], F32)
        size_cols = sbt("size_cols", [P, PACK], F32)
        books = [sbt("book%d" % t, [P, C], F32) for t in range(PACK)]
        q_raw = sbt("q_raw", [P, PACK, Q], F32)
        warm_in = sbt("warm_in", [P, 1], F32)

        nc.vector.memset(key_scales[32:64, :].bitcast(I32), 0)
        nc.vector.memset(key_scales[64:P, :].bitcast(I32), 0)
        key_plane = sbt("key_plane", [P, I], U8)
        nc.vector.memset(key_plane[:].bitcast(I32), 0)
        nc.vector.memset(ident[:], 0.0)
        nc.vector.memset(warm_in[:], 0.0)
        make_identity(nc, ident[:], nomemset=True)

        book_rows = vbook.rearrange("(p t) c -> p t c", t=PACK)
        out_rows = out_0.rearrange("(p t) q -> p t q", t=PACK)
        out_words = out_1[0].rearrange("p c r -> p (c r)").bitcast(I32)

        nc.sync.dma_start(key_scales[0:32, :].bitcast(I32), keys_scales[0].bitcast(I32).unsqueeze(1).to_broadcast([16, 2, T // 4]))
        nc.sync.dma_start(key_list[:], offs)
        nc.sync.dma_start(vsc_cols[:], vsc.rearrange("(s r) o -> s (r o)", r=PACK))
        nc.sync.dma_start(key_words[:].bitcast(I32), keys_words[0].bitcast(I32))
        nc.sync.dma_start(q_raw[:], query.rearrange("(p t) q -> p t q", t=PACK))
        nc.sync.dma_start(books[0][:], book_rows[:, 0, :])
        nc.sync.dma_start(code_lists[:], offs2)

        nc.scalar.activation(sbt("warm", [P, 1], F32)[:], warm_in[:], EXP)

        def quantise(name, source):
            codes = sbt(name + "_codes", [P, P], U32)
            scales = sbt(name + "_scales", [P, P], U8)
            nc.vector.quantize_mx(out=codes[:].bitcast(FP8X4), scales=scales[:], in_=source)

        def spread(name, cols, tag):
            row = bank(name, [P, PACK, P], tag)
            for r in range(PACK):
                nc.tensor.transpose(row[:, r, :], cols[:, r : r + 1].to_broadcast([P, P]), ident[:])

        def round_queries(h):
            nc.scalar.copy(
                sbt("q_in", [P, HALVES, P * PACK], BF16)[:, h, :].rearrange("p (c j t) -> p c t j", j=4, t=PACK),
                q_raw[:, :, h * P : (h + 1) * P].rearrange("p t (c j) -> p c t j", j=4),
            )

        def score(h):
            nc.tensor.matmul_mx(
                out=bank("scores%d" % h, [P, I], "ab"[h])[:],
                lhsT=tiles["q%d_codes" % h][:].bitcast(FP8X4),
                lhsT_scale=tiles["q%d_scales" % h][:],
                rhs=tiles["kg_words"][:].bitcast(FP4X4),
                rhs_scale=key_plane[:],
                start=True,
                stop=True,
            )

        def gathered(t):
            return sbt("vg%d" % t, [P, I], F32)

        def rounded(t):
            return sbt("vv_bf%d" % t, [P, I], BF16)

        def run(k):
            return slice(k * MID, (k + 1) * MID)

        def listed(t, k):
            return books[t][:].indirect(code_lists[:, k * MID // 16 : (k + 1) * MID // 16])

        def gather_on_scalar(t, k):
            nc.scalar.activation(gathered(t)[:, run(k)], listed(t, k), COPY)

        def gather_on_vector(t, k):
            nc.vector.tensor_tensor(gathered(t)[:, run(k)], listed(t, k), tiles["vsc_row"][:, run(k)], MULT)

        def round_on_gpsimd(t, k):
            nc.gpsimd.tensor_copy(rounded(t)[:, run(k)], gathered(t)[:, run(k)])

        def scale_on_gpsimd(t, k):
            nc.gpsimd.tensor_tensor(rounded(t)[:, run(k)], gathered(t)[:, run(k)], tiles["vsc_row"][:, run(k)], MULT)

        def scale_on_vector(t, u):
            nc.vector.tensor_tensor(
                rounded(t)[:].rearrange("p (u s e) -> p u s e", u=2, e=2)[:, u, :, :],
                gathered(t)[:].rearrange("p (s u e) -> p u s e", u=2, e=2)[:, u, :, :],
                tiles["vsc_bank"][:, 2 * u : 2 * u + 2, :].rearrange("p e s -> p s e"),
                MULT,
            )

        def neg_max(h):
            return gathered(2)[:, I - 1 : I] if h == 0 else sbt("neg_max1", [P, 1], F32)[:]

        def row_max(h):
            nc.vector.tensor_reduce(neg_max(h), tiles["scores%d" % h][:], AX, MAX, negate=True)

        def numerator(h):
            nc.scalar.activation(
                sbt("p_exp", [P, HALVES, I], F32)[:, h, :].rearrange("q (u s e) -> q u s e", u=2, e=2),
                tiles["scores%d" % h][:].rearrange("q (s u e) -> q u s e", u=2, e=2),
                EXP,
                bias=neg_max(h),
                accum_out=sbt("row_sum", [P, HALVES], F32)[:, h : h + 1],
            )

        def weigh(h):
            for u in range(2):
                nc.vector.scalar_tensor_tensor(
                    sbt("w_bf%d" % h, [P, I], BF16)[:, run(u)].rearrange("q (s e) -> q s e", e=2),
                    tiles["p_exp"][:, h, run(u)].rearrange("q (s e) -> q s e", e=2),
                    tiles["inv_sum"][:, h : h + 1],
                    tiles["size_bank"][:, 2 * u : 2 * u + 2, :].rearrange("q e s -> q s e"),
                    MULT,
                    MULT,
                )

        def turn_in_order(source, turned):
            words = tiles[source][:].bitcast(F32)
            for u in range(2):
                nc.tensor.transpose(turned[:, u, :], words[:, u : 2 * P : 2], ident[:])

        def turn_dealt(source, tag):
            words = tiles[source][:].bitcast(F32)
            turned = bank(source + "_turned", [P, 2, P], tag)
            for u in range(2):
                nc.tensor.transpose(turned[:, u, :], words[:, u * P : (u + 1) * P], ident[:])

        def fetch(copy, name, source):
            copy(
                sbt(name, [P, I], BF16)[:].bitcast(F32).rearrange("s (p u) -> s p u", u=2),
                tiles[source + "_turned"][:].rearrange("s u p -> s p u"),
            )

        def product(t, h):
            nc.tensor.matmul_mx(
                out=bank("acc%d%d" % (t // 2, h), [P, 2, P], ("hd", "eb")[t // 2][h])[:, t % 2, :],
                lhsT=tiles["v%d_codes" % t][:].bitcast(FP8X4),
                lhsT_scale=tiles["v%d_scales" % t][:],
                rhs=tiles["w%d_codes" % h][:].bitcast(FP8X4),
                rhs_scale=tiles["w%d_scales" % h][:],
                start=True,
                stop=True,
            )

        def result(u, h):
            return sbt("o_f32_%d" % u, [P, 2, Q], F32)[:, :, h * P : (h + 1) * P]

        def result_pair(u, h):
            return sbt("o_in%d" % h, [P, P * PACK], BF16)[:].rearrange("p (q u e) -> p u q e", u=2, e=2)[:, u, :, :]

        def copy_vsc_row():
            nc.scalar.copy(
                sbt("vsc_row", [P, I], F32)[:].rearrange("p (s r) -> p s r", r=PACK),
                tiles["vsc_bank"][:].rearrange("p r s -> p s r"),
            )

        nc.vector.tensor_copy(sbt("kg_scales", [P, I], U8)[:], key_scales[:].indirect(key_list[:]))
        for quad in range(4):
            nc.sync.dma_start(key_plane[32 * quad : 32 * quad + 4, :].bitcast(I32), tiles["kg_scales"][8 * quad : 8 * quad + 8 : 2, :].bitcast(I32))
        nc.vector.tensor_copy(sbt("kg_words", [P, I], U16)[:], key_words[:].indirect(key_list[:]))
        nc.sync.dma_start(books[2][:], book_rows[:, 2, :])
        nc.sync.dma_start(books[1][:], book_rows[:, 1, :])
        nc.sync.dma_start(size_cols[:], size.rearrange("o (s r) -> s (o r)", r=PACK))
        nc.sync.dma_start(books[3][:], book_rows[:, 3, :])
        spread("vsc_bank", vsc_cols, "c")
        copy_vsc_row()
        for h in range(HALVES):
            round_queries(h)
            quantise("q%d" % h, tiles["q_in"][:, h, :])
            score(h)

        gather_on_scalar(0, 0)
        gather_on_vector(0, 1)
        gather_on_scalar(2, 0)
        for h in range(HALVES):
            row_max(h)
            numerator(h)
        scale_on_gpsimd(0, 0)
        round_on_gpsimd(0, 1)
        spread("size_bank", size_cols, "a")
        early = bank("early_turned", [P, 2, 2, P], "b")
        turn_in_order("vv_bf0", early[:, 0, :, :])

        nc.vector.tensor_tensor(gathered(1)[:], books[1][:].indirect(code_lists[:]), tiles["vsc_row"][:], MULT)
        gather_on_scalar(2, 1)
        nc.scalar.activation(gathered(3)[:], books[3][:].indirect(code_lists[:]), COPY)
        nc.vector.reciprocal(sbt("inv_sum", [P, HALVES], F32)[:], tiles["row_sum"][:])
        nc.gpsimd.tensor_copy(rounded(1)[:], gathered(1)[:])
        nc.gpsimd.tensor_tensor(rounded(2)[:], gathered(2)[:], tiles["vsc_row"][:], MULT)
        turn_in_order("vv_bf1", early[:, 1, :, :])
        weigh(0)
        turn_dealt("w_bf0", "e")
        weigh(1)
        turn_dealt("w_bf1", "f")
        turn_in_order("vv_bf2", bank("vv_bf2_turned", [P, 2, P], "a"))
        for u in range(2):
            scale_on_vector(3, u)
        turn_dealt("vv_bf3", "g")
        nc.scalar.copy(
            sbt("vv_in01", [P, 2, I], BF16)[:].rearrange("s t c -> s (t c)").bitcast(F32).rearrange("s (t p u) -> s t p u", t=2, u=2),
            early[:].rearrange("s t u p -> s t p u"),
        )
        fetch(nc.scalar.copy, "w_in0", "w_bf0")
        fetch(nc.scalar.copy, "w_in1", "w_bf1")
        fetch(nc.scalar.copy, "vv_in2", "vv_bf2")
        fetch(nc.scalar.copy, "vv_in3", "vv_bf3")

        quantise("v0", tiles["vv_in01"][:, 0, :])
        quantise("w0", tiles["w_in0"][:])
        product(0, 0)
        quantise("v1", tiles["vv_in01"][:, 1, :])
        product(1, 0)
        quantise("w1", tiles["w_in1"][:])
        product(0, 1)
        product(1, 1)
        quantise("v2", tiles["vv_in2"][:])
        product(2, 0)
        product(2, 1)
        quantise("v3", tiles["vv_in3"][:])
        product(3, 1)
        product(3, 0)

        for h in range(HALVES):
            nc.scalar.copy(result(0, h), tiles["acc0%d" % h][:])
        for h in range(HALVES):
            nc.vector.tensor_copy(result_pair(0, h), result(0, h).rearrange("p e q -> p q e"))
        nc.sync.dma_start(out_rows[:, 0:2, :], tiles["o_f32_0"][:])
        copies = (nc.vector.tensor_copy, nc.scalar.copy)
        for h in range(HALVES):
            copies[h](result_pair(1, h), tiles["acc1%d" % h][:].rearrange("p e q -> p q e"))
        for h in (1, 0):
            copies[h](result(1, h), tiles["acc1%d" % h][:])
            (nc.sync, nc.scalar)[h].dma_start(out_rows[:, 2:PACK, h * P : (h + 1) * P], result(1, h))
        o_codes = sbt("o_codes", [P, Q], U32)
        o_scales = sbt("o_scales", [P, Q], U8)
        for h in (1, 0):
            cols = slice(h * P, (h + 1) * P)
            nc.vector.quantize_mx(out=o_codes[:, cols].bitcast(FP8X4), scales=o_scales[:, cols], in_=tiles["o_in%d" % h][:])
        nc.sync.dma_start(out_words, o_codes[:].bitcast(I32))
        for quad in range(4):
            queue = nc.scalar if quad >= 2 else nc.sync
            queue.dma_start(out_2[0, 4 * quad : 4 * quad + 4, :].bitcast(I32), o_scales[32 * quad : 32 * quad + 4, :].bitcast(I32))
